import numpy as np, ml_dtypes
CORES = [2,6,10,14,18,22,26,30]
N = 8
BF = ml_dtypes.bfloat16
P, BK, W, SH, NB, EV = 384, 4096, 16, 4, 2048, 3
LV, AR, LIVE = 32, 64, 512
def group():
    return np.arange(8)[None, :, None]
def event(bm, cs, ls, e, sd, t):
    q = e >> 16; u = e & 65535; g = group()
    m = bm[q, g, u >> SH]; b = (m >> 5) + ((u & (W - 1)) >= (m & 31))
    c = cs.reshape(N, 8, 16, NB)[q, g, :, b]
    k = np.sum(c <= ((sd >> (4 * t)) & 4095)[..., None], axis=-1)
    return c, np.maximum(e - ls.reshape(N, 8, 16, NB)[q, g, k, b].astype(np.float32).astype(np.int64), 0)
def first(rng, key, on, cap):
    k = np.where(on, key, 9999); o = np.lexsort((rng.random(k.size), k)); s = k[o]; r = np.empty_like(o)
    r[o] = np.arange(s.size) - np.searchsorted(s, s); return on & (r < cap)
def plant(rng, d, u, sd):
    e = u + 65536 * np.arange(N)[:, None, None]; d["en"] = e.astype(np.int32); g = np.broadcast_to(group(), e.shape).ravel()
    for t in range(EV - 1):
        s = sd + (rng.integers(0, 16, sd.shape) << (8 + 4 * t)); v = event(d["bm"], d["cs"], d["ls"], e, s, t)[1]
        a = (e >> 16).ravel(); z = (v >> 16).ravel()
        ok = first(rng, z * 8 + g, first(rng, (a * N + z) * 8 + g, a != z, LV), AR)
        no = ((a != z) & ~ok).reshape(e.shape); sd = np.where(no, sd, s); e = np.where(no, e, v)
    d["sd"] = sd.astype(np.int32); return d
def sections(c):
    return c.reshape(N, 128, NB).astype(np.int32)
def losses(v):
    v[:, :, 0] = 0; return v.reshape(N, 128, NB).astype(np.float32).astype(BF)
def setup_inputs(rng):
    h = np.zeros((N, 8, BK), np.int64); h[:, :, -1] = 1
    np.put_along_axis(h[..., :-1], np.argsort(rng.random((N, 8, BK - 1)), axis=-1)[..., :NB - 2], 1, -1)
    bm = (np.cumsum(h, axis=-1) - h) * 32 + np.where(h == 1, rng.integers(0, W, h.shape), W)
    c = np.sort(rng.integers(256, 4097, (N, 8, 16, NB)), axis=2); c[:, :, 15] = rng.integers(4096, 8192, (N, 8, NB))
    v = rng.integers(0, 256, c.shape) << rng.integers(0, 11 + 1, c.shape)
    d = {"bm": bm.astype(np.int32), "cs": sections(c), "ls": losses(v), "en": None, "sd": None}
    return plant(rng, d, rng.integers(0, 65536, (N, 8, P)), rng.integers(0, 256, (N, 8, P)))
def setup_inputs_full(rng):
    d = setup_inputs(rng); v = losses(rng.integers(64, 256, (N, 8, 16, NB)) * 512); d["ls"][1:] = v[1:]
    return plant(rng, d, rng.integers(0, 65536, (N, 8, P)), rng.integers(0, 256, (N, 8, P)))
def setup_inputs_ends(rng):
    d = setup_inputs(rng); m = d["bm"]; n = (N, 8, P)
    d["bm"] = np.where((m & 31) < W, (m >> 5) * 32 + rng.choice(np.array([0, 1, W - 1]), m.shape), m).astype(np.int32)
    c = 256 * np.sort(rng.integers(1, 17, (N, 8, 16, NB)), axis=2); c[:, :, 15] = rng.choice(np.array([4096, 8191]), (N, 8, NB)); d["cs"] = sections(c)
    d["ls"] = losses(rng.choice(np.array([0, 1, 1, 2, 255, 32768, 65280, 65536, 131072, 65536 * N]), c.shape))
    u = W * rng.integers(0, BK, n) + rng.choice(np.array([0, 1, W - 1]), n)
    u = np.where(rng.random(n) < 0.25, rng.choice(np.array([0, 1, 65534, 65535]), n), u)
    return plant(rng, d, u, np.zeros(n, np.int64))
def setup_inputs_still(rng):
    d = setup_inputs(rng); w = (N, 8, 16, NB)
    c = np.sort(rng.integers(0, 4097, w), axis=2); c[:, :, 15] = rng.integers(4096, 8192, (N, 8, NB)); d["cs"] = sections(c)
    d["ls"] = rng.integers(1, 256, w).reshape(N, 128, NB).astype(np.float32).astype(BF)
    return plant(rng, d, rng.integers(4096, 65536, (N, 8, P)), rng.integers(0, 256, (N, 8, P)))
def setup_inputs_spread(rng):
    d = setup_inputs(rng); w = (N, 8, 16, NB)
    d["bm"] = ((rng.random((N, 8, BK)) ** 4 * (NB - 1)).astype(np.int64) * 32 + rng.integers(0, W + 1, (N, 8, BK))).astype(np.int32)
    c = 256 + (rng.random(w) ** 3 * 7936).astype(np.int64); c[:, :, 15] = np.maximum(c[:, :, 15], 4096); d["cs"] = sections(c)
    d["ls"] = losses((rng.random(w) ** 4 * 256).astype(np.int64) << rng.integers(0, 11 + 1, w))
    return plant(rng, d, (rng.random((N, 8, P)) ** 4 * 65536).astype(np.int64), rng.integers(0, 256, (N, 8, P)))
def check_inputs(d):
    bad = []; m = d["bm"]; c = d["cs"].reshape(N, 8, 16, NB); v = d["ls"].astype(np.float32); e = d["en"].astype(np.int64); s = d["sd"].astype(np.int64)
    if not ((m >= 0) & ((m >> 5) <= NB - 2) & ((m & 31) <= W)).all(): bad.append("buckets")
    if not ((c >= 0) & (c <= 8191)).all() or not (c[:, :, 15] >= 4096).all(): bad.append("sections")
    if not ((v >= 0) & (v <= 65536 * N) & (v == np.floor(v))).all(): bad.append("losses")
    if not ((e >> 16) == np.arange(N)[:, None, None]).all(): bad.append("energies")
    if not ((s >= 0) & (s < 16 ** (EV + 1))).all(): bad.append("seeds")
    if bad: return bad
    for t in range(EV - 1):
        a = e >> 16; e = event(m, d["cs"], d["ls"], e, s, t)[1]; z = e >> 16
        n = np.bincount(((a * N + z) * 8 + group()).ravel(), minlength=N * N * 8).reshape(N, N, 8)
        if (n[~np.eye(N, dtype=bool)] > LV).any(): bad.append("leavers")
        if (np.sum(n, axis=0) > LIVE).any(): bad.append("live")
    return sorted(set(bad))
def reference(bm, cs, ls, en, sd):
    e = en.astype(np.int64); s = sd.astype(np.int64); tally = np.zeros((N, 8, P, 16), np.int64)
    for t in range(EV):
        c, e = event(bm, cs, ls, e, s, t)
        tally += c
    return {"y": tally.transpose(0, 1, 3, 2).reshape(N, 128, P).astype(np.float32)}

@@ -1,0 +1,561 @@
+import numpy as np
+from concourse.bass import DstId, RemoteDMATransfer
+from concourse.mybir import AluOpType as OP, AxisListType, ActivationFunctionType as AF
+
+N, NP, LV, NB, BAND = 8, 384, 32, 2048, 65536
+NA = LV * (N - 1)
+NW = NP + NA
+OFF = [NW + sum(LV * (N - 1 - j) for j in range(s)) for s in range(N)]
+RW = 72
+EMPTY = float(2 ** 21)
+BIG = 1.0e9
+M13, M16, M20, M23, M0 = (1.5 * 2.0 ** (23 + k) for k in (13, 16, 20, 23, 0))
+
+F32, BF, I32, F16, U16 = "float32", "bfloat16", "int32", "float16", "uint16"
+SB = {
+    "CS": (NB, I32), "LS": (NB, BF), "RB": (512, I32), "RB2": (512, I32), "RB3": (512, I32), "BH": (512, F16), "TB": (4096, F32),
+    "RP": (NP, I32), "RP2": (NP, I32), "RP3": (NP, I32), "P0": (NP, BF), "PA": (NW, BF), "PB": (NW, BF), "L2": (NA, BF),
+    "V0": (NP, F32), "V1": (NW, F32), "BITS": (NW, BF), "LG": (NW, BF), "PR": (NW, BF), "SS": (NW, F32), "DD": (NW, F16),
+    "MK": (NP, BF), "MS": (NP, BF), "GH": (NP, F16), "GM": (NW, F32), "SC": (NW, F32), "D0": (NW, F32), "ONE": (NP, BF),
+    "LB": (40, U16), "LN0": (24, U16), "LN1": (40, U16), "LN2": (40, U16), "LN3": (40, U16),
+    "LS0": (24, U16), "LS1": (40, U16), "LL": (16, U16), "LF": (24, U16), "LF1": (24, U16),
+    "XS": (40, F32), "RR": (40, F32), "B32": (24, I32), "B33": (24, I32), "FR": (24, F32), "TT": (24, F32),
+    "M0": (24, F32), "M1": (40, F32), "M2": (24, F32), "M3": (24, F32), "M4": (24, F32), "K0": (40, F32), "K1": (40, F32),
+    "WIN": (OFF[-1] + NA, BF), "F": (OFF[-1] + NA, F32), "F1": (NW, F32), "T0": (NP, F32), "T1": (NP, F32), "YO": (NP, F32),
+    "S3": (NA, U16), "SG": (2 * NA, U16),
+    "KI": (8, I32), "CT": (64, F32), "OM": (NP, BF), "DIAG": (NP, BF), "EQ": (16, F32), "LT": (24, F32), "D8": (24, F32), "RC": (16, F32),
+    "BL0": (128, BF), "BLK": (128, BF), "ID": (128, BF), "G1": (144, BF), "GW": (144, BF), "GC": (144, BF), "G2": (144, BF),
+    "MX": (128, BF), "MP": (128, BF), "MV0": (128, BF), "MV1": (128, BF), "MB": (128, BF), "NBL": (128, BF), "MD": (128, BF),
+    "HH": (128, BF), "MY": (128, BF), "REP": (1024, BF),
+}
+SCRATCH = {k: ("sbuf", [128, w], d) for k, (w, d) in SB.items()}
+SCRATCH.update({"RA": ("sbuf", [128, N - 1, RW], U16), "LA": ("sbuf", [128, N - 1, RW], U16), "L3": ("sbuf", [128, N - 1, NA], U16)})
+SCRATCH.update({"Q%d" % i: ("psum", [128, 512], F32) for i in range(8)})
+SEMAPHORES = ["cV", "cP", "cS", "cG", "dB", "dP", "dC", "dL", "dY", "a1", "a2", "aR", "gone"] + ["a3%d" % s for s in range(N - 1)]
+
+ARR = {"a1": [19500, 18500, 18500, 19000, 19000, 19500, 17500, 0], "a2": 27000, "aR": 31000, "a3": 34000}
+TAIL = {"s1": 26000, "s2": 15000, "sR": 8000, "s3": 8000}
+AIM = {"a1": 2.0, "a2": 2.0, "aR": 1.0, "a3": 2.0}
+PACE = [dict(c=1.0, g=1.5, s=3.5, p=0.5, y=180, t=1.0, a=1.05), dict(c=0.9, g=1.2, s=2.5, p=0.42, y=100, t=0.85, a=0.9),
+        dict(c=1.2, g=1.9, s=5.0, p=0.7, y=250, t=1.3, a=1.3), dict(c=0.9, g=1.2, s=2.0, p=0.42, y=180, t=1.0, a=1.25),
+        dict(c=1.1, g=1.5, s=4.5, p=0.6, y=100, t=1.0, a=1.0)]
+TRIES = 400
+SEED = 0
+KEPT = {}
+PER = 2
+
+
+def calls(topo, cores, src, dests):
+    me = cores[src]
+    far = [d for d in dests if topo.chip(cores[d]) != topo.chip(me)]
+    near = [d for d in dests if d not in far]
+    out = []
+    used = set()
+    for i in range(0, len(far), PER):
+        part = far[i:i + PER]
+        eng = topo.engines(me, cores[part[0]])
+        used.update(eng)
+        share = [1] * len(part)
+        j = 0
+        while sum(share) + share[j] <= len(eng):
+            share[j] *= 2
+            j = min(range(len(part)), key=lambda x: (share[x], x))
+        call, at = [], 0
+        for d, n in zip(part, share):
+            call.append((d, sum(1 << e for e in eng[at:at + n])))
+            at += n
+        out.append(call)
+    for d in near:
+        eng = [e for e in topo.engines(me, cores[d]) if e not in used][:4]
+        if not out:
+            out.append([])
+        out[0].append((d, sum(1 << e for e in eng)))
+    return out
+
+
+def rank_program(g, core, T, topo):
+    q = T.rank_of(core)
+    if q is None:
+        return
+    cores = T.cores
+    nb = N - 1 - q
+    na = LV * nb
+    C = float(BAND * (q + 1))
+    W2 = OFF[q - 1] + LV if q else NW
+    ops = []
+    eng = {"V": g.vector, "P": g.tensor, "S": g.scalar, "G": g, "Y": g.sync}
+    csem = {"V": "cV", "P": "cP", "S": "cS", "G": "cG"}
+
+    def A(name, a=None, b=None, step=1):
+        if a is None:
+            a, b = 0, T[name].shape[1]
+        elif b is None:
+            b = a + 1
+        ap = T[name][:, a:b:step] if step > 1 else T[name][:, a:b]
+        return (ap, (name, 0, 512) if name[0] == "Q" else (name, a, b), len(range(a, b, step)), SCRATCH[name])
+
+    def A3(name, j0, j1, a, b):
+        return (T[name][:, j0:j1, a:b], (name, j0, j1), (j1 - j0) * (b - a), SCRATCH[name])
+
+    def IND(w, l):
+        return (w[0].indirect(l[0]), w[1], 16 * l[2], w[3], l[1])
+
+    def add(e, fn, out, ins, cost, **kw):
+        rd = [x[1] for x in ins if isinstance(x, tuple)] + [x[4] for x in list(ins) + [out] if isinstance(x, tuple) and len(x) > 4]
+        o = dict(e=e, fn=fn, W=[out[1]] if out else [], R=rd, cost=cost, lat=0, tail=0, sem=None, at=0)
+        o.update(kw)
+        ops.append(o)
+
+    def ap(x):
+        return x[0] if isinstance(x, tuple) else x
+
+    def two(x):
+        return x[3][2] in (BF, F16, U16)
+
+    def cyc(out, i, per):
+        if len(out) > 4:
+            return (50, "s", out[2])
+        if len(i) > 4:
+            return (50, "g", i[2])
+        return (0, "c", max(64, per * i[2]))
+
+    def ts(out, i, s1, s2, o0, o1=None):
+        fn = (lambda: g.vector.tensor_scalar(out[0], i[0], ap(s1), ap(s2), o0, o1)) if o1 is not None else \
+             (lambda: g.vector.tensor_scalar(out[0], i[0], ap(s1), None, o0))
+        add("V", fn, out, [i, s1, s2], cyc(out, i, 0.5 if two(out) and two(i) else 1))
+
+    def tt(out, a, b, o):
+        add("V", lambda: g.vector.tensor_tensor(out[0], a[0], b[0], o), out, [a, b], cyc(out, a, 2 if a[3][0] == b[3][0] else 1))
+
+    def cp(out, i):
+        add("V", lambda: g.vector.tensor_copy(out[0], i[0]), out, [i], cyc(out, i, 0.5 if two(out) and two(i) else 1))
+
+    def ms(out, v, tail=0):
+        add("V", lambda: g.vector.memset(out[0], v), out, [], (0, "c", max(64, out[2] * (0.5 if two(out) else 1))), tail=tail)
+
+    def scan(out, d0, d1, ini, o0, o1):
+        add("V", lambda: g.vector.tensor_tensor_scan(out[0], d0[0], d1[0], ap(ini), o0, o1), out, [d0, d1, ini], (0, "c", max(64, out[2])))
+
+    def act(out, i, scale=1.0, bias=0.0):
+        add("S", lambda: g.scalar.activation(out[0], i[0], AF.Identity, bias=ap(bias), scale=ap(scale)), out, [i, scale, bias], cyc(out, i, 1))
+
+    def mm(out, l, r, start, stop):
+        add("P", lambda: g.tensor.matmul(out[0], l[0], r[0], start, stop), out, [l, r], (0, "p", max(64, r[2])))
+
+    def wrap(bank, G, name, a, b):
+        out = A(bank, 0, (b - a) // 16)
+        add("P", lambda: [g.tensor.matmul(out[0], T[G][:, 15 - p:143 - p], T[name][:, a + p:b:16], p == 0, p == 15) for p in range(16)][-1],
+            out, [A(G), A(name, a, b)], (0, "p", 16 * 64))
+        return out
+
+    def iota(out, pat, base, cm):
+        kw = {} if out[3][2] == I32 else {"allow_small_or_imprecise_dtypes": True}
+        add("G", lambda: g.iota(out[0], pat, base, cm, **kw), out, [], (130, "c", 2 * out[2]))
+
+    def sel(out, i, pat, o, fill, base, cm):
+        add("G", lambda: g.affine_select(out[0], i[0], pat, o, fill, base, cm), out, [i], (170, "c", 2 * out[2]))
+
+    def dma(e, out, src, region, sem, lat, ins=()):
+        add(e, lambda: eng[e].dma_start(out, src), (None, region), list(ins), (60, "t", 0), sem=sem, lat=lat, tail=lat, aim=sem == "dY")
+
+    def arrive(sem, count, regions, at):
+        ops.append(dict(e=None, W=regions, R=[], cost=(0, "t", 0), lat=0, tail=0, sem=sem, cnt=count, at=at))
+
+    sent = [0]
+
+    def send(dests, src, dst, sem, tail):
+        plan = calls(topo, cores, q, dests)
+        for call in plan:
+            tr, rd = [], []
+            for d, mask in call:
+                s = src(d, call)
+                rid, pid = topo.addr(cores[d])[:2]
+                tr.append(RemoteDMATransfer(dst_ids=[DstId(rid=rid, pnc=pid)], dma_engine_mask=mask, remote_sem=T.sem[sem], src=s[0], dst=dst(d, call)))
+                rd.append(s)
+                sent[0] += bin(mask).count("1")
+            add("G", lambda tr=tr: g.remote_dma_fused(tr, local_sem=T.sem.gone), None, rd, (0, "t", 500), tail=tail, aim=AIM[sem[:2]] / len(plan))
+            tail -= 600
+
+    def count(src, dests):
+        return sum(bin(m).count("1") for call in calls(topo, cores, src, dests) for d, m in call if d == q)
+
+    low = lambda r: list(range(r))
+    first = lambda r: low(r)[1:] + low(r)[:1]
+    up = lambda s: list(range(N - 1, s, -1))
+
+    ms(A("RP"), 0)
+    for h in range(2):
+        dma("Y", T.RB[h::2, :], T.bm[:], ("RB", h, h + 1), "dB", 2500)
+    for o in (0, 2, 4):
+        dma("Y", T.RP[o::16, :], T.en[:], ("RP", o, o + 1), "dP", 2500)
+    for o in (8, 9, 10, 11):
+        dma("S", T.RP[o::16, :], T.sd[:], ("RP", o, o + 1), "dP", 2500)
+    dma("Y", T.CS[:], T.cs[:], ("CS", 0, NB), "dC", 5200, [(None, ("order", 0, 1))])
+    dma("Y", T.LS[:], T.ls[:], ("LS", 0, NB), "dL", 6500, [(None, ("order", 0, 1))])
+    for o in ops[1:6]:
+        o["first"] = True
+
+    col = {}
+
+    def c_(name):
+        if name not in col:
+            col[name] = A("CT", len(col))
+        return col[name]
+
+    EQ = lambda i: A("EQ", i)
+    LT = lambda i: A("LT", i)
+    iota(A("KI", 0), [[0, 1]], 0, 1)
+    iota(A("OM", 0, 128), [[0, 8], [1, 16]], 0, 0)
+    iota(A("OM", 128, NP), [[0, NP // 16 - 8], [1, 16]], 0, 0)
+    ms(A("ONE"), 1.0)
+    for j, (m, name) in enumerate(((15, "o"), (1, "par"), (7, "o7"))):
+        ts(A("KI", 2 + 2 * j), A("KI", 0), m, None, OP.bitwise_and)
+        cp(c_(name), A("KI", 2 + 2 * j))
+    ts(c_("sB"), c_("par"), 64 - 1 / 32, 1 / 32, OP.mult, OP.add)
+    ts(c_("cB"), c_("par"), 15.5 / 32, -15.5 / 32, OP.mult, OP.add)
+    ts(A("D8", 0, 8), A("OM", 0, 8), c_("o7"), None, OP.is_lt)
+    ts(A("D8", 8, 16), A("D8", 0, 8), -15 / 16, 1.0, OP.mult, OP.add)
+    ts(A("D8", 16, 24), A("D8", 0, 8), 15.0, 1.0, OP.mult, OP.add)
+    for name, a in (("sP", 8), ("uP", 16)):
+        add("V", lambda name=name, a=a: g.vector.tensor_reduce(c_(name)[0], T.D8[:, a:a + 8], AxisListType.X, OP.mult),
+            c_(name), [A("D8", a, a + 8)], (0, "c", 64))
+    ts(c_("cP"), c_("sP"), 0.5, -0.5, OP.mult, OP.add)
+    ts(A("EQ"), A("OM", 0, 16), c_("o"), None, OP.is_equal)
+    ts(A("LT", 0, 16), A("OM", 0, 16), c_("o"), None, OP.is_gt)
+    ts(A("DIAG"), A("OM"), c_("o"), None, OP.is_equal)
+    act(c_("one"), LT(14), -1.0, 1.0)
+    act(c_("sg"), c_("par"), -2.0, 1.0)
+    act(c_("w"), c_("sg"), LT(5))
+    act(c_("w16"), c_("w"), 1 / 16)
+    act(c_("wx0"), EQ(14), -4096.0, c_("w"))
+    act(c_("wx"), EQ(15), 0.5, c_("wx0"))
+    ts(c_("v0"), EQ(8), EQ(10), EQ(11), OP.add, OP.subtract)
+    ts(c_("v1"), EQ(9), EQ(11), 1 / 16, OP.add, OP.mult)
+    act(c_("v15"), EQ(15), 8192.0)
+    act(c_("g2"), c_("par"), -2 - 1 / 1024, 2.0)
+    tt(A("RC", 0, 8), A("EQ", 0, 16, 2), A("EQ", 1, 16, 2), OP.add)
+    act(A("RC", 8, 16), A("RC", 0, 8), c_("g2"))
+    ts(c_("sg0"), c_("o"), c_("par"), 4096.0, OP.subtract, OP.mult)
+    ts(c_("seg"), c_("sg0"), M13 + BAND * q, None, OP.add)
+    act(c_("ya"), EQ(15), -2.0 ** 20)
+    act(c_("yb"), LT(15), 2.0 ** 20)
+    act(c_("nc"), LT(15), -C)
+    sel(A("BL0"), A("ONE", 0, 128), [[16, 8], [0, 16]], OP.is_ge, 0.0, 15, -1)
+    sel(A("BLK"), A("BL0"), [[-16, 8], [0, 16]], OP.is_ge, 0.0, 0, 1)
+    ms(A("G1", 128, 144), 0.0)
+    sel(A("G1", 0, 128), A("BLK"), [[0, 8], [1, 16]], OP.is_equal, 0.0, -15, 0)
+    sel(A("ID"), A("ONE", 0, 128), [[-1, 128]], OP.is_equal, 0.0, 0, 1)
+    iota(A("K0"), [[16, 40]], 1, 0)
+    act(A("K1"), A("K0"), 1.0, c_("o"))
+    act(A("GW"), A("G1"), c_("w16"))
+    act(A("G2"), A("G1"), c_("g2"))
+    act(A("GC"), A("G1"), c_("nc"))
+    act(A("MX"), A("BLK"), c_("wx"))
+    act(A("MV0"), A("BLK"), c_("v0"))
+    act(A("MV1"), A("BLK"), c_("v1"))
+    act(A("HH"), A("OM", 0, 128), c_("ya"), c_("yb"))
+    tt(A("MY"), A("HH"), A("BLK"), OP.mult)
+    for s in range(8):
+        act(A("REP", 128 * s, 128 * s + 128), A("BLK"), A("RC", 8 + s))
+    ms(A("D0", 0, NP), BIG)
+    ms(A("D0", NP, NW), BIG)
+    if q:
+        act(A("MP"), A("BLK"), c_("w"))
+        act(A("NBL"), A("BLK"), -1.0)
+        act(c_("pc"), LT(15), C)
+        act(c_("dead"), LT(q), EMPTY)
+        act(A("MD"), A("BLK"), c_("dead"))
+        act(A("MB"), A("BLK"), c_("pc"))
+        sel(A("MB"), A("MB"), [[0, 128]], OP.not_equal, -BAND / 2, -15, 1)
+        sel(A("MB"), A("MB"), [[0, 128]], OP.not_equal, 0.5, -31, 1)
+        sel(A("MB"), A("MB"), [[0, 8], [1, 16]], OP.not_equal, -8.5 * BAND, -16 * 47, 16)
+        sel(A("MB"), A("MB"), [[0, 8], [1, 16]], OP.not_equal, -BAND * (63.5 + q), -16 * 63 - q, 16)
+        ts(c_("s1a"), EQ(0), M20 - M16, M16, OP.mult, OP.add)
+        ts(c_("s1"), EQ(q), M23 - M16, c_("s1a"), OP.mult, OP.add)
+        ts(c_("s2a"), c_("o"), float(BAND), c_("s1"), OP.mult, OP.add)
+        ts(c_("s2"), EQ(0), -2.0 ** 20, c_("s2a"), OP.mult, OP.add)
+        act(c_("i0a"), c_("o"), -float(LV), float(W2 + LV * (q - 1)))
+        act(c_("i0"), c_("i0a"), LT(q))
+        act(c_("i1a"), c_("o"), -LV / 2, LV * (N - 1.5))
+        act(c_("i1b"), c_("i1a"), c_("o"), float(NW + LV * (q - 1)))
+        act(c_("i1"), c_("i1b"), LT(q))
+        ms(A("WIN", NW, W2 + LV * q), EMPTY)
+        if nb:
+            for a in [NP + LV * q] + [OFF[s] + LV * (q - s) for s in range(q - 1)]:
+                ms(A("F", a, a + na), 0.0, 12000)
+    if nb:
+        ms(A3("RA", 0, nb, 64, RW), 0)
+
+    ts(A("RB2"), A("RB"), c_("sB"), c_("cB"), OP.mult, OP.add)
+    ts(A("RB3"), A("RB2"), 2047, None, OP.bitwise_and)
+    ts(A("RP2"), A("RP"), c_("sP"), c_("cP"), OP.mult, OP.add)
+    ts(A("RP3"), A("RP2"), 255, None, OP.bitwise_and)
+    ts(A("P0"), A("RP3"), c_("uP"), c_("one"), OP.mult, OP.add)
+    cp(A("BH"), A("RB3"))
+    for s in range(8):
+        bank = "Q%d" % (6 + s % 2)
+        mm(A(bank, 0, 512), A("REP", 128 * s, 128 * s + 128), A("BH"), True, True)
+        act(A("TB", 512 * s, 512 * s + 512), A(bank, 0, 512), 1.0, 2.0)
+    xc = -(BAND // 16) * q - 7.5 / 16
+
+    def seeds(out, M, pay, a, b, bank):
+        mm(A(bank, 0, b - a), A(M), A(pay, a, b), True, True)
+        act(A(out, a, b), A(bank, 0, b - a), 1.0, c_("v15"))
+
+    def lookup(pay, a, b, at, bank, LN):
+        n = b - a
+        k, ka = n // 16, at // 16
+        x = wrap(bank, "GW", pay, a, b)
+        ts(A("LB", ka, ka + k), x, xc, 4095.0, OP.add, OP.min)
+        ts(A("XS", ka, ka + k), x, xc, -7.5 / 16, OP.add, OP.max)
+        ts(A("RR", ka, ka + k), A("XS", ka, ka + k), M0, M0, OP.add, OP.subtract)
+        tt(A("GM", at, at + n), IND(A("TB"), A("LB", ka, ka + k)), A("DIAG", 0, n), OP.mult)
+        tt(A("D0", at, at + n, 16), A("XS", ka, ka + k), A("RR", ka, ka + k), OP.subtract)
+        scan(A("SC", at, at + n), A("D0", at, at + n), A("GM", at, at + n), BIG, OP.min, OP.add)
+        ts(A(LN, ka, ka + k), A("SC", at + 15, at + n, 16), 0.5, -0.25, OP.mult, OP.add)
+
+    def spread(pay, LN):
+        k = NP // 16
+        x = wrap("Q5", "GW", pay, 0, NP)
+        mm(A("Q4", 0, NP), A("MX"), A(pay, 0, NP), True, True)
+        ts(A("MS"), A("Q4", 0, NP), M13, c_("seg"), OP.add, OP.is_equal)
+        ts(A("B32"), x, xc, None, OP.add)
+        ts(A("B33"), A("B32"), 511, None, OP.bitwise_and)
+        cp(A("LB", 0, k), A("B33"))
+        tt(A("FR"), x, A("B32"), OP.subtract)
+        tt(A("GH"), IND(A("RB3"), A("LB", 0, k)), A("MS"), OP.mult)
+        tt(A("TT"), wrap("Q5", "G2", "GH", 0, NP), A("FR"), OP.add)
+        ts(A(LN, 0, k), A("TT"), 0.5, 0.75 + xc / 2, OP.mult, OP.add)
+
+    def event(t, old, new, V, parts, lst, init, wend):
+        p = 1 + 2 * t
+        for a, b, bY, bX, bB in parts:
+            B = A(bB, 0, b - a)
+            mm(B, A("ID"), A(old, a, b), True, False)
+            ln = A("LN%d" % t, a // 16, b // 16)
+            Y, X = A(bY, 0, b - a), A(bX, 0, b - a)
+            act(A("LG", a, b), IND(A("LS"), ln))
+            tt(A("BITS", a, b), IND(A("CS"), ln), A(V, a, b), OP.is_le)
+            if q:
+                mm(X, A("MP"), A(old, a, b), True, False)
+                if t and a < NP:
+                    mm(X, A("MD"), A("MK", a, b), False, False)
+            mm(Y, A("ID"), A("LG", a, b), True, False)
+            mm(Y, A("MY"), A("BITS", a, b), False, True)
+            ts(A("PR", a, b), Y, 0.0, C, OP.max, OP.min)
+            if q:
+                mm(X, A("MB"), A("BITS", a, b), False, False)
+                mm(X, A("NBL"), A("PR", a, b), False, True)
+            mm(B, A("GC", 15 - p, 143 - p), A("BITS", a, b), False, False)
+            mm(B, A("G1", 15 - p, 143 - p), A("PR", a, b), False, True)
+            act(A(new, a, b), B)
+        for a, b, bY, bX, bB in parts if q else ():
+            ka, kb = a // 16, b // 16
+            D, X = A(bY, 0, b - a), A(bX, 0, b - a)
+            ts(D, X, c_("s1"), c_("s2"), OP.add, OP.is_equal)
+            scan(A("SS", a, b), A("ONE", 0, b - a), D, init, OP.mult, OP.add)
+            init = A("SS", b - 1)
+            tt(A("DD", a, b), A("SS", a, b), D, OP.mult)
+            if t == 0:
+                act(A("MK", a, b), D)
+            x = wrap(bX, "G1", "DD", a, b)
+            ts(A(lst, ka, kb), x, -1.0, None, OP.add)
+            cp(IND(A("WIN", 0, wend), A(lst, ka, kb)), A(new, a, b))
+            tt(A("M%d" % t, ka, kb), x, A("K1", ka, kb), OP.max)
+
+    own = [(0, NP // 2, "Q0", "Q1", "Q4"), (NP // 2, NP, "Q2", "Q3", "Q5")]
+
+    k = NP // 16
+    seeds("V0", "MV0", "P0", 0, NP, "Q0")
+    seeds("V1", "MV1", "P0", 0, NP, "Q2")
+    spread("P0", "LN0")
+    event(0, "P0", "PA", "V0", own, "LS0", c_("i0") if q else None, W2 + LV * q)
+    cp(A("T0"), IND(A("CS"), A("LN0", 0, k)))
+    send(first(q), lambda d, c: A("WIN", W2 + LV * (q - d - 1), W2 + LV * (q - d)),
+         lambda d, c: T.PA[:, NP + LV * (q - d - 1):NP + LV * (q - d)], "a1", TAIL["s1"])
+
+    if q:
+        spread("PA", "LN1")
+    else:
+        lookup("PA", 0, NP, 0, "Q5", "LN1")
+    event(1, "PA", "PB", "V1", own, "LS1", c_("i1") if q else None, W2)
+    if q:
+        cp(A("F1", 0, NP), IND(A("CS"), A("LN1", 0, k)))
+    else:
+        tt(A("T1"), IND(A("CS"), A("LN1", 0, k)), A("T0"), OP.add)
+    e, ke = NP + na, (NP + na) // 16
+    if nb:
+        arrive("a1", sum(count(r, first(r)) for r in up(q)), [("PA", NP, e)], ARR["a1"][q])
+        lookup("PA", NP, e, NP, "Q7", "LN1")
+        seeds("V1", "MV1", "PA", NP, e, "Q6")
+        event(1, "PA", "PB", "V1", [(NP, e, "Q6", "Q7", "Q4")], "LS1", A("SS", NP - 1), W2)
+        cp(A("SG", 0, na), IND(A("CS"), A("LN1", k, ke)))
+        cp(A3("RA", 0, nb, 0, LV), A("SG", 0, na))
+        ts(A3("RA", 0, nb, 64, 66), A("M1" if q else "K1", k, ke), -1.0, None, OP.add)
+    send(low(q), lambda d, c: A("WIN", OFF[d] + LV * (q - d - 1), OFF[d] + LV * (q - d)),
+         lambda d, c: T.L2[:, LV * (q - d - 1):LV * (q - d)], "a2", TAIL["s2"])
+
+    lookup("PB", 0, NP, 0, "Q5", "LN2")
+    if q:
+        cp(A("F", 0, NP), IND(A("CS"), A("LN2", 0, k)))
+    else:
+        tt(A("YO"), IND(A("CS"), A("LN2", 0, k)), A("T1"), OP.add)
+        dma("Y", T.y[:], T.YO[:], ("y", 0, 1), "dY", 2500, [A("YO")])
+    if nb:
+        lookup("PB", NP, e, NP, "Q4", "LN2")
+        cp(A("SG", NA, NA + na), IND(A("CS"), A("LN2", k, ke)))
+        cp(A3("RA", 0, nb, LV, 2 * LV), A("SG", NA, NA + na))
+        send(up(q), lambda d, c: A3("RA", d - q - 1, d - q, 0, RW), lambda d, c: T.LA[:, d - q - 1:d - q, :], "aR", TAIL["sR"])
+        arrive("a2", sum(count(r, low(r)) for r in up(q)), [("L2", 0, na)], ARR["a2"])
+        lookup("L2", 0, na, NP, "Q6", "LN3")
+        cp(A("S3", 0, na), IND(A("CS"), A("LN3", k, ke)))
+        wide = lambda c: LV * (max(d for d, m in c) - q)
+        send(up(q), lambda d, c: A("S3", 0, wide(c)), lambda d, c: T.L3[:, q, 0:wide(c)], "a3%d" % q, TAIL["s3"])
+
+    if q:
+        m = LV * q
+        tt(A("M2"), A("M1", 0, k), A("M0"), OP.max)
+        ts(A("LF"), A("M2"), -1.0, None, OP.add)
+        ts(A("M3"), A("M0"), float(NP - W2), None, OP.add)
+        tt(A("M4"), A("M3"), A("K1", 0, k), OP.max)
+        ts(A("LF1"), A("M4"), -1.0, None, OP.add)
+        arrive("aR", sum(count(s, up(s)) for s in low(q)), [("LA", 0, q)], ARR["aR"])
+        cp(A("F1", NP, NP + m), A3("LA", 0, q, 0, LV))
+        cp(A("F", NP, NP + m), A3("LA", 0, q, LV, 2 * LV))
+        cp(A("LL", 0, 2 * q), A3("LA", 0, q, 64, 66))
+        tt(A("T1"), IND(A("F1", 0, NP + m), A("LF1")), A("T0"), OP.add)
+        for s in low(q):
+            arrive("a3%d" % s, count(s, up(s)), [("L3", s, s + 1)], ARR["a3"] - 100 * s)
+            cp(A("F", OFF[s], OFF[s] + LV * (q - s)), A3("L3", s, s + 1, 0, LV * (q - s)))
+        cp(A("F", W2, W2 + m), IND(A("F", 0, W2), A("LL", 0, 2 * q)))
+        for h, x in enumerate("YS"):
+            a, b = h * NP // 2, (h + 1) * NP // 2
+            tt(A("YO", a, b), IND(A("F", 0, W2 + m), A("LF", a // 16, b // 16)), A("T1", a, b), OP.add)
+            dma(x, T.y[:, a:b], T.YO[:, a:b], ("y", h, h + 1), "dY", 2500, [A("YO", a, b)])
+
+    hit = lambda x, y: x[1] < y[2] and y[1] < x[2]
+    acc = {}
+    for i, o in enumerate(ops):
+        dep = {}
+        for r in o["R"]:
+            for j, x, w in acc.get(r[0], ()):
+                if hit(r, x) and (w or (r[0][0] == "Q" and ops[j]["e"] != o["e"])):
+                    dep[j] = True
+        for r in o["W"]:
+            for j, x, w in acc.get(r[0], ()):
+                if hit(r, x) and o["e"] is not None:
+                    dep[j] = True
+        if o["R"] and o["R"][0][0] == "order":
+            dep = {j: None for j in range(i) if ops[j].get("first") or ops[j]["sem"] == "dC"}
+        o["dep"] = dep
+        for r in o["R"]:
+            acc.setdefault(r[0], []).append((i, r, False))
+        for r in o["W"]:
+            acc.setdefault(r[0], []).append((i, r, True))
+
+    def free(j, o):
+        return o["dep"][j] is None or ops[j]["e"] == o["e"] == "P"
+
+    def span(o, m):
+        return o["cost"][0] + m[o["cost"][1]] * o["cost"][2]
+
+    def gap(j, o, m):
+        return 0 if free(j, o) else (ops[j]["lat"] * m["t"] if ops[j]["sem"] else m["y"])
+
+    def place(noise):
+        m = PACE[0]
+        tail = [o["tail"] for o in ops]
+        for i in range(len(ops) - 1, -1, -1):
+            o = ops[i]
+            tail[i] += span(o, m) + noise[i]
+            for j in o["dep"]:
+                tail[j] = max(tail[j], tail[i] + gap(j, o, m))
+        at, busy = [0] * len(ops), {x: [] for x in eng}
+        for i in sorted(range(len(ops)), key=lambda i: (-tail[i], i)):
+            o = ops[i]
+            d = span(o, m)
+            t = max([o["at"]] + [at[j] + span(ops[j], m) + gap(j, o, m) for j in o["dep"]])
+            if o["e"]:
+                row = busy[o["e"]]
+                n = len(row)
+                for x, (a, b, j) in enumerate(row):
+                    if t + d <= a:
+                        n = x
+                        break
+                    t = max(t, b)
+                row.insert(n, (t, t + d, i))
+            at[i] = t
+        return at, busy
+
+    def worth(at):
+        v = 0
+        order = sorted(range(len(ops)), key=lambda i: (at[i], i))
+        for m in PACE:
+            end, last = [0] * len(ops), {}
+            for i in order:
+                o = ops[i]
+                t = max([o["at"] * m["a"], last.get(o["e"], 0)] + [end[j] + gap(j, o, m) for j in o["dep"]])
+                end[i] = t + span(o, m)
+                if o["e"]:
+                    last[o["e"]] = end[i]
+                v += o.get("aim", 0) * end[i] / m["t"]
+        return v
+
+    rng = np.random.default_rng(q + SEED)
+    noise = KEPT.get(q, [0.0] * len(ops))
+    at, busy = place(noise)
+    best = worth(at)
+    for it in range(0 if q in KEPT else TRIES):
+        new = [max(0.0, x + float(r)) if u < (0.02, 0.1)[it % 2] else x
+               for x, r, u in zip(noise, rng.normal(0, (1500, 400)[it % 2], len(ops)), rng.random(len(ops)))]
+        a2, b2 = place(new)
+        v = worth(a2)
+        if v < best:
+            best, noise, at, busy = v, new, a2, b2
+    KEPT[q] = noise
+    for i, o in enumerate(ops):
+        o["at"] = at[i]
+
+    total = {}
+    for o in ops:
+        if o["sem"]:
+            total[o["sem"]] = o.get("cnt", total.get(o["sem"], 0) + 16)
+    need = set()
+    for x in eng:
+        seen = {}
+        for a, b, i in busy[x]:
+            o = ops[i]
+            o["waits"] = []
+            for j in sorted(o["dep"], key=lambda j: -ops[j]["at"]):
+                p = ops[j]
+                if free(j, o):
+                    continue
+                key = p["sem"] or p["e"]
+                if seen.get(key, -1) < (0 if p["sem"] else p["at"]):
+                    seen[key] = 0 if p["sem"] else p["at"]
+                    o["waits"].append(j)
+                    need.add(j)
+    num = {}
+    for x in csem:
+        n = 0
+        for a, b, i in busy[x]:
+            if i in need and not ops[i]["sem"]:
+                n += 1
+                num[i] = n
+    for x in eng:
+        for a, b, i in busy[x]:
+            o = ops[i]
+            for j in o["waits"]:
+                p = ops[j]
+                if p["sem"]:
+                    eng[x].wait_ge(T.sem[p["sem"]], total[p["sem"]])
+                else:
+                    eng[x].wait_ge(T.sem[csem[p["e"]]], num[j])
+            ins = o["fn"]()
+            if o["sem"]:
+                ins.then_inc(T.sem[o["sem"]], 16)
+            elif i in num:
+                ins.then_inc(T.sem[csem[x]], 1)
+    g.sync.wait_ge(T.sem.dY, total["dY"])
+    if sent[0]:
+        g.wait_ge(T.sem.gone, sent[0])

@@ -3,56 +3,66 @@ from concourse.bass import DstId, RemoteDMATransfer
 from concourse.mybir import AluOpType as OP, AxisListType, ActivationFunctionType as AF
 
 N, NP, LV, NB, BAND = 8, 384, 32, 2048, 65536
+BK = BAND // 16
 NA = LV * (N - 1)
 NW = NP + NA
-OFF = [NW + sum(LV * (N - 1 - j) for j in range(s)) for s in range(N)]
-RW = 72
-EMPTY = float(2 ** 21)
-BIG = 1.0e9
-M13, M16, M20, M23, M0 = (1.5 * 2.0 ** (23 + k) for k in (13, 16, 20, 23, 0))
+W3 = LV * N
+N3 = LV * (N + 2) * (N - 1) // 2
+Z = 8
+RW = 34
+EMPTY = 64.0
+M16, M20, M23 = (1.5 * 2.0 ** (23 + k) for k in (16, 20, 23))
+HALF = 7.5 / 16
 
 F32, BF, I32, F16, U16 = "float32", "bfloat16", "int32", "float16", "uint16"
 SB = {
-    "CS": (NB, I32), "LS": (NB, BF), "RB": (512, I32), "RB2": (512, I32), "RB3": (512, I32), "BH": (512, F16), "TB": (4096, F32),
-    "RP": (NP, I32), "RP2": (NP, I32), "RP3": (NP, I32), "P0": (NP, BF), "PA": (NW, BF), "PB": (NW, BF), "L2": (NA, BF),
-    "V0": (NP, F32), "V1": (NW, F32), "BITS": (NW, BF), "LG": (NW, BF), "PR": (NW, BF), "SS": (NW, F32), "DD": (NW, F16),
-    "MK": (NP, BF), "MS": (NP, BF), "GH": (NP, F16), "GM": (NW, F32), "SC": (NW, F32), "D0": (NW, F32), "ONE": (NP, BF),
-    "LB": (40, U16), "LN0": (24, U16), "LN1": (40, U16), "LN2": (40, U16), "LN3": (40, U16),
-    "LS0": (24, U16), "LS1": (40, U16), "LL": (16, U16), "LF": (24, U16), "LF1": (24, U16),
-    "XS": (40, F32), "RR": (40, F32), "B32": (24, I32), "B33": (24, I32), "FR": (24, F32), "TT": (24, F32),
-    "M0": (24, F32), "M1": (40, F32), "M2": (24, F32), "M3": (24, F32), "M4": (24, F32), "K0": (40, F32), "K1": (40, F32),
-    "WIN": (OFF[-1] + NA, BF), "F": (OFF[-1] + NA, F32), "F1": (NW, F32), "T0": (NP, F32), "T1": (NP, F32), "YO": (NP, F32),
-    "S3": (NA, U16), "SG": (2 * NA, U16),
-    "KI": (8, I32), "CT": (64, F32), "OM": (NP, BF), "DIAG": (NP, BF), "EQ": (16, F32), "LT": (24, F32), "D8": (24, F32), "RC": (16, F32),
-    "BL0": (128, BF), "BLK": (128, BF), "ID": (128, BF), "G1": (144, BF), "GW": (144, BF), "GC": (144, BF), "G2": (144, BF),
+    "CS": (Z + NB, I32), "LS": (Z + NB, BF), "RB": (512, I32), "RB2": (512, I32), "RB3": (512, I32), "TB": (BK + 2 * Z, I32),
+    "XN": (184, F32), "RP": (NP, I32), "RP2": (NP, I32), "RP3": (NP, I32), "P0": (NP, BF), "PA": (NW, BF), "PB": (NP, BF),
+    "V0": (NP, F32), "V1": (NW, F32), "BITS": (NW, BF), "LG": (NW, BF), "PR": (NW, BF), "SS": (NP, F32), "DD": (NP, F16),
+    "MK": (NP, BF), "MS": (NP, BF), "GH": (NW, F16), "G3H": (N3, F16), "ONE": (256, BF),
+    "LB": (184, U16), "LN": (184, U16), "XS": (184, F32), "L2": (16 * N, F32),
+    "LS0": (24, U16), "LS1": (24, U16), "LL": (16, U16), "LF": (24, U16), "PL": (6, U16), "PLC": (80, BF),
+    "M0": (24, F32), "M1": (24, F32), "K0": (16, F32), "LL1": (16, F32), "LL2": (16, F32),
+    "WIN": (NP + 2 * NA, BF), "FA": (Z + 2 * NA, F32), "FB": (LV * (N - 1) ** 2, F32), "T0": (NP, F32), "T1": (NP, F32), "T2": (NP, F32),
+    "YO": (NP, F32), "S3": (N3, U16), "SG": (NA, F32), "A12": (NA, F32), "S2": (NA, U16), "L0": (LV, U16), "AF": (NA, F32),
+    "KI": (8, I32), "CT": (64, F32), "OM": (128, BF), "EQ": (16, F32), "LT": (16, F32), "D8": (8, F32),
+    "BL0": (128, BF), "BLK": (128, BF), "ID": (128, BF), "I32": (128, F32), "G1": (144, BF), "GY": (144, BF), "GW": (144, BF),
+    "GC": (144, BF), "G2": (144, BF), "GK": (144, BF), "GN": (144, BF),
     "MX": (128, BF), "MP": (128, BF), "MV0": (128, BF), "MV1": (128, BF), "MB": (128, BF), "NBL": (128, BF), "MD": (128, BF),
-    "HH": (128, BF), "MY": (128, BF), "REP": (1024, BF),
+    "HH": (128, BF), "BN": (128, BF), "MY": (128, BF),
 }
 SCRATCH = {k: ("sbuf", [128, w], d) for k, (w, d) in SB.items()}
-SCRATCH.update({"RA": ("sbuf", [128, N - 1, RW], U16), "LA": ("sbuf", [128, N - 1, RW], U16), "L3": ("sbuf", [128, N - 1, NA], U16)})
+SCRATCH.update({"RA": ("sbuf", [128, N - 1, RW], U16), "LA": ("sbuf", [128, N - 1, RW], U16), "L3": ("sbuf", [128, N - 1, W3], U16)})
 SCRATCH.update({"Q%d" % i: ("psum", [128, 512], F32) for i in range(8)})
-SEMAPHORES = ["cV", "cP", "cS", "cG", "dB", "dP", "dC", "dL", "dY", "a1", "a2", "aR", "gone"] + ["a3%d" % s for s in range(N - 1)]
+SEMAPHORES = ["cV", "cP", "cS", "cG", "dB", "dP", "dC", "dL", "dT", "dY", "a1", "a2", "aR", "aS", "gone"] + ["a3%d" % s for s in range(N - 1)]
 
-ARR = {"a1": [19500, 18500, 18500, 19000, 19000, 19500, 17500, 0], "a2": 27000, "aR": 31000, "a3": 34000}
-TAIL = {"s1": 26000, "s2": 15000, "sR": 8000, "s3": 8000}
-AIM = {"a1": 2.0, "a2": 2.0, "aR": 1.0, "a3": 2.0}
-PACE = [dict(c=1.0, g=1.5, s=3.5, p=0.5, y=180, t=1.0, a=1.05), dict(c=0.9, g=1.2, s=2.5, p=0.42, y=100, t=0.85, a=0.9),
-        dict(c=1.2, g=1.9, s=5.0, p=0.7, y=250, t=1.3, a=1.3), dict(c=0.9, g=1.2, s=2.0, p=0.42, y=180, t=1.0, a=1.25),
-        dict(c=1.1, g=1.5, s=4.5, p=0.6, y=100, t=1.0, a=1.0)]
-TRIES = 400
-SEED = 0
+ARR = {"a1": [15400, 15400, 16000, 16000, 16700, 16700, 15200, 0], "a2": [22400, 22800, 23400, 23400, 23200, 23200, 20000], "aR": 26000,
+       "a3": [27500, 27500, 28000, 28000, 27500, 27500, 24000]}
+TAIL = {"s1": 22000, "s2": 12000, "sR": 8000, "s3": 6500, "tb": 25500}
+AIM = {"a1": 2.0, "a2": 2.0, "aR": 0.5, "aS": 0.5, "a3": 2.0, "tb": 0.1}
+DUE = {"a1": [0, 13500, 13500, 13500, 13500, 13500, 13000, 13000], "a2": [0, 19800, 19500, 19500, 19500, 19500, 19800, 20500],
+       "aS": [22000], "aR": [20500, 22500, 23500, 23500, 24500, 24500, 25000], "a3": [24500, 25000, 26000, 26000, 27500, 27500, 28000]}
+PACE = [dict(c=0.95, g=1.4, s=3.2, p=0.47, y=100, t=0.9, w=1.05, a=1.0), dict(c=0.9, g=1.3, s=2.8, p=0.45, y=90, t=0.87, w=0.95, a=0.92),
+        dict(c=1.15, g=1.8, s=4.5, p=0.58, y=140, t=0.95, w=1.45, a=1.19), dict(c=0.87, g=1.1, s=2.0, p=0.43, y=120, t=1.0, w=1.3, a=1.03),
+        dict(c=1.1, g=1.3, s=4.5, p=0.5, y=80, t=0.85, w=0.9, a=1.03)]
+TRIES = 8000
+HEAT = 4000
 KEPT = {}
 PER = 2
+ALONE = {"a1": 0, "a2": 2, "aR": 0, "a3": 6}
+LATE = ()
+SPLIT = 0.4
+ORD1 = [0, 1, 2, 3, 4, 5, 6]
 
 
 def calls(topo, cores, src, dests):
     me = cores[src]
+    dests, alone = dests
     far = [d for d in dests if topo.chip(cores[d]) != topo.chip(me)]
     near = [d for d in dests if d not in far]
     out = []
     used = set()
-    for i in range(0, len(far), PER):
-        part = far[i:i + PER]
+    for part in [far[i:i + 1] for i in range(min(alone, len(far)))] + [far[i:i + PER] for i in range(alone, len(far), PER)]:
         eng = topo.engines(me, cores[part[0]])
         used.update(eng)
         share = [1] * len(part)
@@ -79,9 +89,9 @@ def rank_program(g, core, T, topo):
         return
     cores = T.cores
     nb = N - 1 - q
-    na = LV * nb
+    na, m = LV * nb, LV * q
     C = float(BAND * (q + 1))
-    W2 = OFF[q - 1] + LV if q else NW
+    W1, W0 = NP, NP + m
     ops = []
     eng = {"V": g.vector, "P": g.tensor, "S": g.scalar, "G": g, "Y": g.sync}
     csem = {"V": "cV", "P": "cP", "S": "cS", "G": "cG"}
@@ -100,9 +110,9 @@ def rank_program(g, core, T, topo):
     def IND(w, l):
         return (w[0].indirect(l[0]), w[1], 16 * l[2], w[3], l[1])
 
-    def add(e, fn, out, ins, cost, **kw):
+    def add(alt, out, ins, **kw):
         rd = [x[1] for x in ins if isinstance(x, tuple)] + [x[4] for x in list(ins) + [out] if isinstance(x, tuple) and len(x) > 4]
-        o = dict(e=e, fn=fn, W=[out[1]] if out else [], R=rd, cost=cost, lat=0, tail=0, sem=None, at=0)
+        o = dict(alt=alt, W=[out[1]] if out else [], R=rd, lat=0, tail=0, sem=None, at=0)
         o.update(kw)
         ops.append(o)
 
@@ -119,49 +129,70 @@ def rank_program(g, core, T, topo):
             return (50, "g", i[2])
         return (0, "c", max(64, per * i[2]))
 
-    def ts(out, i, s1, s2, o0, o1=None):
+    def vts(out, i, s1, s2, o0, o1):
         fn = (lambda: g.vector.tensor_scalar(out[0], i[0], ap(s1), ap(s2), o0, o1)) if o1 is not None else \
              (lambda: g.vector.tensor_scalar(out[0], i[0], ap(s1), None, o0))
-        add("V", fn, out, [i, s1, s2], cyc(out, i, 0.5 if two(out) and two(i) else 1))
+        return fn, cyc(out, i, 0.5 if two(out) and two(i) else 1)
+
+    def sact(out, i, scale, bias, f):
+        return (lambda: g.scalar.activation(out[0], i[0], f, bias=ap(bias), scale=ap(scale))), cyc(out, i, 1)
+
+    def ts(out, i, s1, s2, o0, o1=None, **kw):
+        add({"V": vts(out, i, s1, s2, o0, o1)}, out, [i, s1, s2], **kw)
+
+    def lin(out, i, scale=1.0, bias=0.0, on="VS", **kw):
+        f = AF.Relu if out[3][2] == U16 else AF.Identity
+        if (scale, bias) == (1.0, 0.0):
+            v = (lambda: g.vector.tensor_copy(out[0], i[0])), cyc(out, i, 0.5 if two(out) and two(i) else 1)
+        else:
+            v = vts(out, i, scale, bias, OP.mult, OP.add)
+        alt = {"V": v, "S": sact(out, i, scale, bias, f)}
+        add({e: alt[e] for e in on}, out, [i, scale, bias], **kw)
+
+    def relu(out, i):
+        add({"V": vts(out, i, 0.0, None, OP.max, None), "S": sact(out, i, 1.0, 0.0, AF.Relu)}, out, [i])
 
     def tt(out, a, b, o):
-        add("V", lambda: g.vector.tensor_tensor(out[0], a[0], b[0], o), out, [a, b], cyc(out, a, 2 if a[3][0] == b[3][0] else 1))
+        add({"V": (lambda: g.vector.tensor_tensor(out[0], a[0], b[0], o), cyc(out, a, 2 if a[3][0] == b[3][0] else 1))}, out, [a, b])
 
-    def cp(out, i):
-        add("V", lambda: g.vector.tensor_copy(out[0], i[0]), out, [i], cyc(out, i, 0.5 if two(out) and two(i) else 1))
+    def ms(out, v, **kw):
+        add({"V": (lambda: g.vector.memset(out[0], v), (0, "c", max(64, out[2] * (0.5 if two(out) else 1))))}, out, [], **kw)
 
-    def ms(out, v, tail=0):
-        add("V", lambda: g.vector.memset(out[0], v), out, [], (0, "c", max(64, out[2] * (0.5 if two(out) else 1))), tail=tail)
+    def fill(name, a, b, v, **kw):
+        for x in range(a, b, 256):
+            out, one = A(name, x, min(b, x + 256)), A("ONE", 0, min(b, x + 256) - x)
+            alt = {"V": (lambda out=out: g.vector.memset(out[0], v), (0, "c", max(64, out[2] * (0.5 if two(out) else 1)))),
+                   "S": sact(out, one, float(v), 0.0, AF.Identity)}
+            if out[3][2] == I32:
+                alt["G"] = (lambda out=out: g.iota(out[0], [[0, out[2]]], v, 0), (130, "c", 2 * out[2]))
+            add(alt, out, [one], **kw)
 
     def scan(out, d0, d1, ini, o0, o1):
-        add("V", lambda: g.vector.tensor_tensor_scan(out[0], d0[0], d1[0], ap(ini), o0, o1), out, [d0, d1, ini], (0, "c", max(64, out[2])))
-
-    def act(out, i, scale=1.0, bias=0.0):
-        add("S", lambda: g.scalar.activation(out[0], i[0], AF.Identity, bias=ap(bias), scale=ap(scale)), out, [i, scale, bias], cyc(out, i, 1))
+        add({"V": (lambda: g.vector.tensor_tensor_scan(out[0], d0[0], d1[0], ap(ini), o0, o1), (0, "c", max(64, out[2])))}, out, [d0, d1, ini])
 
     def mm(out, l, r, start, stop):
-        add("P", lambda: g.tensor.matmul(out[0], l[0], r[0], start, stop), out, [l, r], (0, "p", max(64, r[2])))
+        add({"P": (lambda: g.tensor.matmul(out[0], l[0], r[0], start, stop), (0, "p", max(64, r[2]) * (4 if l[3][2] == F32 else 1)))}, out, [l, r])
 
-    def wrap(bank, G, name, a, b):
+    def wrap(bank, G, name, a, b, start=True, stop=True):
         out = A(bank, 0, (b - a) // 16)
-        add("P", lambda: [g.tensor.matmul(out[0], T[G][:, 15 - p:143 - p], T[name][:, a + p:b:16], p == 0, p == 15) for p in range(16)][-1],
-            out, [A(G), A(name, a, b)], (0, "p", 16 * 64))
+        add({"P": (lambda: [g.tensor.matmul(out[0], T[G][:, 15 - p:143 - p], T[name][:, a + p:b:16], start and p == 0, stop and p == 15)
+                            for p in range(16)][-1], (0, "p", 16 * max(64, out[2])))}, out, [A(G), A(name, a, b)])
         return out
 
     def iota(out, pat, base, cm):
         kw = {} if out[3][2] == I32 else {"allow_small_or_imprecise_dtypes": True}
-        add("G", lambda: g.iota(out[0], pat, base, cm, **kw), out, [], (130, "c", 2 * out[2]))
+        add({"G": (lambda: g.iota(out[0], pat, base, cm, **kw), (130, "c", 2 * out[2]))}, out, [])
 
     def sel(out, i, pat, o, fill, base, cm):
-        add("G", lambda: g.affine_select(out[0], i[0], pat, o, fill, base, cm), out, [i], (170, "c", 2 * out[2]))
+        add({"G": (lambda: g.affine_select(out[0], i[0], pat, o, fill, base, cm), (170, "c", 2 * out[2]))}, out, [i])
 
     def dma(e, out, src, region, sem, lat, ins=()):
-        add(e, lambda: eng[e].dma_start(out, src), (None, region), list(ins), (60, "t", 0), sem=sem, lat=lat, tail=lat, aim=sem == "dY")
+        add({e: (lambda: eng[e].dma_start(out, src), (60, "t", 0))}, (None, region), list(ins), sem=sem, lat=lat, tail=lat, aim=1.0 * (sem == "dY"))
 
     def arrive(sem, count, regions, at):
-        ops.append(dict(e=None, W=regions, R=[], cost=(0, "t", 0), lat=0, tail=0, sem=sem, cnt=count, at=at))
+        ops.append(dict(alt={None: (None, (0, "t", 0))}, W=regions, R=[], lat=0, tail=0, sem=sem, cnt=count, at=at))
 
-    sent = [0]
+    sent, began = [0], []
 
     def send(dests, src, dst, sem, tail):
         plan = calls(topo, cores, q, dests)
@@ -173,26 +204,38 @@ def rank_program(g, core, T, topo):
                 tr.append(RemoteDMATransfer(dst_ids=[DstId(rid=rid, pnc=pid)], dma_engine_mask=mask, remote_sem=T.sem[sem], src=s[0], dst=dst(d, call)))
                 rd.append(s)
                 sent[0] += bin(mask).count("1")
-            add("G", lambda tr=tr: g.remote_dma_fused(tr, local_sem=T.sem.gone), None, rd, (0, "t", 500), tail=tail, aim=AIM[sem[:2]] / len(plan))
+            rows = 128 // bin(call[0][1]).count("1")
+            add({"G": (lambda tr=tr: g.remote_dma_fused(tr, local_sem=T.sem.gone), (0, "t", 400 if began else 2000))}, (None, ("call", len(ops), len(ops) + 1)), rd,
+                tail=tail, after=2 * (call is not plan[0]))
+            began.append(1)
+            add({"E": (None, (0, "w", rows * (18 + rd[0][2] * (4 if rd[0][3][2] == F32 else 2) / 16)))}, None, [(None, ("call", len(ops) - 1, len(ops)))],
+                tail=tail - 1200, aim=AIM[sem[:2]] / len(plan), due=DUE[sem[:2]][q] + 700 * plan.index(call), after=2 * (call is not plan[0]))
             tail -= 600
 
     def count(src, dests):
-        return sum(bin(m).count("1") for call in calls(topo, cores, src, dests) for d, m in call if d == q)
+        return sum(bin(x).count("1") for call in calls(topo, cores, src, dests) for d, x in call if d == q)
 
     low = lambda r: list(range(r))
-    first = lambda r: low(r)[1:] + low(r)[:1]
     up = lambda s: list(range(N - 1, s, -1))
+    first = lambda r: ([d for d in ORD1 if d < r], ALONE["a1"])
+    second = lambda r: (low(r), ALONE["a2"])
+    reply = lambda s: (up(s), ALONE["aR"])
+    back = lambda s: (up(s), ALONE["a3"])
+    blocks = lambda s, r: r - s + (s in LATE)
 
-    ms(A("RP"), 0)
+    def last(s):
+        return [sorted((d for d, x in call), reverse=True) for call in calls(topo, cores, s, back(s))]
+
+    ms(A("RP"), 0, tail=40000)
     for h in range(2):
-        dma("Y", T.RB[h::2, :], T.bm[:], ("RB", h, h + 1), "dB", 2500)
-    for o in (0, 2, 4):
-        dma("Y", T.RP[o::16, :], T.en[:], ("RP", o, o + 1), "dP", 2500)
-    for o in (8, 9, 10, 11):
-        dma("S", T.RP[o::16, :], T.sd[:], ("RP", o, o + 1), "dP", 2500)
-    dma("Y", T.CS[:], T.cs[:], ("CS", 0, NB), "dC", 5200, [(None, ("order", 0, 1))])
-    dma("Y", T.LS[:], T.ls[:], ("LS", 0, NB), "dL", 6500, [(None, ("order", 0, 1))])
-    for o in ops[1:6]:
+        dma("S", T.RB[h::2, :], T.bm[:], ("RB", h, h + 1), "dB", 2500)
+        ops[-1]["tail"] = 50000
+    for o in (0, 1, 2, 4, 5, 6):
+        dma("Y", T.RP[o::16, :], T.en[:] if o < 4 else T.sd[:], ("RP", o, o + 1), "dP", 2100)
+        ops[-1]["tail"] = 40000
+    dma("Y", T.CS[:, Z:], T.cs[:], ("CS", Z, Z + NB), "dC", 4600, [(None, ("order", 0, 1))])
+    dma("Y", T.LS[:, Z:], T.ls[:], ("LS", Z, Z + NB), "dL", 5900, [(None, ("order", 0, 1))])
+    for o in ops[1:9]:
         o["first"] = True
 
     col = {}
@@ -205,151 +248,146 @@ def rank_program(g, core, T, topo):
     EQ = lambda i: A("EQ", i)
     LT = lambda i: A("LT", i)
     iota(A("KI", 0), [[0, 1]], 0, 1)
-    iota(A("OM", 0, 128), [[0, 8], [1, 16]], 0, 0)
-    iota(A("OM", 128, NP), [[0, NP // 16 - 8], [1, 16]], 0, 0)
+    iota(A("OM"), [[0, 8], [1, 16]], 0, 0)
     ms(A("ONE"), 1.0)
-    for j, (m, name) in enumerate(((15, "o"), (1, "par"), (7, "o7"))):
-        ts(A("KI", 2 + 2 * j), A("KI", 0), m, None, OP.bitwise_and)
-        cp(c_(name), A("KI", 2 + 2 * j))
-    ts(c_("sB"), c_("par"), 64 - 1 / 32, 1 / 32, OP.mult, OP.add)
-    ts(c_("cB"), c_("par"), 15.5 / 32, -15.5 / 32, OP.mult, OP.add)
-    ts(A("D8", 0, 8), A("OM", 0, 8), c_("o7"), None, OP.is_lt)
-    ts(A("D8", 8, 16), A("D8", 0, 8), -15 / 16, 1.0, OP.mult, OP.add)
-    ts(A("D8", 16, 24), A("D8", 0, 8), 15.0, 1.0, OP.mult, OP.add)
-    for name, a in (("sP", 8), ("uP", 16)):
-        add("V", lambda name=name, a=a: g.vector.tensor_reduce(c_(name)[0], T.D8[:, a:a + 8], AxisListType.X, OP.mult),
-            c_(name), [A("D8", a, a + 8)], (0, "c", 64))
-    ts(c_("cP"), c_("sP"), 0.5, -0.5, OP.mult, OP.add)
+    ms(A("CS", 0, Z), 0)
+    ms(A("LS", 0, Z), 0.0)
+    for j, (x, name) in enumerate(((15, "o"), (1, "par"), (3, "o3"))):
+        ts(A("KI", 2 + 2 * j), A("KI", 0), x, None, OP.bitwise_and)
+        lin(c_(name), A("KI", 2 + 2 * j))
+    lin(c_("sB"), c_("par"), 64 - 1 / 32, 1 / 32)
+    lin(c_("cB"), c_("par"), 15.5 / 32, -15.5 / 32)
     ts(A("EQ"), A("OM", 0, 16), c_("o"), None, OP.is_equal)
-    ts(A("LT", 0, 16), A("OM", 0, 16), c_("o"), None, OP.is_gt)
-    ts(A("DIAG"), A("OM"), c_("o"), None, OP.is_equal)
-    act(c_("one"), LT(14), -1.0, 1.0)
-    act(c_("sg"), c_("par"), -2.0, 1.0)
-    act(c_("w"), c_("sg"), LT(5))
-    act(c_("w16"), c_("w"), 1 / 16)
-    act(c_("wx0"), EQ(14), -4096.0, c_("w"))
-    act(c_("wx"), EQ(15), 0.5, c_("wx0"))
-    ts(c_("v0"), EQ(8), EQ(10), EQ(11), OP.add, OP.subtract)
-    ts(c_("v1"), EQ(9), EQ(11), 1 / 16, OP.add, OP.mult)
-    act(c_("v15"), EQ(15), 8192.0)
-    act(c_("g2"), c_("par"), -2 - 1 / 1024, 2.0)
-    tt(A("RC", 0, 8), A("EQ", 0, 16, 2), A("EQ", 1, 16, 2), OP.add)
-    act(A("RC", 8, 16), A("RC", 0, 8), c_("g2"))
-    ts(c_("sg0"), c_("o"), c_("par"), 4096.0, OP.subtract, OP.mult)
-    ts(c_("seg"), c_("sg0"), M13 + BAND * q, None, OP.add)
-    act(c_("ya"), EQ(15), -2.0 ** 20)
-    act(c_("yb"), LT(15), 2.0 ** 20)
-    act(c_("nc"), LT(15), -C)
+    ts(A("LT"), A("OM", 0, 16), c_("o"), None, OP.is_gt)
+    ts(A("D8", 0, 3), A("OM", 0, 3), c_("o3"), 255.0, OP.is_lt, OP.mult)
+    lin(A("D8", 4, 7), A("D8", 0, 3), 1.0, 1.0)
+    add({"V": (lambda: g.vector.tensor_reduce(c_("u3")[0], T.D8[:, 4:7], AxisListType.X, OP.mult), (0, "c", 64))}, c_("u3"), [A("D8", 4, 7)])
+    lin(c_("f3"), LT(4), -2.0 ** -13, 2.0 ** -12)
+    lin(c_("sP"), c_("u3"), c_("f3"), 0.0)
+    lin(c_("cP0"), c_("sP"), 0.5, -0.5)
+    ts(c_("cP"), c_("cP0"), 0.0, None, OP.min)
+    lin(c_("y1"), EQ(1), 2.0, 0.0)
+    lin(c_("wy"), EQ(2), 1 / 128, c_("y1"))
+    ts(c_("w1"), EQ(8), EQ(9), -1 / 16, OP.add, OP.mult)
+    lin(c_("w2"), EQ(0), 512.0, c_("wy"))
+    lin(c_("w16"), c_("w1"), 1.0, c_("w2"))
+    lin(c_("v00"), EQ(5), 16.0, 0.0)
+    lin(c_("v0"), EQ(6), 1 / 16, c_("v00"))
+    lin(c_("v1"), EQ(4), 256.0, EQ(5))
+    lin(c_("v15"), EQ(15), 8192.0, 0.0)
+    lin(c_("g2"), c_("par"), -1 - 1 / 1024, 1.0)
+    ts(c_("seg"), c_("o"), c_("par"), 0.5, OP.subtract, OP.mult)
     sel(A("BL0"), A("ONE", 0, 128), [[16, 8], [0, 16]], OP.is_ge, 0.0, 15, -1)
     sel(A("BLK"), A("BL0"), [[-16, 8], [0, 16]], OP.is_ge, 0.0, 0, 1)
     ms(A("G1", 128, 144), 0.0)
     sel(A("G1", 0, 128), A("BLK"), [[0, 8], [1, 16]], OP.is_equal, 0.0, -15, 0)
     sel(A("ID"), A("ONE", 0, 128), [[-1, 128]], OP.is_equal, 0.0, 0, 1)
-    iota(A("K0"), [[16, 40]], 1, 0)
-    act(A("K1"), A("K0"), 1.0, c_("o"))
-    act(A("GW"), A("G1"), c_("w16"))
-    act(A("G2"), A("G1"), c_("g2"))
-    act(A("GC"), A("G1"), c_("nc"))
-    act(A("MX"), A("BLK"), c_("wx"))
-    act(A("MV0"), A("BLK"), c_("v0"))
-    act(A("MV1"), A("BLK"), c_("v1"))
-    act(A("HH"), A("OM", 0, 128), c_("ya"), c_("yb"))
-    tt(A("MY"), A("HH"), A("BLK"), OP.mult)
-    for s in range(8):
-        act(A("REP", 128 * s, 128 * s + 128), A("BLK"), A("RC", 8 + s))
-    ms(A("D0", 0, NP), BIG)
-    ms(A("D0", NP, NW), BIG)
+    lin(A("I32"), A("ID"))
+    for G, w in (("GY", "wy"), ("GW", "w16"), ("G2", "g2")):
+        lin(A(G), A("G1"), c_(w), 0.0, "V")
+    ts(A("GC"), A("G1"), LT(15), -C, OP.mult, OP.mult)
+    lin(A("MX"), A("BLK"), EQ(0), 0.0, "V")
+    lin(A("MV0"), A("BLK"), c_("v0"), 0.0, "V")
+    lin(A("MV1"), A("BLK"), c_("v1"), 0.0, "V")
+    ts(A("HH"), A("OM"), EQ(15), LT(15), OP.mult, OP.subtract)
+    lin(A("BN"), A("BLK"), -2.0 ** 20, 0.0, "V")
+    tt(A("MY"), A("HH"), A("BN"), OP.mult)
     if q:
-        act(A("MP"), A("BLK"), c_("w"))
-        act(A("NBL"), A("BLK"), -1.0)
-        act(c_("pc"), LT(15), C)
-        act(c_("dead"), LT(q), EMPTY)
-        act(A("MD"), A("BLK"), c_("dead"))
-        act(A("MB"), A("BLK"), c_("pc"))
+        ts(A("MP"), A("BLK"), c_("w16"), 16.0, OP.mult, OP.mult)
+        lin(A("NBL"), A("BLK"), -1.0, 0.0, "V")
+        ts(A("MD"), A("BLK"), LT(q), 2.0 ** 21, OP.mult, OP.mult)
+        ts(A("MB"), A("BLK"), LT(15), C, OP.mult, OP.mult)
         sel(A("MB"), A("MB"), [[0, 128]], OP.not_equal, -BAND / 2, -15, 1)
         sel(A("MB"), A("MB"), [[0, 128]], OP.not_equal, 0.5, -31, 1)
         sel(A("MB"), A("MB"), [[0, 8], [1, 16]], OP.not_equal, -8.5 * BAND, -16 * 47, 16)
         sel(A("MB"), A("MB"), [[0, 8], [1, 16]], OP.not_equal, -BAND * (63.5 + q), -16 * 63 - q, 16)
-        ts(c_("s1a"), EQ(0), M20 - M16, M16, OP.mult, OP.add)
-        ts(c_("s1"), EQ(q), M23 - M16, c_("s1a"), OP.mult, OP.add)
-        ts(c_("s2a"), c_("o"), float(BAND), c_("s1"), OP.mult, OP.add)
-        ts(c_("s2"), EQ(0), -2.0 ** 20, c_("s2a"), OP.mult, OP.add)
-        act(c_("i0a"), c_("o"), -float(LV), float(W2 + LV * (q - 1)))
-        act(c_("i0"), c_("i0a"), LT(q))
-        act(c_("i1a"), c_("o"), -LV / 2, LV * (N - 1.5))
-        act(c_("i1b"), c_("i1a"), c_("o"), float(NW + LV * (q - 1)))
-        act(c_("i1"), c_("i1b"), LT(q))
-        ms(A("WIN", NW, W2 + LV * q), EMPTY)
-        if nb:
-            for a in [NP + LV * q] + [OFF[s] + LV * (q - s) for s in range(q - 1)]:
-                ms(A("F", a, a + na), 0.0, 12000)
+        lin(c_("s1a"), EQ(0), M20 - M16, M16, "V")
+        lin(c_("s1"), EQ(q), M23 - M16, c_("s1a"), "V")
+        lin(c_("s2a"), c_("o"), float(BAND), c_("s1"), "V")
+        lin(c_("s2"), EQ(0), -2.0 ** 20, c_("s2a"), "V")
+        lin(c_("ia"), c_("o"), float(LV), float(W1))
+        lin(c_("i1"), c_("ia"), LT(q), 0.0)
+        lin(c_("i0"), LT(q), float(m), c_("i1"))
+        fill("WIN", W1, W0 + m, EMPTY)
+        ms(A("FA", 0, Z), 0.0)
+        iota(A("K0"), [[16, 16]], 0, 0)
+        for s in range(1, q):
+            fill("FB", m * s, m * s + LV * (s + 1), 0)
     if nb:
-        ms(A3("RA", 0, nb, 64, RW), 0)
+        lin(A("GK"), A("GC"), -1 / 16, 0.0, "V")
+        lin(A("GN"), A("G1"), -1 / 16, 0.0, "V")
+    ms(A("L2", 14, 16), 0.0)
 
-    ts(A("RB2"), A("RB"), c_("sB"), c_("cB"), OP.mult, OP.add)
+    lin(A("RB2"), A("RB"), c_("sB"), c_("cB"))
     ts(A("RB3"), A("RB2"), 2047, None, OP.bitwise_and)
-    ts(A("RP2"), A("RP"), c_("sP"), c_("cP"), OP.mult, OP.add)
-    ts(A("RP3"), A("RP2"), 255, None, OP.bitwise_and)
-    ts(A("P0"), A("RP3"), c_("uP"), c_("one"), OP.mult, OP.add)
-    cp(A("BH"), A("RB3"))
-    for s in range(8):
-        bank = "Q%d" % (6 + s % 2)
-        mm(A(bank, 0, 512), A("REP", 128 * s, 128 * s + 128), A("BH"), True, True)
-        act(A("TB", 512 * s, 512 * s + 512), A(bank, 0, 512), 1.0, 2.0)
-    xc = -(BAND // 16) * q - 7.5 / 16
+    for a in (0, NP // 2):
+        b = a + NP // 2
+        lin(A("RP2", a, b), A("RP", a, b), c_("sP"), c_("cP"))
+        ops[-1]["R"].append(("RP", 0, NP))
+        ts(A("RP3", a, b), A("RP2", a, b), 255, None, OP.bitwise_and)
+        lin(A("P0", a, b), A("RP3", a, b))
+    fill("TB", Z, Z + BK, 0)
+    ms(A("TB", 0, Z), -8192)
+    ms(A("TB", Z + BK, 2 * Z + BK), -8192)
+    for o in range(2):
+        dma("Y", T.TB[o::16, Z:Z + BK], T.RB3[o::2, :], ("TBd", o, o + 1), "dT", 2900, [A("RB3"), A("TB", Z, Z + BK)])
+        ops[-1].update(tail=TAIL["tb"], aim=AIM["tb"])
+    TBL = (T.TB[:, 0:BK + 2 * Z], ("TB", 0, BK + 2 * Z), BK + 2 * Z, SCRATCH["TB"])
 
     def seeds(out, M, pay, a, b, bank):
         mm(A(bank, 0, b - a), A(M), A(pay, a, b), True, True)
-        act(A(out, a, b), A(bank, 0, b - a), 1.0, c_("v15"))
+        lin(A(out, a, b), A(bank, 0, b - a), 1.0, c_("v15"))
 
-    def lookup(pay, a, b, at, bank, LN):
-        n = b - a
-        k, ka = n // 16, at // 16
-        x = wrap(bank, "GW", pay, a, b)
-        ts(A("LB", ka, ka + k), x, xc, 4095.0, OP.add, OP.min)
-        ts(A("XS", ka, ka + k), x, xc, -7.5 / 16, OP.add, OP.max)
-        ts(A("RR", ka, ka + k), A("XS", ka, ka + k), M0, M0, OP.add, OP.subtract)
-        tt(A("GM", at, at + n), IND(A("TB"), A("LB", ka, ka + k)), A("DIAG", 0, n), OP.mult)
-        tt(A("D0", at, at + n, 16), A("XS", ka, ka + k), A("RR", ka, ka + k), OP.subtract)
-        scan(A("SC", at, at + n), A("D0", at, at + n), A("GM", at, at + n), BIG, OP.min, OP.add)
-        ts(A(LN, ka, ka + k), A("SC", at + 15, at + n, 16), 0.5, -0.25, OP.mult, OP.add)
+    def bins(xs, at, gh, ga, bank, cuts):
+        k = xs[2]
+        for a, b in zip(cuts, cuts[1:]):
+            lin(A(gh, ga + 16 * a, ga + 16 * b), IND(TBL, A("LB", at + a, at + b)))
+            ops[-1]["R"].append(("TBd", 0, 2))
+        tt(A("XN", at, at + k), xs, A("LB", at, at + k), OP.subtract)
+        mm(A(bank, 0, k), A("I32"), A("XN", at, at + k), True, False)
+        x = wrap(bank, "G2", gh, ga, ga + 16 * k, False, True)
+        lin(A("LN", at, at + k), x, 1.0, 2 * Z + 1 - HALF - BK * q)
 
-    def spread(pay, LN):
-        k = NP // 16
-        x = wrap("Q5", "GW", pay, 0, NP)
-        mm(A("Q4", 0, NP), A("MX"), A(pay, 0, NP), True, True)
-        ts(A("MS"), A("Q4", 0, NP), M13, c_("seg"), OP.add, OP.is_equal)
-        ts(A("B32"), x, xc, None, OP.add)
-        ts(A("B33"), A("B32"), 511, None, OP.bitwise_and)
-        cp(A("LB", 0, k), A("B33"))
-        tt(A("FR"), x, A("B32"), OP.subtract)
-        tt(A("GH"), IND(A("RB3"), A("LB", 0, k)), A("MS"), OP.mult)
-        tt(A("TT"), wrap("Q5", "G2", "GH", 0, NP), A("FR"), OP.add)
-        ts(A(LN, 0, k), A("TT"), 0.5, 0.75 + xc / 2, OP.mult, OP.add)
+    def lookup(pay, a, b, at, bx, bl, cuts):
+        k = (b - a) // 16
+        x = wrap(bx, "GW", pay, a, b)
+        if not q:
+            relu(A("XS", at, at + k), x)
+            x = A("XS", at, at + k)
+        if a < NP:
+            lin(A("LB", at, at + k), x, 1.0, Z - HALF - BK * q)
+        else:
+            ts(A("LB", at, at + k), x, Z - HALF - BK * q, float(Z + BK), OP.add, OP.min)
+        bins(x, at, "GH", a, bl, cuts)
 
-    def event(t, old, new, V, parts, lst, init, wend):
-        p = 1 + 2 * t
-        for a, b, bY, bX, bB in parts:
-            B = A(bB, 0, b - a)
-            mm(B, A("ID"), A(old, a, b), True, False)
-            ln = A("LN%d" % t, a // 16, b // 16)
-            Y, X = A(bY, 0, b - a), A(bX, 0, b - a)
-            act(A("LG", a, b), IND(A("LS"), ln))
-            tt(A("BITS", a, b), IND(A("CS"), ln), A(V, a, b), OP.is_le)
+    def react(a, b, ln, V, Y):
+        lin(A("LG", a, b), IND(A("LS"), ln), on="S")
+        tt(A("BITS", a, b), IND(A("CS"), ln), A(V, a, b), OP.is_le)
+        mm(Y, A("ID"), A("LG", a, b), True, False)
+        mm(Y, A("MY"), A("BITS", a, b), False, True)
+        ts(A("PR", a, b), Y, 0.0, C, OP.max, OP.min)
+
+    own = [(0, NP // 2, "Q0", "Q1"), (NP // 2, NP, "Q2", "Q3")]
+
+    def event(t, old, new, V, at, wend):
+        p = 8 + t
+        lst = "LS%d" % t
+        for a, b, bY, bX in own:
+            Y, X, B = A(bY, 0, b - a), A(bX, 0, b - a), A("Q4", 0, b - a)
             if q:
                 mm(X, A("MP"), A(old, a, b), True, False)
-                if t and a < NP:
+                if t:
                     mm(X, A("MD"), A("MK", a, b), False, False)
-            mm(Y, A("ID"), A("LG", a, b), True, False)
-            mm(Y, A("MY"), A("BITS", a, b), False, True)
-            ts(A("PR", a, b), Y, 0.0, C, OP.max, OP.min)
+            react(a, b, A("LN", at + a // 16, at + b // 16), V, Y)
             if q:
                 mm(X, A("MB"), A("BITS", a, b), False, False)
                 mm(X, A("NBL"), A("PR", a, b), False, True)
+            mm(B, A("ID"), A(old, a, b), True, False)
             mm(B, A("GC", 15 - p, 143 - p), A("BITS", a, b), False, False)
             mm(B, A("G1", 15 - p, 143 - p), A("PR", a, b), False, True)
-            act(A(new, a, b), B)
-        for a, b, bY, bX, bB in parts if q else ():
+            lin(A(new, a, b), B, on="S")
+        init = c_("i%d" % t) if q else None
+        for a, b, bY, bX in own if q else ():
             ka, kb = a // 16, b // 16
             D, X = A(bY, 0, b - a), A(bX, 0, b - a)
             ts(D, X, c_("s1"), c_("s2"), OP.add, OP.is_equal)
@@ -357,164 +395,301 @@ def rank_program(g, core, T, topo):
             init = A("SS", b - 1)
             tt(A("DD", a, b), A("SS", a, b), D, OP.mult)
             if t == 0:
-                act(A("MK", a, b), D)
+                lin(A("MK", a, b), D, on="S")
             x = wrap(bX, "G1", "DD", a, b)
-            ts(A(lst, ka, kb), x, -1.0, None, OP.add)
-            cp(IND(A("WIN", 0, wend), A(lst, ka, kb)), A(new, a, b))
-            tt(A("M%d" % t, ka, kb), x, A("K1", ka, kb), OP.max)
-
-    own = [(0, NP // 2, "Q0", "Q1", "Q4"), (NP // 2, NP, "Q2", "Q3", "Q5")]
+            lin(A(lst, ka, kb), x, 1.0, -1.0)
+            lin(IND(A("WIN", 0, wend), A(lst, ka, kb)), A(new, a, b), on="V")
+            if t == 0:
+                lin(A("M0", ka, kb), x)
+            else:
+                tt(A("M1", ka, kb), x, A("M0", ka, kb), OP.max)
 
     k = NP // 16
+    O0, O1, O2, A1, A2, H3 = 0, 24, 48, 72, 88, 104
+
     seeds("V0", "MV0", "P0", 0, NP, "Q0")
     seeds("V1", "MV1", "P0", 0, NP, "Q2")
-    spread("P0", "LN0")
-    event(0, "P0", "PA", "V0", own, "LS0", c_("i0") if q else None, W2 + LV * q)
-    cp(A("T0"), IND(A("CS"), A("LN0", 0, k)))
-    send(first(q), lambda d, c: A("WIN", W2 + LV * (q - d - 1), W2 + LV * (q - d)),
+    y = wrap("Q6", "GY", "P0", 0, NP)
+    lin(A("LB", O0, O0 + k), y, 1.0, -HALF)
+    mm(A("Q4", 0, NP), A("MX"), A("P0"), True, True)
+    ts(A("MS"), A("Q4", 0, NP), -8.0 * q, c_("seg"), OP.add, OP.is_equal)
+    tt(A("GH", 0, NP), IND(A("RB3"), A("LB", O0, O0 + k)), A("MS"), OP.mult)
+    tt(A("XN", O0, O0 + k), y, A("LB", O0, O0 + k), OP.subtract)
+    mm(A("Q7", 0, k), A("I32"), A("XN", O0, O0 + k), True, False)
+    x = wrap("Q7", "G2", "GH", 0, NP, False, True)
+    lin(A("LN", O0, O0 + k), x, 1.0, Z + 1 - HALF)
+    event(0, "P0", "PA", "V0", O0, W0 + m)
+    lin(A("T0"), IND(A("CS"), A("LN", O0, O0 + k)))
+    send(first(q), lambda d, c: A("WIN", W0 + LV * d, W0 + LV * (d + 1)),
          lambda d, c: T.PA[:, NP + LV * (q - d - 1):NP + LV * (q - d)], "a1", TAIL["s1"])
 
+    lookup("PA", 0, NP, O1, "Q6", "Q7", [0, k // 2, k])
+    event(1, "PA", "PB", "V1", O1, W0)
     if q:
-        spread("PA", "LN1")
-    else:
-        lookup("PA", 0, NP, 0, "Q5", "LN1")
-    event(1, "PA", "PB", "V1", own, "LS1", c_("i1") if q else None, W2)
-    if q:
-        cp(A("F1", 0, NP), IND(A("CS"), A("LN1", 0, k)))
-    else:
-        tt(A("T1"), IND(A("CS"), A("LN1", 0, k)), A("T0"), OP.add)
-    e, ke = NP + na, (NP + na) // 16
+        relu(A("L2", 0, 2 * q), wrap("Q1", "GW", "WIN", W1, W0))
+    e, ka = NP + na, 2 * nb
     if nb:
         arrive("a1", sum(count(r, first(r)) for r in up(q)), [("PA", NP, e)], ARR["a1"][q])
-        lookup("PA", NP, e, NP, "Q7", "LN1")
-        seeds("V1", "MV1", "PA", NP, e, "Q6")
-        event(1, "PA", "PB", "V1", [(NP, e, "Q6", "Q7", "Q4")], "LS1", A("SS", NP - 1), W2)
-        cp(A("SG", 0, na), IND(A("CS"), A("LN1", k, ke)))
-        cp(A3("RA", 0, nb, 0, LV), A("SG", 0, na))
-        ts(A3("RA", 0, nb, 64, 66), A("M1" if q else "K1", k, ke), -1.0, None, OP.add)
-    send(low(q), lambda d, c: A("WIN", OFF[d] + LV * (q - d - 1), OFF[d] + LV * (q - d)),
-         lambda d, c: T.L2[:, LV * (q - d - 1):LV * (q - d)], "a2", TAIL["s2"])
+        seeds("V1", "MV1", "PA", NP, e, "Q5")
+        lookup("PA", NP, e, A1, "Q6", "Q7", [0, ka])
+        react(NP, e, A("LN", A1, A1 + ka), "V1", A("Q5", 0, na))
+        if q:
+            lin(A("XS", A1, A1 + ka), A("Q6", 0, ka))
+        mm(A("Q6", 0, ka), A("I32"), A("XS", A1, A1 + ka), True, False)
+        wrap("Q6", "GK", "BITS", NP, e, False, False)
+        x = wrap("Q6", "GN", "PR", NP, e, False, True)
+        ts(A("L2", 2 * q, 14), x, 0.0, BK * (q + 1) - 1 / 16, OP.max, OP.min)
+    send(second(q), lambda d, c: A("L2", 0, 16), lambda d, c: T.L2[:, 16 * (q - d):16 * (q - d + 1)], "a2", TAIL["s2"])
 
-    lookup("PB", 0, NP, 0, "Q5", "LN2")
-    if q:
-        cp(A("F", 0, NP), IND(A("CS"), A("LN2", 0, k)))
-    else:
-        tt(A("YO"), IND(A("CS"), A("LN2", 0, k)), A("T1"), OP.add)
+    gate = ops[-1 if nb == 0 else max(i for i, o in enumerate(ops) if o["W"] and o["W"][0][0] == "L2")]
+    x = len(ops)
+    tt(A("T1"), IND(A("CS"), A("LN", O1, O1 + k)), A("T0"), OP.add)
+    lookup("PB", 0, NP, O2, "Q0", "Q2", [0, k])
+    tt(A("T2" if q else "YO"), IND(A("CS"), A("LN", O2, O2 + k)), A("T1"), OP.add)
+    if not q:
         dma("Y", T.y[:], T.YO[:], ("y", 0, 1), "dY", 2500, [A("YO")])
+        ops[-1]["due"] = DUE["a3"][0]
+    else:
+        for o in ops[x:]:
+            o["behind"] = gate
     if nb:
-        lookup("PB", NP, e, NP, "Q4", "LN2")
-        cp(A("SG", NA, NA + na), IND(A("CS"), A("LN2", k, ke)))
-        cp(A3("RA", 0, nb, LV, 2 * LV), A("SG", NA, NA + na))
-        send(up(q), lambda d, c: A3("RA", d - q - 1, d - q, 0, RW), lambda d, c: T.LA[:, d - q - 1:d - q, :], "aR", TAIL["sR"])
-        arrive("a2", sum(count(r, low(r)) for r in up(q)), [("L2", 0, na)], ARR["a2"])
-        lookup("L2", 0, na, NP, "Q6", "LN3")
-        cp(A("S3", 0, na), IND(A("CS"), A("LN3", k, ke)))
-        wide = lambda c: LV * (max(d for d, m in c) - q)
-        send(up(q), lambda d, c: A("S3", 0, wide(c)), lambda d, c: T.L3[:, q, 0:wide(c)], "a3%d" % q, TAIL["s3"])
+        xs = A("L2", 2 * q, 14)
+        lin(A("SG", 0, na), IND(A("CS"), A("LN", A1, A1 + ka)))
+        if q not in LATE:
+            lin(A("LB", A2, A2 + ka), xs, 1.0, Z - HALF - BK * q)
+            bins(xs, A2, "GH", NP, "Q7", [0, ka // 4 * 2, ka] if ka > 8 else [0, ka])
+        if q:
+            tt(A("A12", 0, na), IND(A("CS"), A("LN", A2, A2 + ka)), A("SG", 0, na), OP.add)
+            lin(A3("RA", 0, nb, 0, LV), A("A12", 0, na))
+            lin(A3("RA", 0, nb, LV, RW), xs, 1 / BK, 2.0 ** -17 - 0.5)
+        else:
+            lin(A3("RA", 0, nb, 0, LV), A("SG", 0, na))
+            ms(A3("RA", 0, nb, LV, RW), 0)
+        send(reply(q), lambda d, c: A3("RA", d - q - 1, d - q, 0, RW), lambda d, c: T.LA[:, q:q + 1, :], "aR", TAIL["sR"] + (0 if q else 6000))
+        if not q and not LATE:
+            lin(A("S2"), IND(A("CS"), A("LN", A2, A2 + ka)))
+            send(reply(q), lambda d, c: A("S2", LV * (d - 1), LV * d), lambda d, c: T.L0[:], "aS", TAIL["sR"] + 2000)
+        end, at = {}, 0
+        for call in last(q):
+            for r in call:
+                if blocks(q, r) > 1:
+                    iota(A("PLC", at, at + 2 * blocks(q, r) - 2), [[16, blocks(q, r) - 1], [1, 2]], 2 * (r - 1), 0)
+                at += 2 * blocks(q, r)
+                iota(A("PLC", at - 2, at), [[1, 2]], 16 * (blocks(q, r) - 1) + 2 * q, 0)
+                end[r] = at
+        kp = -(-at // 16)
+        if at % 16:
+            ms(A("PLC", at, 16 * kp), 0.0)
+        lin(A("PL", 0, kp), wrap("Q5", "G1", "PLC", 0, 16 * kp), 1 / 16, 0.0)
+        ops[-1]["early"] = ops[-2]["early"] = True
+        arrive("a2", sum(count(r, second(r)) for r in up(q)), [("L2", 16, 16 * (nb + 1))], ARR["a2"][q])
+        xl = IND(A("L2", 0 if q in LATE else 16, 16 * (nb + 1)), A("PL", 0, kp))
+        ts(A("LB", H3, H3 + 16 * kp), xl, Z - HALF - BK * q, float(Z + BK), OP.add, OP.min)
+        lin(A("XS", H3, H3 + 16 * kp), xl, on="S")
+        cut = min((end[c[-1]] for c in last(q)), key=lambda x: abs(x - SPLIT * at)) if at > 24 else at
+        for a, b, bank in ((0, cut, "Q5"), (cut, at, "Q6")):
+            if b > a:
+                bins(A("XS", H3 + a, H3 + b), H3 + a, "G3H", 16 * a, bank, [0, (b - a) // 4 * 2, b - a] if b - a > 8 else [0, b - a])
+        for call in calls(topo, cores, q, back(q)):
+            c = sorted((d for d, x in call), reverse=True)
+            a, b = end[c[0]] - 2 * blocks(q, c[0]), end[c[-1]]
+            cuts = [a, (a + b) // 4 * 2, b] if b - a > 8 else [a, b]
+            for a, b in zip(cuts, cuts[1:]):
+                lin(A("S3", 16 * a, 16 * b), IND(A("CS"), A("LN", H3 + a, H3 + b)))
+        wide = lambda c: LV * blocks(q, max(d for d, x in c))
+        send(back(q), lambda d, c: A("S3", 16 * end[d] - wide(c), 16 * end[d]), lambda d, c: T.L3[:, q, W3 - wide(c):W3], "a3%d" % q, TAIL["s3"])
 
     if q:
-        m = LV * q
-        tt(A("M2"), A("M1", 0, k), A("M0"), OP.max)
-        ts(A("LF"), A("M2"), -1.0, None, OP.add)
-        ts(A("M3"), A("M0"), float(NP - W2), None, OP.add)
-        tt(A("M4"), A("M3"), A("K1", 0, k), OP.max)
-        ts(A("LF1"), A("M4"), -1.0, None, OP.add)
-        arrive("aR", sum(count(s, up(s)) for s in low(q)), [("LA", 0, q)], ARR["aR"])
-        cp(A("F1", NP, NP + m), A3("LA", 0, q, 0, LV))
-        cp(A("F", NP, NP + m), A3("LA", 0, q, LV, 2 * LV))
-        cp(A("LL", 0, 2 * q), A3("LA", 0, q, 64, 66))
-        tt(A("T1"), IND(A("F1", 0, NP + m), A("LF1")), A("T0"), OP.add)
+        lin(A("LF"), A("M1"), 1.0, Z - 1.0 - NP)
+        arrive("aR", sum(count(s, reply(s)) for s in low(q)), [("LA", 0, q)], ARR["aR"])
+        if not LATE:
+            arrive("aS", count(0, reply(0)), [("L0", 0, LV)], ARR["aR"])
+            lin(A("FB", 0, LV), A("L0"))
+        lin(A("AF", 0, m), A3("LA", 0, q, 0, LV))
+        lin(A("LL1", 0, 2 * q), A3("LA", 0, q, LV, RW), float(m), c_("o"))
+        tt(A("LL2", 0, 2 * q), A("LL1", 0, 2 * q), A("K0", 0, 2 * q), OP.add)
+        lin(A("LL", 0, 2 * q), A("LL2", 0, 2 * q))
         for s in low(q):
-            arrive("a3%d" % s, count(s, up(s)), [("L3", s, s + 1)], ARR["a3"] - 100 * s)
-            cp(A("F", OFF[s], OFF[s] + LV * (q - s)), A3("L3", s, s + 1, 0, LV * (q - s)))
-        cp(A("F", W2, W2 + m), IND(A("F", 0, W2), A("LL", 0, 2 * q)))
+            c = max(c for c in last(s) if q in c)
+            arrive("a3%d" % s, count(s, back(s)), [("L3", s, s + 1)], ARR["a3"][s] + 500 * last(s).index(c))
+            if blocks(s, q) > 1:
+                lin(A("FB", m * (s + 1) - LV * (blocks(s, q) - 1), m * (s + 1)), A3("L3", s, s + 1, W3 - LV * blocks(s, q), W3 - LV))
+        runs = []
+        for s in low(q):
+            if runs and topo.chip(cores[s]) == topo.chip(cores[s - 1]):
+                runs[-1][1] = s + 1
+            else:
+                runs.append([s, s + 1])
+        for a, b in runs:
+            lin(A("FA", Z + LV * a, Z + LV * b), A3("L3", a, b, W3 - LV, W3))
+        tt(A("FA", Z + m, Z + 2 * m), IND(A("FB", 0, m * q), A("LL", 0, 2 * q)), A("AF", 0, m), OP.add)
         for h, x in enumerate("YS"):
             a, b = h * NP // 2, (h + 1) * NP // 2
-            tt(A("YO", a, b), IND(A("F", 0, W2 + m), A("LF", a // 16, b // 16)), A("T1", a, b), OP.add)
+            tt(A("YO", a, b), IND(A("FA", 0, Z + 2 * m), A("LF", a // 16, b // 16)), A("T2", a, b), OP.add)
             dma(x, T.y[:, a:b], T.YO[:, a:b], ("y", h, h + 1), "dY", 2500, [A("YO", a, b)])
 
+    early = [i for i, o in enumerate(ops) if o.get("early")]
+    if early:
+        at = next(i for i, o in enumerate(ops) if o["sem"] == "a1")
+        moved = [i for i, o in enumerate(ops) if i > at and (o.get("early") or any(r[0] == "PLC" for r in o["W"]))]
+        ops[:] = ops[:at] + [ops[i] for i in moved] + [o for i, o in enumerate(ops) if i >= at and i not in moved]
     hit = lambda x, y: x[1] < y[2] and y[1] < x[2]
     acc = {}
     for i, o in enumerate(ops):
         dep = {}
         for r in o["R"]:
             for j, x, w in acc.get(r[0], ()):
-                if hit(r, x) and (w or (r[0][0] == "Q" and ops[j]["e"] != o["e"])):
-                    dep[j] = True
+                if hit(r, x) and w:
+                    dep[j] = "data"
+                elif hit(r, x) and r[0][0] == "Q":
+                    dep.setdefault(j, "bank")
         for r in o["W"]:
             for j, x, w in acc.get(r[0], ()):
-                if hit(r, x) and o["e"] is not None:
-                    dep[j] = True
+                if hit(r, x) and None not in o["alt"]:
+                    dep[j] = "data"
         if o["R"] and o["R"][0][0] == "order":
-            dep = {j: None for j in range(i) if ops[j].get("first") or ops[j]["sem"] == "dC"}
+            dep = {j: "order" for j in range(i) if ops[j].get("first") or ops[j]["sem"] == "dC"}
+        if o.get("after"):
+            dep[i - 2] = "order"
+        if "behind" in o:
+            dep.setdefault(next(j for j in range(i) if ops[j] is o["behind"]), "order")
         o["dep"] = dep
         for r in o["R"]:
             acc.setdefault(r[0], []).append((i, r, False))
         for r in o["W"]:
             acc.setdefault(r[0], []).append((i, r, True))
+    n = len(ops)
+    spans = [[{e: c[0] + p[c[1]] * c[2] for e, (f, c) in o["alt"].items()} for o in ops] for p in PACE]
+    full = [list(o["dep"].items()) for o in ops]
+    above, deps = [], []
+    for i in range(n):
+        far = set().union(*[above[j] for j, kind in full[i]])
+        deps.append([(j, kind) for j, kind in full[i] if j not in far or ops[j]["sem"]])
+        above.append(far | {j for j, kind in full[i]})
 
-    def free(j, o):
-        return o["dep"][j] is None or ops[j]["e"] == o["e"] == "P"
+    def free(j, kind, ej, e):
+        return kind == "order" or (ej == e and (e == "P" or kind == "bank"))
 
-    def span(o, m):
-        return o["cost"][0] + m[o["cost"][1]] * o["cost"][2]
+    def gap(j, kind, ej, e, p):
+        return 0 if free(j, kind, ej, e) else (ops[j]["lat"] * p["t"] if ops[j]["sem"] else p["y"])
 
-    def gap(j, o, m):
-        return 0 if free(j, o) else (ops[j]["lat"] * m["t"] if ops[j]["sem"] else m["y"])
-
-    def place(noise):
-        m = PACE[0]
+    def place(noise, lean):
+        p, sp = PACE[0], spans[0]
         tail = [o["tail"] for o in ops]
-        for i in range(len(ops) - 1, -1, -1):
-            o = ops[i]
-            tail[i] += span(o, m) + noise[i]
-            for j in o["dep"]:
-                tail[j] = max(tail[j], tail[i] + gap(j, o, m))
-        at, busy = [0] * len(ops), {x: [] for x in eng}
-        for i in sorted(range(len(ops)), key=lambda i: (-tail[i], i)):
-            o = ops[i]
-            d = span(o, m)
-            t = max([o["at"]] + [at[j] + span(ops[j], m) + gap(j, o, m) for j in o["dep"]])
-            if o["e"]:
-                row = busy[o["e"]]
-                n = len(row)
-                for x, (a, b, j) in enumerate(row):
-                    if t + d <= a:
-                        n = x
-                        break
-                    t = max(t, b)
-                row.insert(n, (t, t + d, i))
-            at[i] = t
-        return at, busy
+        for i in range(n - 1, -1, -1):
+            tail[i] += min(sp[i].values()) + noise[i]
+            for j, kind in deps[i]:
+                tail[j] = max(tail[j], tail[i] + gap(j, kind, 0, 1, p))
+        at, on, busy = [0] * n, [None] * n, {x: [] for x in list(eng) + ["E"]}
+        for i in sorted(range(n), key=lambda i: (-tail[i], i)):
+            best = None
+            for e, d in sp[i].items():
+                t = max([ops[i]["at"]] + [at[j] + sp[j][on[j]] + gap(j, kind, on[j], e, p) for j, kind in deps[i]])
+                z = 0
+                if e:
+                    row = busy[e]
+                    z = len(row)
+                    for x, (a, b, j) in enumerate(row):
+                        if t + d * 1.15 + 30 <= a:
+                            z = x
+                            break
+                        t = max(t, b)
+                v = t + 2 * d + (lean[i] if e == "V" else 0)
+                if best is None or v < best[0]:
+                    best = (v, e, t, d, z)
+            v, e, t, d, z = best
+            if e:
+                busy[e].insert(z, (t, t + d, i))
+            at[i], on[i] = t, e
+        return at, on, busy
 
-    def worth(at):
-        v = 0
-        order = sorted(range(len(ops)), key=lambda i: (at[i], i))
-        for m in PACE:
-            end, last = [0] * len(ops), {}
+    aims = [(i, o["aim"], o.get("due", 0)) for i, o in enumerate(ops) if o.get("aim")]
+    fixed = [next(iter(o["alt"])) if len(o["alt"]) == 1 else 0 for o in ops]
+    edges = [[[(j, gap(j, kind, fixed[j], fixed[i] if kind == "data" else 1, p), kind == "bank") for j, kind in deps[i]] for i in range(n)] for p in PACE]
+    succ = [[] for i in range(n)]
+    for i in range(n):
+        for j, kind in deps[i]:
+            succ[j].append(i)
+
+    def worth(order, on):
+        v, why = 0, []
+        for p, sp, ed in zip(PACE, spans, edges):
+            end, prev, cause = [0] * n, {}, [-1] * n
             for i in order:
-                o = ops[i]
-                t = max([o["at"] * m["a"], last.get(o["e"], 0)] + [end[j] + gap(j, o, m) for j in o["dep"]])
-                end[i] = t + span(o, m)
-                if o["e"]:
-                    last[o["e"]] = end[i]
-                v += o.get("aim", 0) * end[i] / m["t"]
-        return v
+                e = on[i]
+                c = prev.get(e, -1)
+                t = end[c] if c >= 0 else ops[i]["at"] * p["a"] if e is None else 0
+                for j, d, bank in ed[i]:
+                    x = end[j] if bank and on[j] == e else end[j] + d
+                    if x >= t:
+                        t, c = x, j
+                end[i], cause[i] = t + sp[i][e], c
+                if e:
+                    prev[e] = i
+            v += sum(a * (0.15 * end[i] + max(0, end[i] - due * p["a"])) for i, a, due in aims) / p["a"]
+            why.append(cause)
+        return v, why
 
-    rng = np.random.default_rng(q + SEED)
-    noise = KEPT.get(q, [0.0] * len(ops))
-    at, busy = place(noise)
-    best = worth(at)
-    for it in range(0 if q in KEPT else TRIES):
-        new = [max(0.0, x + float(r)) if u < (0.02, 0.1)[it % 2] else x
-               for x, r, u in zip(noise, rng.normal(0, (1500, 400)[it % 2], len(ops)), rng.random(len(ops)))]
-        a2, b2 = place(new)
-        v = worth(a2)
-        if v < best:
-            best, noise, at, busy = v, new, a2, b2
-    KEPT[q] = noise
-    for i, o in enumerate(ops):
-        o["at"] = at[i]
+    def improve(order, on):
+        rng = np.random.default_rng(q)
+        best, why = worth(order, on)
+        kept = (best, order, on)
+        share = np.array([a for i, a, due in aims])
+        for it in range(TRIES):
+            cause = why[int(rng.integers(len(PACE)))]
+            i, pairs = aims[int(rng.choice(len(aims), p=share / share.sum()))][0], []
+            while cause[i] >= 0:
+                j = cause[i]
+                if on[j] == on[i] and i not in succ[j]:
+                    pairs.append((j, i))
+                i = j
+            if not pairs:
+                continue
+            j, i = pairs[int(rng.integers(len(pairs)))]
+            move, new, no = int(rng.integers(4)), list(order), on
+            pos = {x: k for k, x in enumerate(order)}
+            if move < 2:
+                x = (j, i)[move]
+                alt = [e for e in ops[x]["alt"] if e != on[x]]
+                if not alt:
+                    continue
+                no = list(on)
+                no[x] = alt[int(rng.integers(len(alt)))]
+            elif move == 2:
+                go = {j}
+                for x in order[pos[j]:pos[i]]:
+                    if x in go:
+                        go.update(succ[x])
+                if i in go:
+                    continue
+                far = min(n, pos[i] + 1 + int(rng.integers(6)) * int(rng.integers(2)))
+                part = order[pos[j]:far]
+                for x in part:
+                    if x in go:
+                        go.update(succ[x])
+                new[pos[j]:far] = [x for x in part if x not in go] + [x for x in part if x in go]
+            else:
+                go = {i}
+                for x in order[pos[i]:pos[j]:-1]:
+                    if x in go:
+                        go.update(y for y, kind in deps[x])
+                if j in go:
+                    continue
+                part = order[pos[j]:pos[i] + 1]
+                new[pos[j]:pos[i] + 1] = [x for x in part if x in go] + [x for x in part if x not in go]
+            v, w = worth(new, no)
+            if v <= best + HEAT * (1 - it / TRIES) ** 2 * rng.random():
+                best, why, order, on = v, w, new, no
+                if v < kept[0]:
+                    kept = (v, new, no)
+        return kept[1:]
+
+    if q not in KEPT:
+        at, on, busy = place([0.0] * n, [100.0] * n)
+        KEPT[q] = improve(sorted(range(n), key=lambda i: (at[i], i)), on)
+    order, on = KEPT[q]
+    at = {i: k for k, i in enumerate(order)}
+    busy = {x: [(0, 0, i) for i in order if on[i] == x] for x in eng}
 
     total = {}
     for o in ops:
@@ -526,22 +701,22 @@ def rank_program(g, core, T, topo):
         for a, b, i in busy[x]:
             o = ops[i]
             o["waits"] = []
-            for j in sorted(o["dep"], key=lambda j: -ops[j]["at"]):
+            for j, kind in sorted(full[i], key=lambda d: -at[d[0]]):
                 p = ops[j]
-                if free(j, o):
+                if free(j, kind, on[j], x):
                     continue
-                key = p["sem"] or p["e"]
-                if seen.get(key, -1) < (0 if p["sem"] else p["at"]):
-                    seen[key] = 0 if p["sem"] else p["at"]
+                key = p["sem"] or on[j]
+                if seen.get(key, -1) < (0 if p["sem"] else at[j]):
+                    seen[key] = 0 if p["sem"] else at[j]
                     o["waits"].append(j)
                     need.add(j)
     num = {}
     for x in csem:
-        n = 0
+        c = 0
         for a, b, i in busy[x]:
             if i in need and not ops[i]["sem"]:
-                n += 1
-                num[i] = n
+                c += 1
+                num[i] = c
     for x in eng:
         for a, b, i in busy[x]:
             o = ops[i]
@@ -550,8 +725,8 @@ def rank_program(g, core, T, topo):
                 if p["sem"]:
                     eng[x].wait_ge(T.sem[p["sem"]], total[p["sem"]])
                 else:
-                    eng[x].wait_ge(T.sem[csem[p["e"]]], num[j])
-            ins = o["fn"]()
+                    eng[x].wait_ge(T.sem[csem[on[j]]], num[j])
+            ins = o["alt"][x][0]()
             if o["sem"]:
                 ins.then_inc(T.sem[o["sem"]], 16)
             elif i in num:

@@ -6,63 +6,68 @@ N, NP, LV, NB, BAND = 8, 384, 32, 2048, 65536
 BK = BAND // 16
 NA = LV * (N - 1)
 NW = NP + NA
-W3 = LV * N
+W3 = NA + LV
 N3 = LV * (N + 2) * (N - 1) // 2
 Z = 8
+R3, RV = Z + 512, Z + 512 + NP
 RW = 34
-EMPTY = 64.0
+EMPTY = -64.0
 M16, M20, M23 = (1.5 * 2.0 ** (23 + k) for k in (16, 20, 23))
 HALF = 7.5 / 16
 
 F32, BF, I32, F16, U16 = "float32", "bfloat16", "int32", "float16", "uint16"
 SB = {
-    "CS": (Z + NB, I32), "LS": (Z + NB, BF), "RB": (512, I32), "RB2": (512, I32), "RB3": (512, I32), "TB": (BK + 2 * Z, I32),
-    "XN": (184, F32), "RP": (NP, I32), "RP2": (NP, I32), "RP3": (NP, I32), "P0": (NP, BF), "PA": (NW, BF), "PB": (NP, BF),
-    "V0": (NP, F32), "V1": (NW, F32), "BITS": (NW, BF), "LG": (NW, BF), "PR": (NW, BF), "SS": (NP, F32), "DD": (NP, F16),
+    "CS": (Z + NB, I32), "LS": (Z + NB, BF), "RB2": (512, I32), "RB3": (512, I32), "TB": (BK + 2 * Z, I32),
+    "XN": (184, BF), "CQ": (24, BF), "RP": (NP, I32), "RP2": (NP, I32), "P0": (NP, BF), "PA": (NW, BF), "PB": (NP, BF),
+    "V1": (NW, F32), "BITS": (NW, BF), "LG": (NW, BF), "PR": (NW, BF), "SS": (NP, F32), "DD": (NP, F16),
     "MK": (NP, BF), "MS": (NP, BF), "GH": (NW, F16), "G3H": (N3, F16), "ONE": (256, BF),
     "LB": (184, U16), "LN": (184, U16), "XS": (184, F32), "L2": (16 * N, F32),
     "LS0": (24, U16), "LS1": (24, U16), "LL": (16, U16), "LF": (24, U16), "PL": (6, U16), "PLC": (80, BF),
-    "M0": (24, F32), "M1": (24, F32), "K0": (16, F32), "LL1": (16, F32), "LL2": (16, F32),
-    "WIN": (NP + 2 * NA, BF), "FA": (Z + 2 * NA, F32), "FB": (LV * (N - 1) ** 2, F32), "T0": (NP, F32), "T1": (NP, F32), "T2": (NP, F32),
-    "YO": (NP, F32), "S3": (N3, U16), "SG": (NA, F32), "A12": (NA, F32), "S2": (NA, U16), "L0": (LV, U16), "AF": (NA, F32),
-    "KI": (8, I32), "CT": (64, F32), "OM": (128, BF), "EQ": (16, F32), "LT": (16, F32), "D8": (8, F32),
+    "M0": (24, F32), "M1": (24, F32), "FR": (24, BF), "K0": (24, F32), "K1": (24, F32),
+    "WIN": (NP + 2 * NA, BF), "FA": (NP + 2 * NA, F32), "T0": (NP, F32), "T1": (NP, F32), "T2": (NP, F32),
+    "YO": (NP, F32), "S3": (N3, U16), "SG": (NA, U16), "S2": (NA, U16), "L0": (LV, U16), "LA": (NA, U16),
+    "KI": (8, I32), "CT": (96, F32), "OM": (128, BF), "EQ": (16, F32), "LT": (16, F32), "D8": (8, F32),
     "BL0": (128, BF), "BLK": (128, BF), "ID": (128, BF), "I32": (128, F32), "G1": (144, BF), "GY": (144, BF), "GW": (144, BF),
-    "GC": (144, BF), "G2": (144, BF), "GK": (144, BF), "GN": (144, BF),
-    "MX": (128, BF), "MP": (128, BF), "MV0": (128, BF), "MV1": (128, BF), "MB": (128, BF), "NBL": (128, BF), "MD": (128, BF),
+    "GC": (144, BF), "G2": (144, BF), "G3": (144, BF), "GK": (144, BF), "GN": (144, BF),
+    "MX": (128, BF), "MV0": (128, BF), "MV1": (128, BF), "MC": (128, BF),
+    "MP": (128, BF), "MB": (128, BF), "NBL": (128, BF), "MD": (128, BF),
     "HH": (128, BF), "BN": (128, BF), "MY": (128, BF),
 }
 SCRATCH = {k: ("sbuf", [128, w], d) for k, (w, d) in SB.items()}
-SCRATCH.update({"RA": ("sbuf", [128, N - 1, RW], U16), "LA": ("sbuf", [128, N - 1, RW], U16), "L3": ("sbuf", [128, N - 1, W3], U16)})
+SCRATCH["L3"] = ("sbuf", [128, N - 1, W3], U16)
 SCRATCH.update({"Q%d" % i: ("psum", [128, 512], F32) for i in range(8)})
 SEMAPHORES = ["cV", "cP", "cS", "cG", "dB", "dP", "dC", "dL", "dT", "dY", "a1", "a2", "aR", "aS", "gone"] + ["a3%d" % s for s in range(N - 1)]
 
 ARR = {"a1": [15400, 15400, 16000, 16000, 16700, 16700, 15200, 0], "a2": [22400, 22800, 23400, 23400, 23200, 23200, 20000], "aR": 26000,
-       "a3": [27500, 27500, 28000, 28000, 27500, 27500, 24000]}
-TAIL = {"s1": 22000, "s2": 12000, "sR": 8000, "s3": 6500, "tb": 25500}
-AIM = {"a1": 2.0, "a2": 2.0, "aR": 0.5, "aS": 0.5, "a3": 2.0, "tb": 0.1}
-DUE = {"a1": [0, 13500, 13500, 13500, 13500, 13500, 13000, 13000], "a2": [0, 19800, 19500, 19500, 19500, 19500, 19800, 20500],
-       "aS": [22000], "aR": [20500, 22500, 23500, 23500, 24500, 24500, 25000], "a3": [24500, 25000, 26000, 26000, 27500, 27500, 28000]}
-PACE = [dict(c=0.95, g=1.4, s=3.2, p=0.47, y=100, t=0.9, w=1.05, a=1.0), dict(c=0.9, g=1.3, s=2.8, p=0.45, y=90, t=0.87, w=0.95, a=0.92),
-        dict(c=1.15, g=1.8, s=4.5, p=0.58, y=140, t=0.95, w=1.45, a=1.19), dict(c=0.87, g=1.1, s=2.0, p=0.43, y=120, t=1.0, w=1.3, a=1.03),
-        dict(c=1.1, g=1.3, s=4.5, p=0.5, y=80, t=0.85, w=0.9, a=1.03)]
-TRIES = 8000
-HEAT = 4000
+       "a3": [26600, 26700, 27400, 27600, 26900, 26800, 23000]}
+TAIL = {"s1": 22000, "s2": 12000, "sR": 8000, "s3": 6500, "tb": 24000}
+PACE = [dict(c=1.04, g=1.6, s=4.0, p=0.52, y=100, t=0.85, a=1.0, i=350, f=1500, h=600, k=750, r=17, b=1 / 18),
+        dict(c=0.9, g=1.3, s=2.8, p=0.45, y=90, t=0.97, a=0.95, i=350, f=1370, h=650, k=800, r=15, b=1 / 13),
+        dict(c=1.15, g=1.8, s=4.5, p=0.58, y=140, t=1.0, a=1.25, i=350, f=2200, h=800, k=1050, r=25, b=1 / 10),
+        dict(c=1.04, g=1.6, s=4.0, p=0.52, y=110, t=0.9, a=1.0, i=350, f=1100, h=550, k=650, r=14, b=1 / 18),
+        dict(c=1.0, g=1.55, s=3.8, p=0.5, y=100, t=0.75, a=0.95, i=300, f=2260, h=550, k=650, r=12, b=1 / 22)]
+ROOM = (2500, 1500, 1000, 800)
+TRIES = 3500
+HEAT = 2500
+SOFT = 0.05
 KEPT = {}
-PER = 2
-ALONE = {"a1": 0, "a2": 2, "aR": 0, "a3": 6}
+ALONE = {"a1": ([2, 2, 2], 1), "a2": ([1, 1, 2, 2], 0), "aR": ([2, 2, 2], 1), "a3": ([1] * 6, 1)}
 LATE = ()
 SPLIT = 0.4
+FEW = 128
+OUT = (0, 64, 192, NP)
+CUT = [(0, 160, NP), (0, 160, NP)]
 ORD1 = [0, 1, 2, 3, 4, 5, 6]
 
 
 def calls(topo, cores, src, dests):
     me = cores[src]
-    dests, alone = dests
+    dests, (sizes, side) = dests
     far = [d for d in dests if topo.chip(cores[d]) != topo.chip(me)]
     near = [d for d in dests if d not in far]
     out = []
     used = set()
-    for part in [far[i:i + 1] for i in range(min(alone, len(far)))] + [far[i:i + PER] for i in range(alone, len(far), PER)]:
+    for part in [far[sum(sizes[:i]):sum(sizes[:i + 1])] for i in range(len(sizes)) if sum(sizes[:i]) < len(far)]:
         eng = topo.engines(me, cores[part[0]])
         used.update(eng)
         share = [1] * len(part)
@@ -79,7 +84,7 @@ def calls(topo, cores, src, dests):
         eng = [e for e in topo.engines(me, cores[d]) if e not in used][:4]
         if not out:
             out.append([])
-        out[0].append((d, sum(1 << e for e in eng)))
+        out[min(side, len(out) - 1)].append((d, sum(1 << e for e in eng)))
     return out
 
 
@@ -87,6 +92,36 @@ def rank_program(g, core, T, topo):
     q = T.rank_of(core)
     if q is None:
         return
+    if not KEPT:
+        KEPT.update(arrange([program(g, r, T, topo) for r in range(N)]))
+    program(g, q, T, topo)["issue"](*KEPT[q])
+
+
+def arrange(ranks):
+    plan = [r["start"]() for r in ranks]
+    for turn in range(len(ROOM)):
+        for x in range(4):
+            ends = [r["worth"](*plan[q])[2] for q, r in enumerate(ranks)]
+            for q, r in enumerate(ranks):
+                for i, sem in r["lands"]:
+                    for k, p in enumerate(PACE):
+                        r["arr"][k][i] = max(ends[s][k][j] + p["k"] for s, o in enumerate(ranks) for j, to in o["goes"] if (q, sem) in to)
+        stop = [max(ends[q][k][i] for q, r in enumerate(ranks) for i in r["stores"]) for k in range(len(PACE))]
+        late = [[{} for p in PACE] for r in ranks]
+        for x in range(4):
+            for q, r in enumerate(ranks):
+                for k, p in enumerate(PACE):
+                    for j, to in r["goes"]:
+                        r["due"][k][j] = min(late[d][k].get(sem, 1e9) - p["k"] for d, sem in to)
+                    for j in r["stores"]:
+                        r["due"][k][j] = stop[k]
+                late[q] = r["latest"](*plan[q])
+        for q, r in enumerate(ranks):
+            plan[q] = r["improve"](*plan[q], turn)
+    return dict(enumerate(plan))
+
+
+def program(g, q, T, topo):
     cores = T.cores
     nb = N - 1 - q
     na, m = LV * nb, LV * q
@@ -97,6 +132,8 @@ def rank_program(g, core, T, topo):
     csem = {"V": "cV", "P": "cP", "S": "cS", "G": "cG"}
 
     def A(name, a=None, b=None, step=1):
+        if name == "V0":
+            name, a, b = "TB", RV + a, RV + b
         if a is None:
             a, b = 0, T[name].shape[1]
         elif b is None:
@@ -187,12 +224,12 @@ def rank_program(g, core, T, topo):
         add({"G": (lambda: g.affine_select(out[0], i[0], pat, o, fill, base, cm), (170, "c", 2 * out[2]))}, out, [i])
 
     def dma(e, out, src, region, sem, lat, ins=()):
-        add({e: (lambda: eng[e].dma_start(out, src), (60, "t", 0))}, (None, region), list(ins), sem=sem, lat=lat, tail=lat, aim=1.0 * (sem == "dY"))
+        add({e: (lambda: eng[e].dma_start(out, src), (60, "t", 0))}, (None, region), list(ins), sem=sem, lat=lat, tail=lat)
 
     def arrive(sem, count, regions, at):
         ops.append(dict(alt={None: (None, (0, "t", 0))}, W=regions, R=[], lat=0, tail=0, sem=sem, cnt=count, at=at))
 
-    sent, began = [0], []
+    sent, began, rowed = [0], [], {}
 
     def send(dests, src, dst, sem, tail):
         plan = calls(topo, cores, q, dests)
@@ -204,12 +241,21 @@ def rank_program(g, core, T, topo):
                 tr.append(RemoteDMATransfer(dst_ids=[DstId(rid=rid, pnc=pid)], dma_engine_mask=mask, remote_sem=T.sem[sem], src=s[0], dst=dst(d, call)))
                 rd.append(s)
                 sent[0] += bin(mask).count("1")
-            rows = 128 // bin(call[0][1]).count("1")
-            add({"G": (lambda tr=tr: g.remote_dma_fused(tr, local_sem=T.sem.gone), (0, "t", 400 if began else 2000))}, (None, ("call", len(ops), len(ops) + 1)), rd,
-                tail=tail, after=2 * (call is not plan[0]))
-            began.append(1)
-            add({"E": (None, (0, "w", rows * (18 + rd[0][2] * (4 if rd[0][3][2] == F32 else 2) / 16)))}, None, [(None, ("call", len(ops) - 1, len(ops)))],
-                tail=tail - 1200, aim=AIM[sem[:2]] / len(plan), due=DUE[sem[:2]][q] + 700 * plan.index(call), after=2 * (call is not plan[0]))
+            at = ("call", len(ops), len(ops) + 1)
+            add({"G": (lambda tr=tr: g.remote_dma_fused(tr, local_sem=T.sem.gone), (0, "i" if began else "f", 1))}, (None, at), rd,
+                tail=tail, tag=(sem[:2], plan.index(call)))
+            if call is not plan[0]:
+                ops[-1]["behind"] = began[-1]
+            began.append(ops[-1])
+            for e in "EN":
+                part = [(d, x) for d, x in call if (topo.chip(cores[d]) == topo.chip(cores[q])) == (e == "N")]
+                if part:
+                    rows, size = 128 // bin(part[0][1]).count("1"), rd[0][2] * (4 if rd[0][3][2] == F32 else 2)
+                    add({e: (None, (rows * size / 27 if e == "N" else 0, "r", rows, "b", rows * size * (e == "E")))}, None, [(None, at)],
+                        tail=tail - 1200, to=[(d, sem) for d, x in part])
+                    if (e, sem) in rowed:
+                        ops[-1]["behind"] = rowed[e, sem]
+                    rowed[e, sem] = ops[-1]
             tail -= 600
 
     def count(src, dests):
@@ -226,16 +272,18 @@ def rank_program(g, core, T, topo):
     def last(s):
         return [sorted((d for d, x in call), reverse=True) for call in calls(topo, cores, s, back(s))]
 
-    ms(A("RP"), 0, tail=40000)
+    ms(A("RP", 0, 288), 0, tail=40000)
+    iota(A("RP", 288, NP), [[0, NP - 288]], 0, 0)
+    ops[-1]["tail"] = 60000
     for h in range(2):
-        dma("S", T.RB[h::2, :], T.bm[:], ("RB", h, h + 1), "dB", 2500)
+        dma("S", T.TB[h::2, Z:Z + 512], T.bm[:], ("TB", Z + h, Z + h + 1), "dB", 2500)
         ops[-1]["tail"] = 50000
     for o in (0, 1, 2, 4, 5, 6):
-        dma("Y", T.RP[o::16, :], T.en[:] if o < 4 else T.sd[:], ("RP", o, o + 1), "dP", 2100)
+        dma("Y", T.RP[o::16, :], T.en[:] if o < 4 else T.sd[:], ("RP", o, o + 1), "dP", 2100, [A("RP", 288, NP)])
         ops[-1]["tail"] = 40000
     dma("Y", T.CS[:, Z:], T.cs[:], ("CS", Z, Z + NB), "dC", 4600, [(None, ("order", 0, 1))])
     dma("Y", T.LS[:, Z:], T.ls[:], ("LS", Z, Z + NB), "dL", 5900, [(None, ("order", 0, 1))])
-    for o in ops[1:9]:
+    for o in ops[2:10]:
         o["first"] = True
 
     col = {}
@@ -282,56 +330,64 @@ def rank_program(g, core, T, topo):
     ms(A("G1", 128, 144), 0.0)
     sel(A("G1", 0, 128), A("BLK"), [[0, 8], [1, 16]], OP.is_equal, 0.0, -15, 0)
     sel(A("ID"), A("ONE", 0, 128), [[-1, 128]], OP.is_equal, 0.0, 0, 1)
-    lin(A("I32"), A("ID"))
+    if nb:
+        lin(A("I32"), A("ID"))
     for G, w in (("GY", "wy"), ("GW", "w16"), ("G2", "g2")):
         lin(A(G), A("G1"), c_(w), 0.0, "V")
-    ts(A("GC"), A("G1"), LT(15), -C, OP.mult, OP.mult)
+    lin(A("G3"), A("G2"), LT(2), 0.0)
+    lin(c_("nc"), LT(15), -C, 0.0)
+    lin(A("GC"), A("G1"), c_("nc"), 0.0)
     lin(A("MX"), A("BLK"), EQ(0), 0.0, "V")
+    if 0 < na <= FEW:
+        lin(A("MC"), A("BLK"), LT(15), 0.0)
     lin(A("MV0"), A("BLK"), c_("v0"), 0.0, "V")
     lin(A("MV1"), A("BLK"), c_("v1"), 0.0, "V")
     ts(A("HH"), A("OM"), EQ(15), LT(15), OP.mult, OP.subtract)
-    lin(A("BN"), A("BLK"), -2.0 ** 20, 0.0, "V")
+    lin(A("BN"), A("BLK"), -2.0 ** 20, 0.0)
     tt(A("MY"), A("HH"), A("BN"), OP.mult)
     if q:
         ts(A("MP"), A("BLK"), c_("w16"), 16.0, OP.mult, OP.mult)
         lin(A("NBL"), A("BLK"), -1.0, 0.0, "V")
-        ts(A("MD"), A("BLK"), LT(q), 2.0 ** 21, OP.mult, OP.mult)
+        lin(c_("dead"), LT(q), 2.0 ** 21, 0.0)
+        lin(A("MD"), A("BLK"), c_("dead"), 0.0)
         ts(A("MB"), A("BLK"), LT(15), C, OP.mult, OP.mult)
         sel(A("MB"), A("MB"), [[0, 128]], OP.not_equal, -BAND / 2, -15, 1)
         sel(A("MB"), A("MB"), [[0, 128]], OP.not_equal, 0.5, -31, 1)
         sel(A("MB"), A("MB"), [[0, 8], [1, 16]], OP.not_equal, -8.5 * BAND, -16 * 47, 16)
         sel(A("MB"), A("MB"), [[0, 8], [1, 16]], OP.not_equal, -BAND * (63.5 + q), -16 * 63 - q, 16)
-        lin(c_("s1a"), EQ(0), M20 - M16, M16, "V")
-        lin(c_("s1"), EQ(q), M23 - M16, c_("s1a"), "V")
-        lin(c_("s2a"), c_("o"), float(BAND), c_("s1"), "V")
-        lin(c_("s2"), EQ(0), -2.0 ** 20, c_("s2a"), "V")
+        lin(c_("s1a"), EQ(0), M20 - M16, M16)
+        lin(c_("s1"), EQ(q), M23 - M16, c_("s1a"))
+        lin(c_("s2a"), c_("o"), float(BAND), c_("s1"))
+        lin(c_("s2"), EQ(0), -2.0 ** 20, c_("s2a"))
+        ms(A("CQ"), -float(BK * q))
         lin(c_("ia"), c_("o"), float(LV), float(W1))
         lin(c_("i1"), c_("ia"), LT(q), 0.0)
         lin(c_("i0"), LT(q), float(m), c_("i1"))
         fill("WIN", W1, W0 + m, EMPTY)
-        ms(A("FA", 0, Z), 0.0)
-        iota(A("K0"), [[16, 16]], 0, 0)
-        for s in range(1, q):
-            fill("FB", m * s, m * s + LV * (s + 1), 0)
     if nb:
-        lin(A("GK"), A("GC"), -1 / 16, 0.0, "V")
-        lin(A("GN"), A("G1"), -1 / 16, 0.0, "V")
+        if na > FEW:
+            lin(A("GK"), A("GC"), -1 / 16, 0.0)
+        lin(A("GN"), A("G1"), -1 / 16, 0.0)
     ms(A("L2", 14, 16), 0.0)
 
-    lin(A("RB2"), A("RB"), c_("sB"), c_("cB"))
+    lin(A("RB2"), A("TB", Z, Z + 512), c_("sB"), c_("cB"))
     ts(A("RB3"), A("RB2"), 2047, None, OP.bitwise_and)
-    for a in (0, NP // 2):
-        b = a + NP // 2
+    for a, b in zip(CUT[0], CUT[0][1:]):
         lin(A("RP2", a, b), A("RP", a, b), c_("sP"), c_("cP"))
         ops[-1]["R"].append(("RP", 0, NP))
-        ts(A("RP3", a, b), A("RP2", a, b), 255, None, OP.bitwise_and)
-        lin(A("P0", a, b), A("RP3", a, b))
-    fill("TB", Z, Z + BK, 0)
-    ms(A("TB", 0, Z), -8192)
-    ms(A("TB", Z + BK, 2 * Z + BK), -8192)
-    for o in range(2):
-        dma("Y", T.TB[o::16, Z:Z + BK], T.RB3[o::2, :], ("TBd", o, o + 1), "dT", 2900, [A("RB3"), A("TB", Z, Z + BK)])
-        ops[-1].update(tail=TAIL["tb"], aim=AIM["tb"])
+        ts(A("TB", R3 + a, R3 + b), A("RP2", a, b), 255, None, OP.bitwise_and)
+        lin(A("P0", a, b), A("TB", R3 + a, R3 + b))
+    fill("TB", RV + NP, Z + BK, 0)
+    ms(A("TB", 0, Z), -60000)
+    ms(A("TB", Z + BK, 2 * Z + BK), -60000)
+
+    def spread():
+        for o in range(2):
+            dma("Y", T.TB[o::16, Z:Z + BK], T.RB3[o::2, :], ("TBd", o, o + 1), "dT", 2900, [A("RB3"), A("TB", Z, Z + BK)])
+            ops[-1]["tail"] = TAIL["tb"]
+        ops[-2]["W"].append(("TB", Z, RV + NP))
+        ops[-1].update(R=[], behind=ops[-2])
+
     TBL = (T.TB[:, 0:BK + 2 * Z], ("TB", 0, BK + 2 * Z), BK + 2 * Z, SCRATCH["TB"])
 
     def seeds(out, M, pay, a, b, bank):
@@ -344,21 +400,25 @@ def rank_program(g, core, T, topo):
             lin(A(gh, ga + 16 * a, ga + 16 * b), IND(TBL, A("LB", at + a, at + b)))
             ops[-1]["R"].append(("TBd", 0, 2))
         tt(A("XN", at, at + k), xs, A("LB", at, at + k), OP.subtract)
-        mm(A(bank, 0, k), A("I32"), A("XN", at, at + k), True, False)
-        x = wrap(bank, "G2", gh, ga, ga + 16 * k, False, True)
-        lin(A("LN", at, at + k), x, 1.0, 2 * Z + 1 - HALF - BK * q)
+        x = wrap(bank, "G3", gh, ga, ga + 16 * k, True, False)
+        mm(x, A("ID"), A("XN", at, at + k), False, True)
+        lin(A("LN", at, at + k), x, 1.0, 2 * Z + 1 - HALF)
 
     def lookup(pay, a, b, at, bx, bl, cuts):
         k = (b - a) // 16
-        x = wrap(bx, "GW", pay, a, b)
+        if q:
+            mm(A(bx, 0, k), A("ID"), A("CQ", 0, k), True, False)
+        x = wrap(bx, "GW", pay, a, b, not q)
         if not q:
             relu(A("XS", at, at + k), x)
             x = A("XS", at, at + k)
-        if a < NP:
-            lin(A("LB", at, at + k), x, 1.0, Z - HALF - BK * q)
+        lin(A("LB", at, at + k), x, 1.0, Z - HALF)
+        if len(bl) == 2:
+            bins(x, at, "GH", a, bl, cuts)
         else:
-            ts(A("LB", at, at + k), x, Z - HALF - BK * q, float(Z + BK), OP.add, OP.min)
-        bins(x, at, "GH", a, bl, cuts)
+            for u, v, bank in zip(cuts, cuts[1:], bl):
+                part = A(bx, u, v) if q else A("XS", at + u, at + v)
+                bins(part, at + u, "GH", a + 16 * u, bank, [0, v - u])
 
     def react(a, b, ln, V, Y):
         lin(A("LG", a, b), IND(A("LS"), ln), on="S")
@@ -367,9 +427,8 @@ def rank_program(g, core, T, topo):
         mm(Y, A("MY"), A("BITS", a, b), False, True)
         ts(A("PR", a, b), Y, 0.0, C, OP.max, OP.min)
 
-    own = [(0, NP // 2, "Q0", "Q1"), (NP // 2, NP, "Q2", "Q3")]
-
     def event(t, old, new, V, at, wend):
+        own = list(zip(CUT[t], CUT[t][1:], ("Q0", "Q2", "Q5"), ("Q1", "Q3", "Q6")))
         p = 8 + t
         lst = "LS%d" % t
         for a, b, bY, bX in own:
@@ -396,34 +455,31 @@ def rank_program(g, core, T, topo):
             tt(A("DD", a, b), A("SS", a, b), D, OP.mult)
             if t == 0:
                 lin(A("MK", a, b), D, on="S")
-            x = wrap(bX, "G1", "DD", a, b)
-            lin(A(lst, ka, kb), x, 1.0, -1.0)
+            lin(A(lst, ka, kb), wrap(bX, "G1", "DD", a, b), 1.0, -1.0)
             lin(IND(A("WIN", 0, wend), A(lst, ka, kb)), A(new, a, b), on="V")
-            if t == 0:
-                lin(A("M0", ka, kb), x)
-            else:
-                tt(A("M1", ka, kb), x, A("M0", ka, kb), OP.max)
 
     k = NP // 16
     O0, O1, O2, A1, A2, H3 = 0, 24, 48, 72, 88, 104
 
-    seeds("V0", "MV0", "P0", 0, NP, "Q0")
-    seeds("V1", "MV1", "P0", 0, NP, "Q2")
     y = wrap("Q6", "GY", "P0", 0, NP)
     lin(A("LB", O0, O0 + k), y, 1.0, -HALF)
-    mm(A("Q4", 0, NP), A("MX"), A("P0"), True, True)
-    ts(A("MS"), A("Q4", 0, NP), -8.0 * q, c_("seg"), OP.add, OP.is_equal)
-    tt(A("GH", 0, NP), IND(A("RB3"), A("LB", O0, O0 + k)), A("MS"), OP.mult)
-    tt(A("XN", O0, O0 + k), y, A("LB", O0, O0 + k), OP.subtract)
-    mm(A("Q7", 0, k), A("I32"), A("XN", O0, O0 + k), True, False)
-    x = wrap("Q7", "G2", "GH", 0, NP, False, True)
-    lin(A("LN", O0, O0 + k), x, 1.0, Z + 1 - HALF)
+    tt(A("FR"), y, A("LB", O0, O0 + k), OP.subtract)
+    for a, b, bm, bv, bl in zip(CUT[0], CUT[0][1:], ("Q4", "Q1"), ("Q0", "Q2"), ("Q7", "Q5")):
+        ka, kb = O0 + a // 16, O0 + b // 16
+        seeds("V0", "MV0", "P0", a, b, bv)
+        mm(A(bm, 0, b - a), A("MX"), A("P0", a, b), True, True)
+        ts(A("MS", a, b), A(bm, 0, b - a), -8.0 * q, c_("seg"), OP.add, OP.is_equal)
+        tt(A("GH", a, b), IND(A("RB3"), A("LB", ka, kb)), A("MS", a, b), OP.mult)
+        x = wrap(bl, "G2", "GH", a, b, True, False)
+        mm(x, A("ID"), A("FR", a // 16, b // 16), False, True)
+        lin(A("LN", ka, kb), x, 1.0, Z + 1 - HALF)
+    seeds("V1", "MV1", "P0", 0, NP, "Q3")
     event(0, "P0", "PA", "V0", O0, W0 + m)
-    lin(A("T0"), IND(A("CS"), A("LN", O0, O0 + k)))
+    spread()
     send(first(q), lambda d, c: A("WIN", W0 + LV * d, W0 + LV * (d + 1)),
          lambda d, c: T.PA[:, NP + LV * (q - d - 1):NP + LV * (q - d)], "a1", TAIL["s1"])
 
-    lookup("PA", 0, NP, O1, "Q6", "Q7", [0, k // 2, k])
+    lookup("PA", 0, NP, O1, "Q6", ["Q7", "Q5", ""], [x // 16 for x in CUT[1]])
     event(1, "PA", "PB", "V1", O1, W0)
     if q:
         relu(A("L2", 0, 2 * q), wrap("Q1", "GW", "WIN", W1, W0))
@@ -432,23 +488,38 @@ def rank_program(g, core, T, topo):
         arrive("a1", sum(count(r, first(r)) for r in up(q)), [("PA", NP, e)], ARR["a1"][q])
         seeds("V1", "MV1", "PA", NP, e, "Q5")
         lookup("PA", NP, e, A1, "Q6", "Q7", [0, ka])
-        react(NP, e, A("LN", A1, A1 + ka), "V1", A("Q5", 0, na))
+        Y, ln = A("Q5", 0, na), A("LN", A1, A1 + ka)
+        if na > FEW:
+            react(NP, e, ln, "V1", Y)
+        else:
+            lin(A("LG", NP, e), IND(A("LS"), ln), on="S")
+            tt(A("BITS", NP, e), IND(A("CS"), ln), A("V1", NP, e), OP.is_le)
+            mm(Y, A("MC"), A("BITS", NP, e), True, True)
+            ts(Y, Y, c_("o"), None, OP.is_equal)
+            tt(A("PR", NP, e), A("LG", NP, e), Y, OP.mult)
         if q:
-            lin(A("XS", A1, A1 + ka), A("Q6", 0, ka))
+            lin(A("XS", A1, A1 + ka), A("Q6", 0, ka), 1.0, float(BK * q))
         mm(A("Q6", 0, ka), A("I32"), A("XS", A1, A1 + ka), True, False)
-        wrap("Q6", "GK", "BITS", NP, e, False, False)
+        if na > FEW:
+            wrap("Q6", "GK", "BITS", NP, e, False, False)
         x = wrap("Q6", "GN", "PR", NP, e, False, True)
-        ts(A("L2", 2 * q, 14), x, 0.0, BK * (q + 1) - 1 / 16, OP.max, OP.min)
+        relu(A("L2", 2 * q, 14), x)
     send(second(q), lambda d, c: A("L2", 0, 16), lambda d, c: T.L2[:, 16 * (q - d):16 * (q - d + 1)], "a2", TAIL["s2"])
 
     gate = ops[-1 if nb == 0 else max(i for i, o in enumerate(ops) if o["W"] and o["W"][0][0] == "L2")]
     x = len(ops)
+    lin(A("T0"), IND(A("CS"), A("LN", O0, O0 + k)))
+    if q:
+        fill("FA", 0, W0 + m, 0.0)
+        iota(A("K0"), [[16, 24]], 0, 0)
+        lin(A("K1"), A("K0"), 1.0, c_("o"))
+        tt(A("M0"), A("LS0"), A("LS1"), OP.max)
+        tt(A("LF"), A("M0"), A("K1"), OP.max)
     tt(A("T1"), IND(A("CS"), A("LN", O1, O1 + k)), A("T0"), OP.add)
     lookup("PB", 0, NP, O2, "Q0", "Q2", [0, k])
     tt(A("T2" if q else "YO"), IND(A("CS"), A("LN", O2, O2 + k)), A("T1"), OP.add)
     if not q:
         dma("Y", T.y[:], T.YO[:], ("y", 0, 1), "dY", 2500, [A("YO")])
-        ops[-1]["due"] = DUE["a3"][0]
     else:
         for o in ops[x:]:
             o["behind"] = gate
@@ -457,15 +528,13 @@ def rank_program(g, core, T, topo):
         lin(A("SG", 0, na), IND(A("CS"), A("LN", A1, A1 + ka)))
         if q not in LATE:
             lin(A("LB", A2, A2 + ka), xs, 1.0, Z - HALF - BK * q)
+            if q:
+                lin(A("XS", A2, A2 + ka), xs, 1.0, -float(BK * q))
+                xs = A("XS", A2, A2 + ka)
             bins(xs, A2, "GH", NP, "Q7", [0, ka // 4 * 2, ka] if ka > 8 else [0, ka])
         if q:
-            tt(A("A12", 0, na), IND(A("CS"), A("LN", A2, A2 + ka)), A("SG", 0, na), OP.add)
-            lin(A3("RA", 0, nb, 0, LV), A("A12", 0, na))
-            lin(A3("RA", 0, nb, LV, RW), xs, 1 / BK, 2.0 ** -17 - 0.5)
-        else:
-            lin(A3("RA", 0, nb, 0, LV), A("SG", 0, na))
-            ms(A3("RA", 0, nb, LV, RW), 0)
-        send(reply(q), lambda d, c: A3("RA", d - q - 1, d - q, 0, RW), lambda d, c: T.LA[:, q:q + 1, :], "aR", TAIL["sR"] + (0 if q else 6000))
+            tt(A("S2", 0, na), IND(A("CS"), A("LN", A2, A2 + ka)), A("SG", 0, na), OP.add)
+        send(reply(q), lambda d, c: A("S2" if q else "SG", LV * (d - q - 1), LV * (d - q)), lambda d, c: T.LA[:, m:m + LV], "aR", TAIL["sR"] + (0 if q else 6000))
         if not q and not LATE:
             lin(A("S2"), IND(A("CS"), A("LN", A2, A2 + ka)))
             send(reply(q), lambda d, c: A("S2", LV * (d - 1), LV * d), lambda d, c: T.L0[:], "aS", TAIL["sR"] + 2000)
@@ -480,12 +549,11 @@ def rank_program(g, core, T, topo):
         kp = -(-at // 16)
         if at % 16:
             ms(A("PLC", at, 16 * kp), 0.0)
-        lin(A("PL", 0, kp), wrap("Q5", "G1", "PLC", 0, 16 * kp), 1 / 16, 0.0)
-        ops[-1]["early"] = ops[-2]["early"] = True
+        lin(A("PL", 0, kp), wrap("Q3", "G1", "PLC", 0, 16 * kp), 1 / 16, 0.0)
         arrive("a2", sum(count(r, second(r)) for r in up(q)), [("L2", 16, 16 * (nb + 1))], ARR["a2"][q])
         xl = IND(A("L2", 0 if q in LATE else 16, 16 * (nb + 1)), A("PL", 0, kp))
         ts(A("LB", H3, H3 + 16 * kp), xl, Z - HALF - BK * q, float(Z + BK), OP.add, OP.min)
-        lin(A("XS", H3, H3 + 16 * kp), xl, on="S")
+        lin(A("XS", H3, H3 + 16 * kp), xl, 1.0, -float(BK * q), on="S")
         cut = min((end[c[-1]] for c in last(q)), key=lambda x: abs(x - SPLIT * at)) if at > 24 else at
         for a, b, bank in ((0, cut, "Q5"), (cut, at, "Q6")):
             if b > a:
@@ -500,39 +568,47 @@ def rank_program(g, core, T, topo):
         send(back(q), lambda d, c: A("S3", 16 * end[d] - wide(c), 16 * end[d]), lambda d, c: T.L3[:, q, W3 - wide(c):W3], "a3%d" % q, TAIL["s3"])
 
     if q:
-        lin(A("LF"), A("M1"), 1.0, Z - 1.0 - NP)
-        arrive("aR", sum(count(s, reply(s)) for s in low(q)), [("LA", 0, q)], ARR["aR"])
-        if not LATE:
-            arrive("aS", count(0, reply(0)), [("L0", 0, LV)], ARR["aR"])
-            lin(A("FB", 0, LV), A("L0"))
-        lin(A("AF", 0, m), A3("LA", 0, q, 0, LV))
-        lin(A("LL1", 0, 2 * q), A3("LA", 0, q, LV, RW), float(m), c_("o"))
-        tt(A("LL2", 0, 2 * q), A("LL1", 0, 2 * q), A("K0", 0, 2 * q), OP.add)
-        lin(A("LL", 0, 2 * q), A("LL2", 0, 2 * q))
-        for s in low(q):
-            c = max(c for c in last(s) if q in c)
-            arrive("a3%d" % s, count(s, back(s)), [("L3", s, s + 1)], ARR["a3"][s] + 500 * last(s).index(c))
-            if blocks(s, q) > 1:
-                lin(A("FB", m * (s + 1) - LV * (blocks(s, q) - 1), m * (s + 1)), A3("L3", s, s + 1, W3 - LV * blocks(s, q), W3 - LV))
-        runs = []
-        for s in low(q):
-            if runs and topo.chip(cores[s]) == topo.chip(cores[s - 1]):
-                runs[-1][1] = s + 1
-            else:
-                runs.append([s, s + 1])
-        for a, b in runs:
-            lin(A("FA", Z + LV * a, Z + LV * b), A3("L3", a, b, W3 - LV, W3))
-        tt(A("FA", Z + m, Z + 2 * m), IND(A("FB", 0, m * q), A("LL", 0, 2 * q)), A("AF", 0, m), OP.add)
-        for h, x in enumerate("YS"):
-            a, b = h * NP // 2, (h + 1) * NP // 2
-            tt(A("YO", a, b), IND(A("FA", 0, Z + 2 * m), A("LF", a // 16, b // 16)), A("T2", a, b), OP.add)
-            dma(x, T.y[:, a:b], T.YO[:, a:b], ("y", h, h + 1), "dY", 2500, [A("YO", a, b)])
+        def more(a, b, x):
+            tt(A("FA", a, b), x, A("FA", a, b), OP.add)
 
-    early = [i for i, o in enumerate(ops) if o.get("early")]
-    if early:
-        at = next(i for i, o in enumerate(ops) if o["sem"] == "a1")
-        moved = [i for i, o in enumerate(ops) if i > at and (o.get("early") or any(r[0] == "PLC" for r in o["W"]))]
-        ops[:] = ops[:at] + [ops[i] for i in moved] + [o for i, o in enumerate(ops) if i >= at and i not in moved]
+        lin(IND(A("FA", 0, W0 + m), A("LF", k // 2, k)), A("T2", NP // 2, NP), on="V")
+        arrive("aR", sum(count(s, reply(s)) for s in low(q)), [("LA", 0, m)], ARR["aR"])
+        z = 0 if LATE else LV
+        if z:
+            arrive("aS", count(0, reply(0)), [("L0", 0, LV)], ARR["aR"])
+            more(W0, W0 + LV, A("LA", 0, LV))
+            more(W0, W0 + LV, A("L0"))
+        if m > z:
+            tt(A("Q1", z, m), A("LA", z, m), A("FA", W0 + z, W0 + m), OP.add)
+        lin(A("Q3", 0, m), A("FA", W1, W0))
+        when = {}
+        for s in low(q):
+            at = ARR["a3"][s]
+            for call in calls(topo, cores, s, back(s)):
+                at += 128 // bin(call[0][1]).count("1") * (18 + 4 * blocks(s, max(call)[0]))
+                if q in [d for d, x in call]:
+                    when[s] = at
+        for s in sorted(low(q)[1:], key=when.get) + [0]:
+            arrive("a3%d" % s, count(s, back(s)), [("L3", s, s + 1)], when[s])
+            w = LV * (blocks(s, q) - 1)
+            if w:
+                tt(A("Q1", m - w, m) if s else A("FA", W0 + z, W0 + m), A3("L3", s, s + 1, W3 - LV - w, W3 - LV), A("Q1", m - w, m), OP.add)
+        tt(A("FA", W1, W0), A3("L3", 0, q, W3 - LV, W3), A("Q3", 0, m), OP.add)
+        for a, b in zip(OUT, OUT[1:]):
+            if a >= NP // 2:
+                lin(A("YO", a, b), IND(A("FA", 0, W0 + m), A("LF", a // 16, b // 16)), on="S")
+            else:
+                tt(A("YO", a, b), IND(A("FA", 0, W0 + m), A("LF", a // 16, b // 16)), A("T2", a, b), OP.add)
+            dma("YS"[a >= NP // 2], T.y[:, a:b], T.YO[:, a:b], ("y", a, b), "dY", 2500, [A("YO", a, b)])
+
+    at = next(i for i, o in enumerate(ops) if o["sem"] == "dT")
+    moved = [o for o in ops[:at] if o["W"][0][0] in ("GK", "GN", "MD", "MC", "L2", "I32", "G3")]
+    for o in moved:
+        o["behind"] = ops[at]
+    ops[:] = [o for o in ops[:at + 2] if all(o is not x for x in moved)] + moved + ops[at + 2:]
+    for o in ops:
+        if q and o["W"] and o["W"][0][0] == "PLC" and "G" in o["alt"]:
+            o["behind"] = [x for x in began if x["tag"][0] == "a1"][-1]
     hit = lambda x, y: x[1] < y[2] and y[1] < x[2]
     acc = {}
     for i, o in enumerate(ops):
@@ -549,8 +625,8 @@ def rank_program(g, core, T, topo):
                     dep[j] = "data"
         if o["R"] and o["R"][0][0] == "order":
             dep = {j: "order" for j in range(i) if ops[j].get("first") or ops[j]["sem"] == "dC"}
-        if o.get("after"):
-            dep[i - 2] = "order"
+        if "to" in o:
+            dep = {j: "call" for j in dep}
         if "behind" in o:
             dep.setdefault(next(j for j in range(i) if ops[j] is o["behind"]), "order")
         o["dep"] = dep
@@ -559,7 +635,7 @@ def rank_program(g, core, T, topo):
         for r in o["W"]:
             acc.setdefault(r[0], []).append((i, r, True))
     n = len(ops)
-    spans = [[{e: c[0] + p[c[1]] * c[2] for e, (f, c) in o["alt"].items()} for o in ops] for p in PACE]
+    spans = [[{e: c[0] + sum(p[x] * y for x, y in zip(c[1::2], c[2::2])) for e, (f, c) in o["alt"].items()} for o in ops] for p in PACE]
     full = [list(o["dep"].items()) for o in ops]
     above, deps = [], []
     for i in range(n):
@@ -571,7 +647,9 @@ def rank_program(g, core, T, topo):
         return kind == "order" or (ej == e and (e == "P" or kind == "bank"))
 
     def gap(j, kind, ej, e, p):
-        return 0 if free(j, kind, ej, e) else (ops[j]["lat"] * p["t"] if ops[j]["sem"] else p["y"])
+        if kind == "call":
+            return p["h"]
+        return 0 if free(j, kind, ej, e) else (ops[j]["lat"] * p["t"] if ops[j]["lat"] else p["y"])
 
     def place(noise, lean):
         p, sp = PACE[0], spans[0]
@@ -580,7 +658,7 @@ def rank_program(g, core, T, topo):
             tail[i] += min(sp[i].values()) + noise[i]
             for j, kind in deps[i]:
                 tail[j] = max(tail[j], tail[i] + gap(j, kind, 0, 1, p))
-        at, on, busy = [0] * n, [None] * n, {x: [] for x in list(eng) + ["E"]}
+        at, on, busy = [0] * n, [None] * n, {x: [] for x in list(eng) + ["E", "N"]}
         for i in sorted(range(n), key=lambda i: (-tail[i], i)):
             best = None
             for e, d in sp[i].items():
@@ -603,22 +681,34 @@ def rank_program(g, core, T, topo):
             at[i], on[i] = t, e
         return at, on, busy
 
-    aims = [(i, o["aim"], o.get("due", 0)) for i, o in enumerate(ops) if o.get("aim")]
+    goes = [(i, o["to"]) for i, o in enumerate(ops) if "to" in o]
+    stores = [i for i, o in enumerate(ops) if o["sem"] == "dY"]
+    lands = [(i, o["sem"]) for i, o in enumerate(ops) if None in o["alt"]]
+    aims = [i for i, to in goes] + stores
+    arr = [{i: ops[i]["at"] * p["a"] for i, sem in lands} for p in PACE]
+    due = [{i: 0 for i in aims} for p in PACE]
+    room = [0]
     fixed = [next(iter(o["alt"])) if len(o["alt"]) == 1 else 0 for o in ops]
     edges = [[[(j, gap(j, kind, fixed[j], fixed[i] if kind == "data" else 1, p), kind == "bank") for j, kind in deps[i]] for i in range(n)] for p in PACE]
+    way = [o["tail"] for o in ops]
+    for i in range(n - 1, -1, -1):
+        way[i] += min(spans[0][i].values())
+        for j, kind in deps[i]:
+            way[j] = max(way[j], way[i] + gap(j, kind, 0, 1, PACE[0]))
+    soft = [SOFT * min(1.0, x / 30000) ** 4 for x in way]
     succ = [[] for i in range(n)]
     for i in range(n):
         for j, kind in deps[i]:
             succ[j].append(i)
 
     def worth(order, on):
-        v, why = 0, []
-        for p, sp, ed in zip(PACE, spans, edges):
+        v, why, ends, over = 0, [], [], []
+        for p, sp, ed, come, by in zip(PACE, spans, edges, arr, due):
             end, prev, cause = [0] * n, {}, [-1] * n
             for i in order:
                 e = on[i]
                 c = prev.get(e, -1)
-                t = end[c] if c >= 0 else ops[i]["at"] * p["a"] if e is None else 0
+                t = end[c] if c >= 0 else come[i] if e is None else 0
                 for j, d, bank in ed[i]:
                     x = end[j] if bank and on[j] == e else end[j] + d
                     if x >= t:
@@ -626,18 +716,37 @@ def rank_program(g, core, T, topo):
                 end[i], cause[i] = t + sp[i][e], c
                 if e:
                     prev[e] = i
-            v += sum(a * (0.15 * end[i] + max(0, end[i] - due * p["a"])) for i, a, due in aims) / p["a"]
+            late = [max(0, end[i] + room[0] - by[i]) for i in aims]
+            v += (sum(late) + max(late) + 0.05 * sum(end[i] for i in aims) + sum(x * y for x, y in zip(end, soft))) / p["a"]
             why.append(cause)
-        return v, why
+            ends.append(end)
+            over.append(late)
+        return v, why, ends, over
 
-    def improve(order, on):
-        rng = np.random.default_rng(q)
-        best, why = worth(order, on)
+    def latest(order, on):
+        out = []
+        for sp, ed, by in zip(spans, edges, due):
+            req, nxt = [1e9] * n, {}
+            for i in order[::-1]:
+                e = on[i]
+                req[i] = min(req[i], by.get(i, 1e9), nxt.get(e, 1e9))
+                t = req[i] - sp[i][e]
+                if e:
+                    nxt[e] = t
+                for j, d, bank in ed[i]:
+                    req[j] = min(req[j], t if bank and on[j] == e else t - d)
+            out.append({sem: req[i] for i, sem in lands})
+        return out
+
+    def improve(order, on, turn):
+        rng = np.random.default_rng([q, turn])
+        room[0] = ROOM[turn]
+        best, why, ends, over = worth(order, on)
         kept = (best, order, on)
-        share = np.array([a for i, a, due in aims])
         for it in range(TRIES):
-            cause = why[int(rng.integers(len(PACE)))]
-            i, pairs = aims[int(rng.choice(len(aims), p=share / share.sum()))][0], []
+            k = int(rng.integers(len(PACE)))
+            cause, share = why[k], np.array(over[k]) + 30.0
+            i, pairs = aims[int(rng.choice(len(aims), p=share / share.sum()))], []
             while cause[i] >= 0:
                 j = cause[i]
                 if on[j] == on[i] and i not in succ[j]:
@@ -677,20 +786,24 @@ def rank_program(g, core, T, topo):
                     continue
                 part = order[pos[j]:pos[i] + 1]
                 new[pos[j]:pos[i] + 1] = [x for x in part if x in go] + [x for x in part if x not in go]
-            v, w = worth(new, no)
-            if v <= best + HEAT * (1 - it / TRIES) ** 2 * rng.random():
-                best, why, order, on = v, w, new, no
+            v, w, ends, ov = worth(new, no)
+            if v <= best + HEAT / (1 + turn) * (1 - it / TRIES) ** 2 * rng.random():
+                best, why, over, order, on = v, w, ov, new, no
                 if v < kept[0]:
                     kept = (v, new, no)
         return kept[1:]
 
-    if q not in KEPT:
+    def start():
         at, on, busy = place([0.0] * n, [100.0] * n)
-        KEPT[q] = improve(sorted(range(n), key=lambda i: (at[i], i)), on)
-    order, on = KEPT[q]
+        return sorted(range(n), key=lambda i: (at[i], i)), on
+
+    return dict(start=start, worth=worth, latest=latest, improve=improve, goes=goes, stores=stores, lands=lands, arr=arr, due=due,
+                issue=lambda order, on: issue(g, T, ops, full, free, eng, csem, sent[0], order, on))
+
+
+def issue(g, T, ops, full, free, eng, csem, sent, order, on):
     at = {i: k for k, i in enumerate(order)}
     busy = {x: [(0, 0, i) for i in order if on[i] == x] for x in eng}
-
     total = {}
     for o in ops:
         if o["sem"]:
@@ -732,5 +845,5 @@ def rank_program(g, core, T, topo):
             elif i in num:
                 ins.then_inc(T.sem[csem[x]], 1)
     g.sync.wait_ge(T.sem.dY, total["dY"])
-    if sent[0]:
-        g.wait_ge(T.sem.gone, sent[0])
+    if sent:
+        g.wait_ge(T.sem.gone, sent)

import numpy as np
from concourse.bass import DstId, RemoteDMATransfer
from concourse.mybir import AluOpType as OP, AxisListType, ActivationFunctionType as AF

N, NP, LV, NB, BAND = 8, 384, 32, 2048, 65536
BK = BAND // 16
NA = LV * (N - 1)
NW = NP + NA
W3 = NA + LV
N3 = LV * (N + 2) * (N - 1) // 2
Z = 8
R3, RV = Z + 512, Z + 512 + NP
RW = 34
EMPTY = -64.0
M16, M20, M23 = (1.5 * 2.0 ** (23 + k) for k in (16, 20, 23))
HALF = 7.5 / 16

F32, BF, I32, F16, U16 = "float32", "bfloat16", "int32", "float16", "uint16"
SB = {
    "CS": (Z + NB, I32), "LS": (Z + NB, BF), "RB2": (512, I32), "RB3": (512, I32), "TB": (BK + 2 * Z, I32),
    "XN": (184, BF), "CQ": (24, BF), "RP": (NP, I32), "RP2": (NP, I32), "P0": (NP, BF), "PA": (NW, BF), "PB": (NP, BF),
    "V1": (NW, F32), "BITS": (NW, BF), "LG": (NW, BF), "PR": (NW, BF), "SS": (NP, F32), "DD": (NP, F16),
    "MK": (NP, BF), "MS": (NP, BF), "GH": (NW, F16), "G3H": (N3, F16), "ONE": (256, BF),
    "LB": (184, U16), "LN": (184, U16), "XS": (184, F32), "L2": (16 * N, F32),
    "LS0": (24, U16), "LS1": (24, U16), "LL": (16, U16), "LF": (24, U16), "PL": (6, U16), "PLC": (80, BF),
    "M0": (24, F32), "M1": (24, F32), "FR": (24, BF), "K0": (24, F32), "K1": (24, F32),
    "WIN": (NP + 2 * NA, BF), "FA": (NP + 2 * NA, F32), "T0": (NP, F32), "T1": (NP, F32), "T2": (NP, F32),
    "YO": (NP, F32), "S3": (N3, U16), "SG": (NA, U16), "S2": (NA, U16), "L0": (LV, U16), "LA": (NA, U16),
    "KI": (8, I32), "CT": (96, F32), "OM": (128, BF), "EQ": (16, F32), "LT": (16, F32), "D8": (8, F32),
    "BL0": (128, BF), "BLK": (128, BF), "ID": (128, BF), "I32": (128, F32), "G1": (144, BF), "GY": (144, BF), "GW": (144, BF),
    "GC": (144, BF), "G2": (144, BF), "G3": (144, BF), "GK": (144, BF), "GN": (144, BF),
    "MX": (128, BF), "MV0": (128, BF), "MV1": (128, BF), "MC": (128, BF),
    "MP": (128, BF), "MB": (128, BF), "NBL": (128, BF), "MD": (128, BF),
    "HH": (128, BF), "BN": (128, BF), "MY": (128, BF),
}
SCRATCH = {k: ("sbuf", [128, w], d) for k, (w, d) in SB.items()}
SCRATCH["L3"] = ("sbuf", [128, N - 1, W3], U16)
SCRATCH.update({"Q%d" % i: ("psum", [128, 512], F32) for i in range(8)})
SEMAPHORES = ["cV", "cP", "cS", "cG", "dB", "dP", "dC", "dL", "dT", "dY", "a1", "a2", "aR", "aS", "gone"] + ["a3%d" % s for s in range(N - 1)]

ARR = {"a1": [15400, 15400, 16000, 16000, 16700, 16700, 15200, 0], "a2": [22400, 22800, 23400, 23400, 23200, 23200, 20000], "aR": 26000,
       "a3": [26600, 26700, 27400, 27600, 26900, 26800, 23000]}
TAIL = {"s1": 22000, "s2": 12000, "sR": 8000, "s3": 6500, "tb": 24000}
PACE = [dict(c=1.04, g=1.6, s=4.0, p=0.52, y=100, t=0.85, a=1.0, i=350, f=1500, h=600, k=750, r=17, b=1 / 18),
        dict(c=0.9, g=1.3, s=2.8, p=0.45, y=90, t=0.97, a=0.95, i=350, f=1370, h=650, k=800, r=15, b=1 / 13),
        dict(c=1.15, g=1.8, s=4.5, p=0.58, y=140, t=1.0, a=1.25, i=350, f=2200, h=800, k=1050, r=25, b=1 / 10),
        dict(c=1.04, g=1.6, s=4.0, p=0.52, y=110, t=0.9, a=1.0, i=350, f=1100, h=550, k=650, r=14, b=1 / 18),
        dict(c=1.0, g=1.55, s=3.8, p=0.5, y=100, t=0.75, a=0.95, i=300, f=2260, h=550, k=650, r=12, b=1 / 22)]
ROOM = (2500, 1500, 1000, 800)
TRIES = 3500
HEAT = 2500
SOFT = 0.05
KEPT = {}
ALONE = {"a1": ([2, 2, 2], 1), "a2": ([1, 1, 2, 2], 0), "aR": ([2, 2, 2], 1), "a3": ([1] * 6, 1)}
LATE = ()
SPLIT = 0.4
FEW = 128
OUT = (0, 64, 192, NP)
CUT = [(0, 160, NP), (0, 160, NP)]
ORD1 = [0, 1, 2, 3, 4, 5, 6]


def calls(topo, cores, src, dests):
    me = cores[src]
    dests, (sizes, side) = dests
    far = [d for d in dests if topo.chip(cores[d]) != topo.chip(me)]
    near = [d for d in dests if d not in far]
    out = []
    used = set()
    for part in [far[sum(sizes[:i]):sum(sizes[:i + 1])] for i in range(len(sizes)) if sum(sizes[:i]) < len(far)]:
        eng = topo.engines(me, cores[part[0]])
        used.update(eng)
        share = [1] * len(part)
        j = 0
        while sum(share) + share[j] <= len(eng):
            share[j] *= 2
            j = min(range(len(part)), key=lambda x: (share[x], x))
        call, at = [], 0
        for d, n in zip(part, share):
            call.append((d, sum(1 << e for e in eng[at:at + n])))
            at += n
        out.append(call)
    for d in near:
        eng = [e for e in topo.engines(me, cores[d]) if e not in used][:4]
        if not out:
            out.append([])
        out[min(side, len(out) - 1)].append((d, sum(1 << e for e in eng)))
    return out


def rank_program(g, core, T, topo):
    q = T.rank_of(core)
    if q is None:
        return
    if not KEPT:
        KEPT.update(arrange([program(g, r, T, topo) for r in range(N)]))
    program(g, q, T, topo)["issue"](*KEPT[q])


def arrange(ranks):
    plan = [r["start"]() for r in ranks]
    for turn in range(len(ROOM)):
        for x in range(4):
            ends = [r["worth"](*plan[q])[2] for q, r in enumerate(ranks)]
            for q, r in enumerate(ranks):
                for i, sem in r["lands"]:
                    for k, p in enumerate(PACE):
                        r["arr"][k][i] = max(ends[s][k][j] + p["k"] for s, o in enumerate(ranks) for j, to in o["goes"] if (q, sem) in to)
        stop = [max(ends[q][k][i] for q, r in enumerate(ranks) for i in r["stores"]) for k in range(len(PACE))]
        late = [[{} for p in PACE] for r in ranks]
        for x in range(4):
            for q, r in enumerate(ranks):
                for k, p in enumerate(PACE):
                    for j, to in r["goes"]:
                        r["due"][k][j] = min(late[d][k].get(sem, 1e9) - p["k"] for d, sem in to)
                    for j in r["stores"]:
                        r["due"][k][j] = stop[k]
                late[q] = r["latest"](*plan[q])
        for q, r in enumerate(ranks):
            plan[q] = r["improve"](*plan[q], turn)
    return dict(enumerate(plan))


def program(g, q, T, topo):
    cores = T.cores
    nb = N - 1 - q
    na, m = LV * nb, LV * q
    C = float(BAND * (q + 1))
    W1, W0 = NP, NP + m
    ops = []
    eng = {"V": g.vector, "P": g.tensor, "S": g.scalar, "G": g, "Y": g.sync}
    csem = {"V": "cV", "P": "cP", "S": "cS", "G": "cG"}

    def A(name, a=None, b=None, step=1):
        if name == "V0":
            name, a, b = "TB", RV + a, RV + b
        if a is None:
            a, b = 0, T[name].shape[1]
        elif b is None:
            b = a + 1
        ap = T[name][:, a:b:step] if step > 1 else T[name][:, a:b]
        return (ap, (name, 0, 512) if name[0] == "Q" else (name, a, b), len(range(a, b, step)), SCRATCH[name])

    def A3(name, j0, j1, a, b):
        return (T[name][:, j0:j1, a:b], (name, j0, j1), (j1 - j0) * (b - a), SCRATCH[name])

    def IND(w, l):
        return (w[0].indirect(l[0]), w[1], 16 * l[2], w[3], l[1])

    def add(alt, out, ins, **kw):
        rd = [x[1] for x in ins if isinstance(x, tuple)] + [x[4] for x in list(ins) + [out] if isinstance(x, tuple) and len(x) > 4]
        o = dict(alt=alt, W=[out[1]] if out else [], R=rd, lat=0, tail=0, sem=None, at=0)
        o.update(kw)
        ops.append(o)

    def ap(x):
        return x[0] if isinstance(x, tuple) else x

    def two(x):
        return x[3][2] in (BF, F16, U16)

    def cyc(out, i, per):
        if len(out) > 4:
            return (50, "s", out[2])
        if len(i) > 4:
            return (50, "g", i[2])
        return (0, "c", max(64, per * i[2]))

    def vts(out, i, s1, s2, o0, o1):
        fn = (lambda: g.vector.tensor_scalar(out[0], i[0], ap(s1), ap(s2), o0, o1)) if o1 is not None else \
             (lambda: g.vector.tensor_scalar(out[0], i[0], ap(s1), None, o0))
        return fn, cyc(out, i, 0.5 if two(out) and two(i) else 1)

    def sact(out, i, scale, bias, f):
        return (lambda: g.scalar.activation(out[0], i[0], f, bias=ap(bias), scale=ap(scale))), cyc(out, i, 1)

    def ts(out, i, s1, s2, o0, o1=None, **kw):
        add({"V": vts(out, i, s1, s2, o0, o1)}, out, [i, s1, s2], **kw)

    def lin(out, i, scale=1.0, bias=0.0, on="VS", **kw):
        f = AF.Relu if out[3][2] == U16 else AF.Identity
        if (scale, bias) == (1.0, 0.0):
            v = (lambda: g.vector.tensor_copy(out[0], i[0])), cyc(out, i, 0.5 if two(out) and two(i) else 1)
        else:
            v = vts(out, i, scale, bias, OP.mult, OP.add)
        alt = {"V": v, "S": sact(out, i, scale, bias, f)}
        add({e: alt[e] for e in on}, out, [i, scale, bias], **kw)

    def relu(out, i):
        add({"V": vts(out, i, 0.0, None, OP.max, None), "S": sact(out, i, 1.0, 0.0, AF.Relu)}, out, [i])

    def tt(out, a, b, o):
        add({"V": (lambda: g.vector.tensor_tensor(out[0], a[0], b[0], o), cyc(out, a, 2 if a[3][0] == b[3][0] else 1))}, out, [a, b])

    def ms(out, v, **kw):
        add({"V": (lambda: g.vector.memset(out[0], v), (0, "c", max(64, out[2] * (0.5 if two(out) else 1))))}, out, [], **kw)

    def fill(name, a, b, v, **kw):
        for x in range(a, b, 256):
            out, one = A(name, x, min(b, x + 256)), A("ONE", 0, min(b, x + 256) - x)
            alt = {"V": (lambda out=out: g.vector.memset(out[0], v), (0, "c", max(64, out[2] * (0.5 if two(out) else 1)))),
                   "S": sact(out, one, float(v), 0.0, AF.Identity)}
            if out[3][2] == I32:
                alt["G"] = (lambda out=out: g.iota(out[0], [[0, out[2]]], v, 0), (130, "c", 2 * out[2]))
            add(alt, out, [one], **kw)

    def scan(out, d0, d1, ini, o0, o1):
        add({"V": (lambda: g.vector.tensor_tensor_scan(out[0], d0[0], d1[0], ap(ini), o0, o1), (0, "c", max(64, out[2])))}, out, [d0, d1, ini])

    def mm(out, l, r, start, stop):
        add({"P": (lambda: g.tensor.matmul(out[0], l[0], r[0], start, stop), (0, "p", max(64, r[2]) * (4 if l[3][2] == F32 else 1)))}, out, [l, r])

    def wrap(bank, G, name, a, b, start=True, stop=True):
        out = A(bank, 0, (b - a) // 16)
        add({"P": (lambda: [g.tensor.matmul(out[0], T[G][:, 15 - p:143 - p], T[name][:, a + p:b:16], start and p == 0, stop and p == 15)
                            for p in range(16)][-1], (0, "p", 16 * max(64, out[2])))}, out, [A(G), A(name, a, b)])
        return out

    def iota(out, pat, base, cm):
        kw = {} if out[3][2] == I32 else {"allow_small_or_imprecise_dtypes": True}
        add({"G": (lambda: g.iota(out[0], pat, base, cm, **kw), (130, "c", 2 * out[2]))}, out, [])

    def sel(out, i, pat, o, fill, base, cm):
        add({"G": (lambda: g.affine_select(out[0], i[0], pat, o, fill, base, cm), (170, "c", 2 * out[2]))}, out, [i])

    def dma(e, out, src, region, sem, lat, ins=()):
        add({e: (lambda: eng[e].dma_start(out, src), (60, "t", 0))}, (None, region), list(ins), sem=sem, lat=lat, tail=lat)

    def arrive(sem, count, regions, at):
        ops.append(dict(alt={None: (None, (0, "t", 0))}, W=regions, R=[], lat=0, tail=0, sem=sem, cnt=count, at=at))

    sent, began, rowed = [0], [], {}

    def send(dests, src, dst, sem, tail):
        plan = calls(topo, cores, q, dests)
        for call in plan:
            tr, rd = [], []
            for d, mask in call:
                s = src(d, call)
                rid, pid = topo.addr(cores[d])[:2]
                tr.append(RemoteDMATransfer(dst_ids=[DstId(rid=rid, pnc=pid)], dma_engine_mask=mask, remote_sem=T.sem[sem], src=s[0], dst=dst(d, call)))
                rd.append(s)
                sent[0] += bin(mask).count("1")
            at = ("call", len(ops), len(ops) + 1)
            add({"G": (lambda tr=tr: g.remote_dma_fused(tr, local_sem=T.sem.gone), (0, "i" if began else "f", 1))}, (None, at), rd,
                tail=tail, tag=(sem[:2], plan.index(call)))
            if call is not plan[0]:
                ops[-1]["behind"] = began[-1]
            began.append(ops[-1])
            for e in "EN":
                part = [(d, x) for d, x in call if (topo.chip(cores[d]) == topo.chip(cores[q])) == (e == "N")]
                if part:
                    rows, size = 128 // bin(part[0][1]).count("1"), rd[0][2] * (4 if rd[0][3][2] == F32 else 2)
                    add({e: (None, (rows * size / 27 if e == "N" else 0, "r", rows, "b", rows * size * (e == "E")))}, None, [(None, at)],
                        tail=tail - 1200, to=[(d, sem) for d, x in part])
                    if (e, sem) in rowed:
                        ops[-1]["behind"] = rowed[e, sem]
                    rowed[e, sem] = ops[-1]
            tail -= 600

    def count(src, dests):
        return sum(bin(x).count("1") for call in calls(topo, cores, src, dests) for d, x in call if d == q)

    low = lambda r: list(range(r))
    up = lambda s: list(range(N - 1, s, -1))
    first = lambda r: ([d for d in ORD1 if d < r], ALONE["a1"])
    second = lambda r: (low(r), ALONE["a2"])
    reply = lambda s: (up(s), ALONE["aR"])
    back = lambda s: (up(s), ALONE["a3"])
    blocks = lambda s, r: r - s + (s in LATE)

    def last(s):
        return [sorted((d for d, x in call), reverse=True) for call in calls(topo, cores, s, back(s))]

    ms(A("RP", 0, 288), 0, tail=40000)
    iota(A("RP", 288, NP), [[0, NP - 288]], 0, 0)
    ops[-1]["tail"] = 60000
    for h in range(2):
        dma("S", T.TB[h::2, Z:Z + 512], T.bm[:], ("TB", Z + h, Z + h + 1), "dB", 2500)
        ops[-1]["tail"] = 50000
    for o in (0, 1, 2, 4, 5, 6):
        dma("Y", T.RP[o::16, :], T.en[:] if o < 4 else T.sd[:], ("RP", o, o + 1), "dP", 2100, [A("RP", 288, NP)])
        ops[-1]["tail"] = 40000
    dma("Y", T.CS[:, Z:], T.cs[:], ("CS", Z, Z + NB), "dC", 4600, [(None, ("order", 0, 1))])
    dma("Y", T.LS[:, Z:], T.ls[:], ("LS", Z, Z + NB), "dL", 5900, [(None, ("order", 0, 1))])
    for o in ops[2:10]:
        o["first"] = True

    col = {}

    def c_(name):
        if name not in col:
            col[name] = A("CT", len(col))
        return col[name]

    EQ = lambda i: A("EQ", i)
    LT = lambda i: A("LT", i)
    iota(A("KI", 0), [[0, 1]], 0, 1)
    iota(A("OM"), [[0, 8], [1, 16]], 0, 0)
    ms(A("ONE"), 1.0)
    ms(A("CS", 0, Z), 0)
    ms(A("LS", 0, Z), 0.0)
    for j, (x, name) in enumerate(((15, "o"), (1, "par"), (3, "o3"))):
        ts(A("KI", 2 + 2 * j), A("KI", 0), x, None, OP.bitwise_and)
        lin(c_(name), A("KI", 2 + 2 * j))
    lin(c_("sB"), c_("par"), 64 - 1 / 32, 1 / 32)
    lin(c_("cB"), c_("par"), 15.5 / 32, -15.5 / 32)
    ts(A("EQ"), A("OM", 0, 16), c_("o"), None, OP.is_equal)
    ts(A("LT"), A("OM", 0, 16), c_("o"), None, OP.is_gt)
    ts(A("D8", 0, 3), A("OM", 0, 3), c_("o3"), 255.0, OP.is_lt, OP.mult)
    lin(A("D8", 4, 7), A("D8", 0, 3), 1.0, 1.0)
    add({"V": (lambda: g.vector.tensor_reduce(c_("u3")[0], T.D8[:, 4:7], AxisListType.X, OP.mult), (0, "c", 64))}, c_("u3"), [A("D8", 4, 7)])
    lin(c_("f3"), LT(4), -2.0 ** -13, 2.0 ** -12)
    lin(c_("sP"), c_("u3"), c_("f3"), 0.0)
    lin(c_("cP0"), c_("sP"), 0.5, -0.5)
    ts(c_("cP"), c_("cP0"), 0.0, None, OP.min)
    lin(c_("y1"), EQ(1), 2.0, 0.0)
    lin(c_("wy"), EQ(2), 1 / 128, c_("y1"))
    ts(c_("w1"), EQ(8), EQ(9), -1 / 16, OP.add, OP.mult)
    lin(c_("w2"), EQ(0), 512.0, c_("wy"))
    lin(c_("w16"), c_("w1"), 1.0, c_("w2"))
    lin(c_("v00"), EQ(5), 16.0, 0.0)
    lin(c_("v0"), EQ(6), 1 / 16, c_("v00"))
    lin(c_("v1"), EQ(4), 256.0, EQ(5))
    lin(c_("v15"), EQ(15), 8192.0, 0.0)
    lin(c_("g2"), c_("par"), -1 - 1 / 1024, 1.0)
    ts(c_("seg"), c_("o"), c_("par"), 0.5, OP.subtract, OP.mult)
    sel(A("BL0"), A("ONE", 0, 128), [[16, 8], [0, 16]], OP.is_ge, 0.0, 15, -1)
    sel(A("BLK"), A("BL0"), [[-16, 8], [0, 16]], OP.is_ge, 0.0, 0, 1)
    ms(A("G1", 128, 144), 0.0)
    sel(A("G1", 0, 128), A("BLK"), [[0, 8], [1, 16]], OP.is_equal, 0.0, -15, 0)
    sel(A("ID"), A("ONE", 0, 128), [[-1, 128]], OP.is_equal, 0.0, 0, 1)
    if nb:
        lin(A("I32"), A("ID"))
    for G, w in (("GY", "wy"), ("GW", "w16"), ("G2", "g2")):
        lin(A(G), A("G1"), c_(w), 0.0, "V")
    lin(A("G3"), A("G2"), LT(2), 0.0)
    lin(c_("nc"), LT(15), -C, 0.0)
    lin(A("GC"), A("G1"), c_("nc"), 0.0)
    lin(A("MX"), A("BLK"), EQ(0), 0.0, "V")
    if 0 < na <= FEW:
        lin(A("MC"), A("BLK"), LT(15), 0.0)
    lin(A("MV0"), A("BLK"), c_("v0"), 0.0, "V")
    lin(A("MV1"), A("BLK"), c_("v1"), 0.0, "V")
    ts(A("HH"), A("OM"), EQ(15), LT(15), OP.mult, OP.subtract)
    lin(A("BN"), A("BLK"), -2.0 ** 20, 0.0)
    tt(A("MY"), A("HH"), A("BN"), OP.mult)
    if q:
        ts(A("MP"), A("BLK"), c_("w16"), 16.0, OP.mult, OP.mult)
        lin(A("NBL"), A("BLK"), -1.0, 0.0, "V")
        lin(c_("dead"), LT(q), 2.0 ** 21, 0.0)
        lin(A("MD"), A("BLK"), c_("dead"), 0.0)
        ts(A("MB"), A("BLK"), LT(15), C, OP.mult, OP.mult)
        sel(A("MB"), A("MB"), [[0, 128]], OP.not_equal, -BAND / 2, -15, 1)
        sel(A("MB"), A("MB"), [[0, 128]], OP.not_equal, 0.5, -31, 1)
        sel(A("MB"), A("MB"), [[0, 8], [1, 16]], OP.not_equal, -8.5 * BAND, -16 * 47, 16)
        sel(A("MB"), A("MB"), [[0, 8], [1, 16]], OP.not_equal, -BAND * (63.5 + q), -16 * 63 - q, 16)
        lin(c_("s1a"), EQ(0), M20 - M16, M16)
        lin(c_("s1"), EQ(q), M23 - M16, c_("s1a"))
        lin(c_("s2a"), c_("o"), float(BAND), c_("s1"))
        lin(c_("s2"), EQ(0), -2.0 ** 20, c_("s2a"))
        ms(A("CQ"), -float(BK * q))
        lin(c_("ia"), c_("o"), float(LV), float(W1))
        lin(c_("i1"), c_("ia"), LT(q), 0.0)
        lin(c_("i0"), LT(q), float(m), c_("i1"))
        fill("WIN", W1, W0 + m, EMPTY)
    if nb:
        if na > FEW:
            lin(A("GK"), A("GC"), -1 / 16, 0.0)
        lin(A("GN"), A("G1"), -1 / 16, 0.0)
    ms(A("L2", 14, 16), 0.0)

    lin(A("RB2"), A("TB", Z, Z + 512), c_("sB"), c_("cB"))
    ts(A("RB3"), A("RB2"), 2047, None, OP.bitwise_and)
    for a, b in zip(CUT[0], CUT[0][1:]):
        lin(A("RP2", a, b), A("RP", a, b), c_("sP"), c_("cP"))
        ops[-1]["R"].append(("RP", 0, NP))
        ts(A("TB", R3 + a, R3 + b), A("RP2", a, b), 255, None, OP.bitwise_and)
        lin(A("P0", a, b), A("TB", R3 + a, R3 + b))
    fill("TB", RV + NP, Z + BK, 0)
    ms(A("TB", 0, Z), -60000)
    ms(A("TB", Z + BK, 2 * Z + BK), -60000)

    def spread():
        for o in range(2):
            dma("Y", T.TB[o::16, Z:Z + BK], T.RB3[o::2, :], ("TBd", o, o + 1), "dT", 2900, [A("RB3"), A("TB", Z, Z + BK)])
            ops[-1]["tail"] = TAIL["tb"]
        ops[-2]["W"].append(("TB", Z, RV + NP))
        ops[-1].update(R=[], behind=ops[-2])

    TBL = (T.TB[:, 0:BK + 2 * Z], ("TB", 0, BK + 2 * Z), BK + 2 * Z, SCRATCH["TB"])

    def seeds(out, M, pay, a, b, bank):
        mm(A(bank, 0, b - a), A(M), A(pay, a, b), True, True)
        lin(A(out, a, b), A(bank, 0, b - a), 1.0, c_("v15"))

    def bins(xs, at, gh, ga, bank, cuts):
        k = xs[2]
        for a, b in zip(cuts, cuts[1:]):
            lin(A(gh, ga + 16 * a, ga + 16 * b), IND(TBL, A("LB", at + a, at + b)))
            ops[-1]["R"].append(("TBd", 0, 2))
        tt(A("XN", at, at + k), xs, A("LB", at, at + k), OP.subtract)
        x = wrap(bank, "G3", gh, ga, ga + 16 * k, True, False)
        mm(x, A("ID"), A("XN", at, at + k), False, True)
        lin(A("LN", at, at + k), x, 1.0, 2 * Z + 1 - HALF)

    def lookup(pay, a, b, at, bx, bl, cuts):
        k = (b - a) // 16
        if q:
            mm(A(bx, 0, k), A("ID"), A("CQ", 0, k), True, False)
        x = wrap(bx, "GW", pay, a, b, not q)
        if not q:
            relu(A("XS", at, at + k), x)
            x = A("XS", at, at + k)
        lin(A("LB", at, at + k), x, 1.0, Z - HALF)
        if len(bl) == 2:
            bins(x, at, "GH", a, bl, cuts)
        else:
            for u, v, bank in zip(cuts, cuts[1:], bl):
                part = A(bx, u, v) if q else A("XS", at + u, at + v)
                bins(part, at + u, "GH", a + 16 * u, bank, [0, v - u])

    def react(a, b, ln, V, Y):
        lin(A("LG", a, b), IND(A("LS"), ln), on="S")
        tt(A("BITS", a, b), IND(A("CS"), ln), A(V, a, b), OP.is_le)
        mm(Y, A("ID"), A("LG", a, b), True, False)
        mm(Y, A("MY"), A("BITS", a, b), False, True)
        ts(A("PR", a, b), Y, 0.0, C, OP.max, OP.min)

    def event(t, old, new, V, at, wend):
        own = list(zip(CUT[t], CUT[t][1:], ("Q0", "Q2", "Q5"), ("Q1", "Q3", "Q6")))
        p = 8 + t
        lst = "LS%d" % t
        for a, b, bY, bX in own:
            Y, X, B = A(bY, 0, b - a), A(bX, 0, b - a), A("Q4", 0, b - a)
            if q:
                mm(X, A("MP"), A(old, a, b), True, False)
                if t:
                    mm(X, A("MD"), A("MK", a, b), False, False)
            react(a, b, A("LN", at + a // 16, at + b // 16), V, Y)
            if q:
                mm(X, A("MB"), A("BITS", a, b), False, False)
                mm(X, A("NBL"), A("PR", a, b), False, True)
            mm(B, A("ID"), A(old, a, b), True, False)
            mm(B, A("GC", 15 - p, 143 - p), A("BITS", a, b), False, False)
            mm(B, A("G1", 15 - p, 143 - p), A("PR", a, b), False, True)
            lin(A(new, a, b), B, on="S")
        init = c_("i%d" % t) if q else None
        for a, b, bY, bX in own if q else ():
            ka, kb = a // 16, b // 16
            D, X = A(bY, 0, b - a), A(bX, 0, b - a)
            ts(D, X, c_("s1"), c_("s2"), OP.add, OP.is_equal)
            scan(A("SS", a, b), A("ONE", 0, b - a), D, init, OP.mult, OP.add)
            init = A("SS", b - 1)
            tt(A("DD", a, b), A("SS", a, b), D, OP.mult)
            if t == 0:
                lin(A("MK", a, b), D, on="S")
            lin(A(lst, ka, kb), wrap(bX, "G1", "DD", a, b), 1.0, -1.0)
            lin(IND(A("WIN", 0, wend), A(lst, ka, kb)), A(new, a, b), on="V")

    k = NP // 16
    O0, O1, O2, A1, A2, H3 = 0, 24, 48, 72, 88, 104

    y = wrap("Q6", "GY", "P0", 0, NP)
    lin(A("LB", O0, O0 + k), y, 1.0, -HALF)
    tt(A("FR"), y, A("LB", O0, O0 + k), OP.subtract)
    for a, b, bm, bv, bl in zip(CUT[0], CUT[0][1:], ("Q4", "Q1"), ("Q0", "Q2"), ("Q7", "Q5")):
        ka, kb = O0 + a // 16, O0 + b // 16
        seeds("V0", "MV0", "P0", a, b, bv)
        mm(A(bm, 0, b - a), A("MX"), A("P0", a, b), True, True)
        ts(A("MS", a, b), A(bm, 0, b - a), -8.0 * q, c_("seg"), OP.add, OP.is_equal)
        tt(A("GH", a, b), IND(A("RB3"), A("LB", ka, kb)), A("MS", a, b), OP.mult)
        x = wrap(bl, "G2", "GH", a, b, True, False)
        mm(x, A("ID"), A("FR", a // 16, b // 16), False, True)
        lin(A("LN", ka, kb), x, 1.0, Z + 1 - HALF)
    seeds("V1", "MV1", "P0", 0, NP, "Q3")
    event(0, "P0", "PA", "V0", O0, W0 + m)
    spread()
    send(first(q), lambda d, c: A("WIN", W0 + LV * d, W0 + LV * (d + 1)),
         lambda d, c: T.PA[:, NP + LV * (q - d - 1):NP + LV * (q - d)], "a1", TAIL["s1"])

    lookup("PA", 0, NP, O1, "Q6", ["Q7", "Q5", ""], [x // 16 for x in CUT[1]])
    event(1, "PA", "PB", "V1", O1, W0)
    if q:
        relu(A("L2", 0, 2 * q), wrap("Q1", "GW", "WIN", W1, W0))
    e, ka = NP + na, 2 * nb
    if nb:
        arrive("a1", sum(count(r, first(r)) for r in up(q)), [("PA", NP, e)], ARR["a1"][q])
        seeds("V1", "MV1", "PA", NP, e, "Q5")
        lookup("PA", NP, e, A1, "Q6", "Q7", [0, ka])
        Y, ln = A("Q5", 0, na), A("LN", A1, A1 + ka)
        if na > FEW:
            react(NP, e, ln, "V1", Y)
        else:
            lin(A("LG", NP, e), IND(A("LS"), ln), on="S")
            tt(A("BITS", NP, e), IND(A("CS"), ln), A("V1", NP, e), OP.is_le)
            mm(Y, A("MC"), A("BITS", NP, e), True, True)
            ts(Y, Y, c_("o"), None, OP.is_equal)
            tt(A("PR", NP, e), A("LG", NP, e), Y, OP.mult)
        if q:
            lin(A("XS", A1, A1 + ka), A("Q6", 0, ka), 1.0, float(BK * q))
        mm(A("Q6", 0, ka), A("I32"), A("XS", A1, A1 + ka), True, False)
        if na > FEW:
            wrap("Q6", "GK", "BITS", NP, e, False, False)
        x = wrap("Q6", "GN", "PR", NP, e, False, True)
        relu(A("L2", 2 * q, 14), x)
    send(second(q), lambda d, c: A("L2", 0, 16), lambda d, c: T.L2[:, 16 * (q - d):16 * (q - d + 1)], "a2", TAIL["s2"])

    gate = ops[-1 if nb == 0 else max(i for i, o in enumerate(ops) if o["W"] and o["W"][0][0] == "L2")]
    x = len(ops)
    lin(A("T0"), IND(A("CS"), A("LN", O0, O0 + k)))
    if q:
        fill("FA", 0, W0 + m, 0.0)
        iota(A("K0"), [[16, 24]], 0, 0)
        lin(A("K1"), A("K0"), 1.0, c_("o"))
        tt(A("M0"), A("LS0"), A("LS1"), OP.max)
        tt(A("LF"), A("M0"), A("K1"), OP.max)
    tt(A("T1"), IND(A("CS"), A("LN", O1, O1 + k)), A("T0"), OP.add)
    lookup("PB", 0, NP, O2, "Q0", "Q2", [0, k])
    tt(A("T2" if q else "YO"), IND(A("CS"), A("LN", O2, O2 + k)), A("T1"), OP.add)
    if not q:
        dma("Y", T.y[:], T.YO[:], ("y", 0, 1), "dY", 2500, [A("YO")])
    else:
        for o in ops[x:]:
            o["behind"] = gate
    if nb:
        xs = A("L2", 2 * q, 14)
        lin(A("SG", 0, na), IND(A("CS"), A("LN", A1, A1 + ka)))
        if q not in LATE:
            lin(A("LB", A2, A2 + ka), xs, 1.0, Z - HALF - BK * q)
            if q:
                lin(A("XS", A2, A2 + ka), xs, 1.0, -float(BK * q))
                xs = A("XS", A2, A2 + ka)
            bins(xs, A2, "GH", NP, "Q7", [0, ka // 4 * 2, ka] if ka > 8 else [0, ka])
        if q:
            tt(A("S2", 0, na), IND(A("CS"), A("LN", A2, A2 + ka)), A("SG", 0, na), OP.add)
        send(reply(q), lambda d, c: A("S2" if q else "SG", LV * (d - q - 1), LV * (d - q)), lambda d, c: T.LA[:, m:m + LV], "aR", TAIL["sR"] + (0 if q else 6000))
        if not q and not LATE:
            lin(A("S2"), IND(A("CS"), A("LN", A2, A2 + ka)))
            send(reply(q), lambda d, c: A("S2", LV * (d - 1), LV * d), lambda d, c: T.L0[:], "aS", TAIL["sR"] + 2000)
        end, at = {}, 0
        for call in last(q):
            for r in call:
                if blocks(q, r) > 1:
                    iota(A("PLC", at, at + 2 * blocks(q, r) - 2), [[16, blocks(q, r) - 1], [1, 2]], 2 * (r - 1), 0)
                at += 2 * blocks(q, r)
                iota(A("PLC", at - 2, at), [[1, 2]], 16 * (blocks(q, r) - 1) + 2 * q, 0)
                end[r] = at
        kp = -(-at // 16)
        if at % 16:
            ms(A("PLC", at, 16 * kp), 0.0)
        lin(A("PL", 0, kp), wrap("Q3", "G1", "PLC", 0, 16 * kp), 1 / 16, 0.0)
        arrive("a2", sum(count(r, second(r)) for r in up(q)), [("L2", 16, 16 * (nb + 1))], ARR["a2"][q])
        xl = IND(A("L2", 0 if q in LATE else 16, 16 * (nb + 1)), A("PL", 0, kp))
        ts(A("LB", H3, H3 + 16 * kp), xl, Z - HALF - BK * q, float(Z + BK), OP.add, OP.min)
        lin(A("XS", H3, H3 + 16 * kp), xl, 1.0, -float(BK * q), on="S")
        cut = min((end[c[-1]] for c in last(q)), key=lambda x: abs(x - SPLIT * at)) if at > 24 else at
        for a, b, bank in ((0, cut, "Q5"), (cut, at, "Q6")):
            if b > a:
                bins(A("XS", H3 + a, H3 + b), H3 + a, "G3H", 16 * a, bank, [0, (b - a) // 4 * 2, b - a] if b - a > 8 else [0, b - a])
        for call in calls(topo, cores, q, back(q)):
            c = sorted((d for d, x in call), reverse=True)
            a, b = end[c[0]] - 2 * blocks(q, c[0]), end[c[-1]]
            cuts = [a, (a + b) // 4 * 2, b] if b - a > 8 else [a, b]
            for a, b in zip(cuts, cuts[1:]):
                lin(A("S3", 16 * a, 16 * b), IND(A("CS"), A("LN", H3 + a, H3 + b)))
        wide = lambda c: LV * blocks(q, max(d for d, x in c))
        send(back(q), lambda d, c: A("S3", 16 * end[d] - wide(c), 16 * end[d]), lambda d, c: T.L3[:, q, W3 - wide(c):W3], "a3%d" % q, TAIL["s3"])

    if q:
        def more(a, b, x):
            tt(A("FA", a, b), x, A("FA", a, b), OP.add)

        lin(IND(A("FA", 0, W0 + m), A("LF", k // 2, k)), A("T2", NP // 2, NP), on="V")
        arrive("aR", sum(count(s, reply(s)) for s in low(q)), [("LA", 0, m)], ARR["aR"])
        z = 0 if LATE else LV
        if z:
            arrive("aS", count(0, reply(0)), [("L0", 0, LV)], ARR["aR"])
            more(W0, W0 + LV, A("LA", 0, LV))
            more(W0, W0 + LV, A("L0"))
        if m > z:
            tt(A("Q1", z, m), A("LA", z, m), A("FA", W0 + z, W0 + m), OP.add)
        lin(A("Q3", 0, m), A("FA", W1, W0))
        when = {}
        for s in low(q):
            at = ARR["a3"][s]
            for call in calls(topo, cores, s, back(s)):
                at += 128 // bin(call[0][1]).count("1") * (18 + 4 * blocks(s, max(call)[0]))
                if q in [d for d, x in call]:
                    when[s] = at
        for s in sorted(low(q)[1:], key=when.get) + [0]:
            arrive("a3%d" % s, count(s, back(s)), [("L3", s, s + 1)], when[s])
            w = LV * (blocks(s, q) - 1)
            if w:
                tt(A("Q1", m - w, m) if s else A("FA", W0 + z, W0 + m), A3("L3", s, s + 1, W3 - LV - w, W3 - LV), A("Q1", m - w, m), OP.add)
        tt(A("FA", W1, W0), A3("L3", 0, q, W3 - LV, W3), A("Q3", 0, m), OP.add)
        for a, b in zip(OUT, OUT[1:]):
            if a >= NP // 2:
                lin(A("YO", a, b), IND(A("FA", 0, W0 + m), A("LF", a // 16, b // 16)), on="S")
            else:
                tt(A("YO", a, b), IND(A("FA", 0, W0 + m), A("LF", a // 16, b // 16)), A("T2", a, b), OP.add)
            dma("YS"[a >= NP // 2], T.y[:, a:b], T.YO[:, a:b], ("y", a, b), "dY", 2500, [A("YO", a, b)])

    at = next(i for i, o in enumerate(ops) if o["sem"] == "dT")
    moved = [o for o in ops[:at] if o["W"][0][0] in ("GK", "GN", "MD", "MC", "L2", "I32", "G3")]
    for o in moved:
        o["behind"] = ops[at]
    ops[:] = [o for o in ops[:at + 2] if all(o is not x for x in moved)] + moved + ops[at + 2:]
    for o in ops:
        if q and o["W"] and o["W"][0][0] == "PLC" and "G" in o["alt"]:
            o["behind"] = [x for x in began if x["tag"][0] == "a1"][-1]
    hit = lambda x, y: x[1] < y[2] and y[1] < x[2]
    acc = {}
    for i, o in enumerate(ops):
        dep = {}
        for r in o["R"]:
            for j, x, w in acc.get(r[0], ()):
                if hit(r, x) and w:
                    dep[j] = "data"
                elif hit(r, x) and r[0][0] == "Q":
                    dep.setdefault(j, "bank")
        for r in o["W"]:
            for j, x, w in acc.get(r[0], ()):
                if hit(r, x) and None not in o["alt"]:
                    dep[j] = "data"
        if o["R"] and o["R"][0][0] == "order":
            dep = {j: "order" for j in range(i) if ops[j].get("first") or ops[j]["sem"] == "dC"}
        if "to" in o:
            dep = {j: "call" for j in dep}
        if "behind" in o:
            dep.setdefault(next(j for j in range(i) if ops[j] is o["behind"]), "order")
        o["dep"] = dep
        for r in o["R"]:
            acc.setdefault(r[0], []).append((i, r, False))
        for r in o["W"]:
            acc.setdefault(r[0], []).append((i, r, True))
    n = len(ops)
    spans = [[{e: c[0] + sum(p[x] * y for x, y in zip(c[1::2], c[2::2])) for e, (f, c) in o["alt"].items()} for o in ops] for p in PACE]
    full = [list(o["dep"].items()) for o in ops]
    above, deps = [], []
    for i in range(n):
        far = set().union(*[above[j] for j, kind in full[i]])
        deps.append([(j, kind) for j, kind in full[i] if j not in far or ops[j]["sem"]])
        above.append(far | {j for j, kind in full[i]})

    def free(j, kind, ej, e):
        return kind == "order" or (ej == e and (e == "P" or kind == "bank"))

    def gap(j, kind, ej, e, p):
        if kind == "call":
            return p["h"]
        return 0 if free(j, kind, ej, e) else (ops[j]["lat"] * p["t"] if ops[j]["lat"] else p["y"])

    def place(noise, lean):
        p, sp = PACE[0], spans[0]
        tail = [o["tail"] for o in ops]
        for i in range(n - 1, -1, -1):
            tail[i] += min(sp[i].values()) + noise[i]
            for j, kind in deps[i]:
                tail[j] = max(tail[j], tail[i] + gap(j, kind, 0, 1, p))
        at, on, busy = [0] * n, [None] * n, {x: [] for x in list(eng) + ["E", "N"]}
        for i in sorted(range(n), key=lambda i: (-tail[i], i)):
            best = None
            for e, d in sp[i].items():
                t = max([ops[i]["at"]] + [at[j] + sp[j][on[j]] + gap(j, kind, on[j], e, p) for j, kind in deps[i]])
                z = 0
                if e:
                    row = busy[e]
                    z = len(row)
                    for x, (a, b, j) in enumerate(row):
                        if t + d * 1.15 + 30 <= a:
                            z = x
                            break
                        t = max(t, b)
                v = t + 2 * d + (lean[i] if e == "V" else 0)
                if best is None or v < best[0]:
                    best = (v, e, t, d, z)
            v, e, t, d, z = best
            if e:
                busy[e].insert(z, (t, t + d, i))
            at[i], on[i] = t, e
        return at, on, busy

    goes = [(i, o["to"]) for i, o in enumerate(ops) if "to" in o]
    stores = [i for i, o in enumerate(ops) if o["sem"] == "dY"]
    lands = [(i, o["sem"]) for i, o in enumerate(ops) if None in o["alt"]]
    aims = [i for i, to in goes] + stores
    arr = [{i: ops[i]["at"] * p["a"] for i, sem in lands} for p in PACE]
    due = [{i: 0 for i in aims} for p in PACE]
    room = [0]
    fixed = [next(iter(o["alt"])) if len(o["alt"]) == 1 else 0 for o in ops]
    edges = [[[(j, gap(j, kind, fixed[j], fixed[i] if kind == "data" else 1, p), kind == "bank") for j, kind in deps[i]] for i in range(n)] for p in PACE]
    way = [o["tail"] for o in ops]
    for i in range(n - 1, -1, -1):
        way[i] += min(spans[0][i].values())
        for j, kind in deps[i]:
            way[j] = max(way[j], way[i] + gap(j, kind, 0, 1, PACE[0]))
    soft = [SOFT * min(1.0, x / 30000) ** 4 for x in way]
    succ = [[] for i in range(n)]
    for i in range(n):
        for j, kind in deps[i]:
            succ[j].append(i)

    def worth(order, on):
        v, why, ends, over = 0, [], [], []
        for p, sp, ed, come, by in zip(PACE, spans, edges, arr, due):
            end, prev, cause = [0] * n, {}, [-1] * n
            for i in order:
                e = on[i]
                c = prev.get(e, -1)
                t = end[c] if c >= 0 else come[i] if e is None else 0
                for j, d, bank in ed[i]:
                    x = end[j] if bank and on[j] == e else end[j] + d
                    if x >= t:
                        t, c = x, j
                end[i], cause[i] = t + sp[i][e], c
                if e:
                    prev[e] = i
            late = [max(0, end[i] + room[0] - by[i]) for i in aims]
            v += (sum(late) + max(late) + 0.05 * sum(end[i] for i in aims) + sum(x * y for x, y in zip(end, soft))) / p["a"]
            why.append(cause)
            ends.append(end)
            over.append(late)
        return v, why, ends, over

    def latest(order, on):
        out = []
        for sp, ed, by in zip(spans, edges, due):
            req, nxt = [1e9] * n, {}
            for i in order[::-1]:
                e = on[i]
                req[i] = min(req[i], by.get(i, 1e9), nxt.get(e, 1e9))
                t = req[i] - sp[i][e]
                if e:
                    nxt[e] = t
                for j, d, bank in ed[i]:
                    req[j] = min(req[j], t if bank and on[j] == e else t - d)
            out.append({sem: req[i] for i, sem in lands})
        return out

    def improve(order, on, turn):
        rng = np.random.default_rng([q, turn])
        room[0] = ROOM[turn]
        best, why, ends, over = worth(order, on)
        kept = (best, order, on)
        for it in range(TRIES):
            k = int(rng.integers(len(PACE)))
            cause, share = why[k], np.array(over[k]) + 30.0
            i, pairs = aims[int(rng.choice(len(aims), p=share / share.sum()))], []
            while cause[i] >= 0:
                j = cause[i]
                if on[j] == on[i] and i not in succ[j]:
                    pairs.append((j, i))
                i = j
            if not pairs:
                continue
            j, i = pairs[int(rng.integers(len(pairs)))]
            move, new, no = int(rng.integers(4)), list(order), on
            pos = {x: k for k, x in enumerate(order)}
            if move < 2:
                x = (j, i)[move]
                alt = [e for e in ops[x]["alt"] if e != on[x]]
                if not alt:
                    continue
                no = list(on)
                no[x] = alt[int(rng.integers(len(alt)))]
            elif move == 2:
                go = {j}
                for x in order[pos[j]:pos[i]]:
                    if x in go:
                        go.update(succ[x])
                if i in go:
                    continue
                far = min(n, pos[i] + 1 + int(rng.integers(6)) * int(rng.integers(2)))
                part = order[pos[j]:far]
                for x in part:
                    if x in go:
                        go.update(succ[x])
                new[pos[j]:far] = [x for x in part if x not in go] + [x for x in part if x in go]
            else:
                go = {i}
                for x in order[pos[i]:pos[j]:-1]:
                    if x in go:
                        go.update(y for y, kind in deps[x])
                if j in go:
                    continue
                part = order[pos[j]:pos[i] + 1]
                new[pos[j]:pos[i] + 1] = [x for x in part if x in go] + [x for x in part if x not in go]
            v, w, ends, ov = worth(new, no)
            if v <= best + HEAT / (1 + turn) * (1 - it / TRIES) ** 2 * rng.random():
                best, why, over, order, on = v, w, ov, new, no
                if v < kept[0]:
                    kept = (v, new, no)
        return kept[1:]

    def start():
        at, on, busy = place([0.0] * n, [100.0] * n)
        return sorted(range(n), key=lambda i: (at[i], i)), on

    return dict(start=start, worth=worth, latest=latest, improve=improve, goes=goes, stores=stores, lands=lands, arr=arr, due=due,
                issue=lambda order, on: issue(g, T, ops, full, free, eng, csem, sent[0], order, on))


def issue(g, T, ops, full, free, eng, csem, sent, order, on):
    at = {i: k for k, i in enumerate(order)}
    busy = {x: [(0, 0, i) for i in order if on[i] == x] for x in eng}
    total = {}
    for o in ops:
        if o["sem"]:
            total[o["sem"]] = o.get("cnt", total.get(o["sem"], 0) + 16)
    need = set()
    for x in eng:
        seen = {}
        for a, b, i in busy[x]:
            o = ops[i]
            o["waits"] = []
            for j, kind in sorted(full[i], key=lambda d: -at[d[0]]):
                p = ops[j]
                if free(j, kind, on[j], x):
                    continue
                key = p["sem"] or on[j]
                if seen.get(key, -1) < (0 if p["sem"] else at[j]):
                    seen[key] = 0 if p["sem"] else at[j]
                    o["waits"].append(j)
                    need.add(j)
    num = {}
    for x in csem:
        c = 0
        for a, b, i in busy[x]:
            if i in need and not ops[i]["sem"]:
                c += 1
                num[i] = c
    for x in eng:
        for a, b, i in busy[x]:
            o = ops[i]
            for j in o["waits"]:
                p = ops[j]
                if p["sem"]:
                    eng[x].wait_ge(T.sem[p["sem"]], total[p["sem"]])
                else:
                    eng[x].wait_ge(T.sem[csem[on[j]]], num[j])
            ins = o["alt"][x][0]()
            if o["sem"]:
                ins.then_inc(T.sem[o["sem"]], 16)
            elif i in num:
                ins.then_inc(T.sem[csem[x]], 1)
    g.sync.wait_ge(T.sem.dY, total["dY"])
    if sent:
        g.wait_ge(T.sem.gone, sent)
